import numpy as np, ml_dtypes
CORES = [23,119,17,113]
N = 4
BF = ml_dtypes.bfloat16
W, K, LP, CAP, PR = 4096, 4096, 2, 256, 6
XS = (1, 2, 3)
MP = K >> LP
def coefs(rng, lo, hi):
    o = np.argsort(rng.random((8, 16, 16)), axis=1)
    v = rng.integers(1, 4, (8, 16, 16)) * np.where(o == 0, 1, np.where(o == 1, -1, 2 * rng.integers(0, 2, (8, 16, 16)) - 1))
    return np.where(o < rng.integers(lo, hi + 1, (8, 1, 16)), v, 0)
def rays(rng, top, dens):
    v = np.floor(rng.random((N, 8, 16, W)) * (np.reshape(top, (1, 8, 1, 1)) + 1.0))
    return (v * (rng.random((N, 8, 16, W)) < dens)).astype(np.int64)
def plant(rng, nn, pz, order, full=False, odd=()):
    c = coefs(rng, 6, 10); x = rng.integers(0, 16, (N, 8, 16, W))
    P = np.argsort(rng.random((8, 16)), axis=1); M = rng.integers(0, 16, 8)
    if full: x[:, 1::2] = np.floor(np.exp2(7.9 * rng.random((N, 4, 16, W)))).astype(np.int64)
    for g in range(8):
        m = M[g]; a, b, e = P[g, :3]; w = int(rng.integers(1, 4))
        if full or g in odd:
            c[g] = 2 * np.sign(c[g]); c[g, e] = rng.choice(np.array([-3, -1, 1, 3]), 16); x[:, g, e] |= 1
        c[g, :, m] = 0; c[g, a, m] = w; c[g, b, m] = -w
        for r in range(N):
            sg = np.zeros(W, np.int64); sg[:int(nn[r, g])] = -1; sg[W - int(pz[r, g]):] = 1
            if order[g] == 0: sg = rng.permutation(sg)
            if order[g] == 2: sg = sg[::-1]
            lo = rng.integers(0, 8, W); d = rng.integers(1, 8, W)
            if full: d = np.where(sg > 0, 7, 1)
            x[r, g, a] = lo + np.where(sg > 0, d, 0); x[r, g, b] = lo + np.where(sg < 0, d, 0)
    return x, c, P, M
def pack(x, c):
    return {"x": np.ascontiguousarray(x.reshape(N, 128, W)).astype(np.float32).astype(BF), "q": np.stack([c.reshape(128, 16)] * N).astype(np.int32)}
def setup_inputs(rng):
    top = rng.permutation(np.array([15, 15, 40, 40, 100, 100, 255, 255]))
    return pack(rays(rng, top, rng.choice(np.array([0.1, 0.3, 0.6, 1.0]), (N, 8, 16, 1))), coefs(rng, 2, 6))
def setup_inputs_room(rng):
    nn = rng.choice(np.array([0, 1, CAP - 1, CAP, CAP + 1, 2 * CAP]), (N, 8)); pz = rng.choice(np.array([0, 1, MP - 1, MP, MP + 1]), (N, 8))
    nn[0] = (CAP, CAP + 1, CAP - 1, CAP, 1, 0, 2 * CAP, CAP + 1); pz[0] = (MP, MP + 1, MP - 1, 1, MP, MP + 1, MP, 0)
    nn[XS[0]] = (2 * CAP, CAP, CAP + 1, CAP - 1, CAP, CAP, 1, CAP); pz[XS[0]] = (MP + 1, MP, MP, MP - 1, MP, MP + 1, MP, MP)
    x, c, P, M = plant(rng, nn, pz, np.zeros(8, np.int64))
    return pack(x, c)
def setup_inputs_full(rng):
    few = CAP + rng.integers(0, 64, (N, 8)); many = W - MP - rng.integers(72, 136, (N, 8))
    nn = np.where(np.array([0, 1, 1, 0, 0, 1, 1, 0]) == 1, many, few); pz = MP + rng.integers(0, 64, (N, 8))
    o = XS[0]; p = W // (2 ** LP + 1)
    nn[0, 0] = CAP; nn[o, 3] = CAP; pz[0, :2] = MP; nn[0, 2] = W - p; pz[0, 2] = p
    x, c, P, M = plant(rng, nn, pz, np.array([0, 0, 0, 0, 1, 1, 2, 2]), True)
    a, b, e, f0, f1, f2, f3 = P[2, :7]
    up = x[0, 2, a] > x[0, 2, b]; dn = x[o, 2, a] < x[o, 2, b]
    x[0, 2, a] = np.where(up, rng.integers(1, 16, W), 0); x[0, 2, b] = np.where(up, 0, rng.integers(2, 8, W))
    u = np.zeros(W, np.int64); u[up] = rng.permutation(4096)[:p]
    for k, v in ((f0, u >> 6), (f1, 63 - (u >> 6)), (f2, u & 63), (f3, 63 - (u & 63))):
        x[0, 2, k] = np.where(up, v, x[0, 2, k]); x[o, 2, k] = np.where(dn, 0, x[o, 2, k])
    x[o, 2, a] = np.where(dn, 0, x[o, 2, a]); x[o, 2, b] = np.where(dn, 1, x[o, 2, b])
    return pack(x, c)
def setup_inputs_ties(rng):
    c = coefs(rng, 2, 4); c[:, :, 8:] = -c[:, :, rng.permutation(8)]; c[0, :, 15] = 0; c[4, :, 0] = 0
    x = rays(rng, np.array([1, 1, 2, 2, 3, 1, 2, 15]), rng.choice(np.array([0.4, 0.6, 0.9]), (N, 8, 16, 1)))
    h = W // 2
    for g in (2, 5): x[:, g, :, h:] = x[:, g][:, :, rng.permutation(h)]
    x[:, 7] = 255 * (rng.random((N, 16, W)) < 0.4)
    return pack(x, c)
def setup_inputs_lean(rng):
    h = W // 2; nn = rng.integers(h // 4, h // 2, (N, 8)); pz = rng.integers(h // 4, h // 2, (N, 8)); o = XS[0]
    nn[:, 0] = 0; pz[:, 1] = 0
    nn[0, 2] = W; pz[0, 2] = 0; nn[o, 2] = h; pz[o, 2] = W - h
    nn[0, 3] = 0; pz[0, 3] = 0; nn[o, 3] = 0; pz[o, 3] = W
    nn[0, 6] = 1; pz[0, 6] = W - 1
    for r in (0, XS[1], XS[0] ^ XS[1]): nn[r, 4] = h // 2; pz[r, 4] = h // 16
    nn[o, 4] = 16; pz[o, 4] = h // 2
    x, c, P, M = plant(rng, nn, pz, np.array([0, 0, 0, 0, 1, 2, 1, 2]), False, (0, 1, 4))
    a, b, e, k, l = P[0, :5]; m = M[0]
    c[0][:, [0, m]] = c[0][:, [m, 0]]; c[0, b, 0] = 0; x[:, 0, a] -= x[:, 0, b]
    c[0, :, 1] = 0; c[0, e, 1] = 2 * rng.integers(0, 2) - 1; c[0, k, 1] = 2; c[0, l, 1] = -2
    a, b = P[1, :2]; c[1, a, M[1]] = 0; x[:, 1, b] -= x[:, 1, a]
    c[4, :, (M[4] + rng.integers(1, 16)) % 16] = c[4, :, M[4]]
    return pack(x, c)
def setup_inputs_spread(rng):
    u = rng.random((N, 8, 16, W)); u[:, 6] = 0.5 + 0.5 * u[:, 6]
    v = np.floor(np.exp2(3 + 5 * rng.random((N, 8, 1, W))) * u) * (rng.random((N, 8, 1, W)) > 0.0625)
    kept = rng.random((N, 8, 16, W)) < rng.choice(np.array([0.4, 0.7, 1.0]), (N, 8, 16, 1)); kept[:, 6] = True
    v = np.minimum(v * kept, 255).astype(np.int64); c = coefs(rng, 2, 16)
    up = rng.permutation(16) < 8; side = (rng.random((N, 1, W)) < 0.5) == up[None, :, None]
    v[:, 7] = np.where(side, rng.integers(192, 256, (N, 16, W)), rng.integers(0, 32, (N, 16, W)))
    c[7] = np.where(up[:, None], 1, -1) * rng.choice(np.array([2, 3, 3, 3]), (16, 16)) * rng.choice(np.array([-1, 1]), (1, 16))
    return pack(v, c)
def check_inputs(d):
    bad = []; x = np.asarray(d["x"]).astype(np.float32); q = np.asarray(d["q"])
    if not (np.all(x >= 0) and np.all(x <= 255) and np.all(x == np.floor(x))): bad.append("range of x")
    if np.min(q) < -3 or np.max(q) > 3: bad.append("range of q")
    if not np.all(q == q[:1]): bad.append("q alike on all ranks")
    return bad
def reference(x, q):
    cur = np.ascontiguousarray(x.astype(np.float32).reshape(N, 8, 16, W).transpose(0, 1, 3, 2)).astype(np.int16)
    co = q[0].astype(np.float32).reshape(8, 16, 16)
    used = np.zeros((8, 16), bool)
    k = np.arange(K); i = k >> LP
    for t in range(len(XS)):
        val = np.matmul(cur.astype(np.float32), co[None])
        cnt = np.where(used, N * W + 1, np.count_nonzero(val, axis=(0, 2)))
        m = np.argmin(cnt, axis=1)
        used[np.arange(8), m] = True
        s = np.take_along_axis(val, m[None, :, None, None], 3)[..., 0].astype(np.int64)
        j = (37 * i + (CAP >> LP) * (k & (2 ** LP - 1)) + t) & (CAP - 1)
        new = cur.copy()
        for r in range(N):
            o = r ^ XS[t]
            for g in range(8):
                own = cur[r, g]; neg = np.flatnonzero(s[r, g] < 0); pos = np.flatnonzero(s[r, g] > 0); guest = np.flatnonzero(s[o, g] < 0)[:CAP]
                ks = np.flatnonzero((i < len(pos)) & (j < len(guest)))
                a = pos[i[ks]]; b = guest[j[ks]]; keep = s[r, g, a] + s[o, g, b] >= 0
                a = a[keep]; b = b[keep]
                z = np.minimum(own[a] + cur[o, g][b], 255)
                v = (17 * a + 5 * j[ks][keep]) & (W - 1); alive = np.ones(len(a), bool)
                for n in range(PR):
                    c = np.where(v == a, 16, np.count_nonzero(own[v] > z, axis=1))
                    alive = alive & (c > 0)
                    v = (5 * v + 241 * c + 1) & (W - 1)
                z = z[alive]; h = min(len(z), len(neg))
                new[r, g, neg[:h]] = z[:h]
        cur = new
    return {"y": np.ascontiguousarray(cur.transpose(0, 1, 3, 2)).reshape(N, 128, W).astype(np.float32).astype(BF)}

@@ -1,0 +1,705 @@
+import numpy as np
+from concourse.bass import DstId, RemoteDMATransfer
+from concourse.mybir import dt, AluOpType as A, AxisListType, ActivationFunctionType as F
+
+XE, XC = 4096, 4128
+SV, SS, FX, FE = 2048, 4096, 8192, 12288
+SB = {
+    "BW0": (XC, "bfloat16"), "BW1": (XC, "bfloat16"), "FW": (FE, "float32"), "Zp": (4096, "bfloat16"),
+    "Zf": (2048, "float32"), "Pg": (1024, "bfloat16"), "Hs": (256, "bfloat16"), "Hl": (256, "bfloat16"),
+    "c1n": (256, "bfloat16"), "c2n": (256, "bfloat16"), "c3n": (256, "bfloat16"),
+    "c1p": (1024, "bfloat16"), "c2p": (1024, "bfloat16"), "c3p": (1024, "bfloat16"),
+    "cmp": (4096, "bfloat16"), "G": (2048, "bfloat16"), "dg": (128, "float32"),
+    "cown": (12, "float32"), "cl": (144, "float32"), "small": (16, "float32"), "lst": (160, "bfloat16"),
+    "qi": (16, "int32"), "qf": (16, "float32"), "Qblk": (128, "bfloat16"), "nQ4": (512, "bfloat16"), "kapT": (512, "float32"),
+    "pi": (1, "int32"), "p16i": (1, "int32"), "pgi": (1, "int32"), "pif": (1, "float32"), "p16f": (1, "float32"),
+    "pgf": (1, "float32"), "e15": (1, "float32"), "p37": (1, "float32"), "ci": (144, "int32"), "cg": (128, "int32"),
+    "Bones": (128, "bfloat16"), "BonesF": (128, "float32"), "ident": (128, "bfloat16"), "identF": (128, "float32"),
+    "nident": (128, "bfloat16"), "I3856": (128, "bfloat16"), "I16384": (128, "bfloat16"), "I8192": (128, "bfloat16"),
+    "N16384": (128, "bfloat16"), "EM1": (144, "bfloat16"), "I16": (128, "bfloat16"),
+    "EM241": (144, "bfloat16"), "EM120": (144, "bfloat16"), "E": (144, "bfloat16"), "M16f": (16, "float32"),
+    "mask16": (16, "float32"), "base": (16, "float32"), "obig": (16, "float32"), "rown": (48, "float32"),
+    "Dm": (128, "bfloat16"), "Ds": (128, "bfloat16"), "dtmp": (128, "bfloat16"),
+    "B4080": (128, "bfloat16"), "c4080": (128, "bfloat16"), "Ji": (602, "int32"), "Jm": (602, "int32"), "JF": (602, "float32"),
+    "IF": (1024, "float32"), "IU": (1024, "uint16"), "JTi": (384, "int32"), "JTk": (384, "int32"), "JTm": (384, "int32"),
+    "JT": (384, "float32"), "VTi": (256, "int32"), "VT": (256, "float32"), "KT": (128, "float32"),
+    "onesF": (256, "float32"), "W2": (48, "float32"), "W3": (528, "float32"),
+    "mn": (1, "float32"), "oh": (16, "float32"), "cq": (16, "float32"), "csel": (1, "float32"),
+    "csb": (1, "bfloat16"), "kaps": (1, "float32"), "kap2": (1, "float32"), "Fl": (512, "bfloat16"), "T2b": (32, "bfloat16"),
+    "I3": (512, "float32"), "I2": (32, "float32"), "bt": (32, "float32"), "bnd": (8, "float32"),
+    "oAn": (16, "uint16"), "oQn": (16, "uint16"), "oPn": (16, "uint16"), "oAp": (64, "uint16"), "oQp": (64, "uint16"),
+    "oPp": (64, "uint16"), "A17": (64, "float32"), "AF": (64, "float32"),
+    "t32": (256, "int32"), "vi": (256, "int32"), "off": (256, "uint16"), "Tf5": (256, "float32"), "eq": (256, "bfloat16"),
+    "NZ": (1792, "bfloat16"), "shr": (48, "float32"), "AL": (256, "bfloat16"), "sc": (64, "float32"), "pb": (64, "float32"),
+    "of": (256, "float32"), "mx": (256, "float32"), "so": (256, "uint16"),
+    "g1": (256, "float32"), "g2": (256, "bfloat16"), "fo": (256, "float32"), "fo16": (256, "uint16"),
+}
+PART = {"lAn": ("lst", 0, 16), "lQn": ("lst", 16, 16), "lAp": ("lst", 32, 64), "lQp": ("lst", 96, 64),
+        "m05": ("small", 0, 1), "nT": ("small", 4, 1), "nS": ("small", 8, 1), "dA": ("small", 12, 1)}
+for _t in range(3):
+    PART["cown%d" % _t] = ("cown", 4 * _t, 1)
+    PART["rown%d" % _t] = ("rown", 16 * _t, 16)
+    PART["cl%d" % _t] = ("cl", 48 * _t, 48)
+SCRATCH = {n: ("sbuf", [128, -(-c // 16) * 16], d) for n, (c, d) in SB.items()}
+for _b in range(8):
+    SCRATCH["b%d" % _b] = ("psum", [128, 512], "float32")
+NX = 8
+QSEM = {"tensor": "sT", "vector": "sV", "scalar": "sS", "g": "sG"}
+SEMAPHORES = (["sT", "sV", "sS", "sG", "qld"] + ["xl%d" % i for i in range(NX)] + ["ys%d" % i for i in range(8)]
+              + ["%s%d" % (s, t) for s in ("cs", "gs", "lc", "lg", "fx", "fz") for t in range(3)])
+XS = (1, 2, 3)
+BIG = 1048576.0
+LOOP = "a2 b2 o2 a0 g2 e2 b0 a3 x2 b3 y2 o0 o3 c0 a1 g3 e0 u2 v2 b1 e3 s y3 v3 x3 o1 t2 e1 u3 t0 c1 t3 t1"
+CE = 4
+
+
+def make_queue(g, T):
+    ops, hist = [], {}
+    eng = {"tensor": g.tensor, "vector": g.vector, "scalar": g.scalar, "sync": g.sync, "g": g}
+
+    def op(q, fn, reads, writes, sem=None, val=0, remote=False):
+        me = len(ops)
+        rec = {"q": q, "fn": fn, "deps": set(), "sem": sem, "val": val, "need": False, "m": [], "remote": remote}
+        acc = []
+        for w in writes:
+            if w[0] == "IND":
+                acc += [(w[1], True), (w[2], False)]
+            else:
+                acc.append((w, True))
+        for r in reads:
+            if r[0] == "IND":
+                acc += [(r[1], False), (r[2], False)]
+            else:
+                acc.append((r, False))
+
+        def mine(o):
+            return o["q"] == q and o["sem"] is None
+        for (n, a, b, _ap), isw in acc:
+            ps = n[0] == "b" and len(n) == 2
+            for (oa, ob, o, ow) in hist.setdefault(n, []):
+                if o == me:
+                    continue
+                hit = oa < b and a < ob
+                if mine(ops[o]):
+                    need = hit and ow and not (ps and q == "tensor")
+                else:
+                    need = ps or (hit and (ow or isw))
+                if need:
+                    rec["deps"].add(o)
+        ops.append(rec)
+        for (n, a, b, _ap), isw in acc:
+            ps = n[0] == "b" and len(n) == 2
+            keep = []
+            for e in hist[n]:
+                inside = a <= e[0] and e[1] <= b
+                if e[2] != me and ((inside and isw) or (inside and not e[3] and mine(ops[e[2]]))
+                                   or (ps and not mine(ops[e[2]]) and not e[3])):
+                    continue
+                keep.append(e)
+            keep.append((a, b, me, isw))
+            hist[n] = keep
+
+    def emit():
+        for r in ops:
+            for d in r["deps"]:
+                ops[d]["need"] = True
+        cnt = {q: 0 for q in QSEM}
+        know = {q: {} for q in eng}
+        for r in ops:
+            q = r["q"]
+            if q is None:
+                r["clock"] = {r["sem"]: r["val"], "own": r["sem"]}
+                continue
+            k = know[q]
+            todo = {}
+            for d in sorted(r["deps"], reverse=True):
+                o = ops[d]
+                s, v = (o["sem"], o["val"]) if o["sem"] is not None else (QSEM[o["q"]], o["at"])
+                if k.get(s, 0) < v and todo.get(s, 0) < v:
+                    todo[s] = v
+                    r["m"].append(o["clock"])
+            for s in sorted(todo):
+                if not any(c["own"] != s and c.get(s, 0) >= todo[s] for c in r["m"]):
+                    eng[q].wait_ge(T.sem[s], int(todo[s]))
+            for c in r["m"]:
+                for s, v in c.items():
+                    if s != "own" and k.get(s, 0) < v:
+                        k[s] = v
+            ins = r["fn"]()
+            if r["sem"] is not None:
+                c = dict(k)
+                c[r["sem"]] = r["val"]
+                c["own"] = r["sem"]
+                if not r["remote"]:
+                    ins.then_inc(T.sem[r["sem"]], r["val"])
+            else:
+                s = QSEM[q]
+                c = dict(k)
+                c["own"] = s
+                if r["need"]:
+                    cnt[q] += 1
+                    ins.then_inc(T.sem[s], 1)
+                    c[s] = cnt[q]
+                    r["at"] = cnt[q]
+            r["clock"] = c
+        for q, n in cnt.items():
+            if n:
+                g.wait_ge(T.sem[QSEM[q]], n)
+        for r in ops:
+            if r["sem"] is not None and r["sem"][:2] in ("ys", "lc", "lg"):
+                g.wait_ge(T.sem[r["sem"]], r["val"])
+
+    return op, emit
+
+
+def rank_program(g, core, T, topo):
+    rank = T.rank_of(core)
+    if rank is None:
+        return
+    op, emit = make_queue(g, T)
+
+    def S(n, a=0, b=None, st=1):
+        n, o, w = PART.get(n, (n, 0, SB[n][0] if n in SB else 512))
+        a, b = a + o, (w if b is None else b) + o
+        return (n, a, b, T[n][:, a:b] if st == 1 else T[n][:, a:b:st])
+
+    def IND(w, o):
+        return ("IND", w, o)
+
+    def AP(x):
+        return x[1][3].indirect(x[2][3]) if x[0] == "IND" else x[3]
+
+    def num(x):
+        return isinstance(x, (int, float))
+
+    def cp(out, in_):
+        op("vector", lambda: g.vector.tensor_copy(AP(out), AP(in_)), [in_], [out])
+
+    def tt(out, a, b, o):
+        op("vector", lambda: g.vector.tensor_tensor(AP(out), AP(a), AP(b), o), [a, b], [out])
+
+    def ts(out, a, s1, o0, s2=None, o1=None):
+        cols = [x for x in (s1, s2) if x is not None and not num(x)]
+        u1 = s1 if num(s1) else AP(s1)
+        if o1 is None:
+            op("vector", lambda: g.vector.tensor_scalar(AP(out), AP(a), u1, None, o0), [a] + cols, [out])
+        else:
+            u2 = s2 if num(s2) else AP(s2)
+            op("vector", lambda: g.vector.tensor_scalar(AP(out), AP(a), u1, u2, o0, o1), [a] + cols, [out])
+
+    def red(out, a, o):
+        op("vector", lambda: g.vector.tensor_reduce(AP(out), AP(a), AxisListType.X, o), [a], [out])
+
+    def scan(out, a, n):
+        one = S("onesF", 0, n)
+        op("vector", lambda: g.vector.tensor_tensor_scan(AP(out), AP(one), AP(a), 0.0, A.mult, A.add), [one, a], [out])
+
+    def fill(out, c):
+        op("vector", lambda: g.vector.memset(AP(out), c), [], [out])
+
+    def act(out, a, f, bias=0.0, scale=1.0):
+        if f == F.Silu:
+            op("scalar", lambda: g.scalar.activation(AP(out), AP(a), f), [a], [out])
+        else:
+            cols = [x for x in (bias, scale) if not num(x)]
+            ub, us = bias if num(bias) else AP(bias), scale if num(scale) else AP(scale)
+            op("scalar", lambda: g.scalar.activation(AP(out), AP(a), f, bias=ub, scale=us), [a] + cols, [out])
+
+    def mm(out, l, r, start, stop):
+        op("tensor", lambda: g.tensor.matmul(AP(out), AP(l), AP(r), start, stop), [l, r], [out])
+
+    def spread(bank, c0, n, emat, src, s0, start, stop):
+        for p in range(16):
+            mm(S(bank, c0, c0 + n), S(emat, 15 - p, 143 - p), S(src, s0 + p, s0 + 16 * n, 16), start and p == 0, stop and p == 15)
+
+    def iota(out, pattern, base=0, cm=0, fl=False):
+        if fl:
+            op("g", lambda: g.iota(AP(out), pattern, base, cm, allow_small_or_imprecise_dtypes=True), [], [out])
+        else:
+            op("g", lambda: g.iota(AP(out), pattern, base, cm), [], [out])
+
+    def cast_in(out, in_ap, reads, sem):
+        op("g", lambda: g.dma_start(AP(out), in_ap), reads, [out], sem, 16)
+
+    op("sync", lambda: g.sync.dma_start(T.qi[:, 0:16], T.q[:]), [], [S("qi")], "qld", 16)
+    w = 4096 // NX
+
+    def load(i, q):
+        o = S("BW1", w * i, w * i + w)
+        op(q, lambda: (g.sync if q == "sync" else g.scalar).dma_start(AP(o), T.x[:, w * i:w * i + w]), [], [o], "xl%d" % i, 16)
+    for i in range(NX):
+        load(i, "sync" if i % 2 else "scalar")
+    iota(S("pi"), [[1, 1]], 0, 1)
+    iota(S("ci"), [[1, 144]])
+    iota(S("Ji"), [[37, 602]])
+    iota(S("IF"), [[1, 1024]], 0, 0, True)
+    iota(S("JTi"), [[1, 3], [64, 4], [592, 32]])
+    iota(S("VTi"), [[16, 256]], FX - SV)
+    iota(S("KT"), [[16, 128]], 16384 - SV, 0, True)
+    ts(S("pgi"), S("pi"), 4, A.arith_shift_right)
+    ts(S("cg"), S("ci", 0, 128), 4, A.arith_shift_right)
+    ts(S("p16i"), S("pi"), 15, A.bitwise_and)
+    cp(S("pgf"), S("pgi"))
+    cp(S("pif"), S("pi"))
+    cp(S("p16f"), S("p16i"))
+    ts(S("BonesF"), S("cg"), S("pgf"), A.is_equal)
+    ts(S("identF"), S("ci", 0, 128), S("pif"), A.is_equal)
+    for k in range(8):
+        ts(S("Qblk", 16 * k, 16 * k + 16), S("qi"), S("BonesF", 16 * k, 16 * k + 1), A.mult)
+    ts(S("M16f"), S("ci", 0, 16), S("p16f"), A.is_equal, 16.0, A.mult)
+    cp(S("base"), S("ci", 0, 16))
+    tt(S("e15"), S("pif"), S("p16f"), A.subtract)
+
+    def consts_a():
+        ts(S("e15"), S("e15"), 15.0, A.add)
+        cp(S("qf"), S("qi"))
+        ts(S("dtmp"), S("ci", 0, 128), S("pif"), A.is_lt, -1.0, A.mult)
+        ts(S("EM1"), S("ci"), S("e15"), A.is_equal)
+        act(S("Bones"), S("BonesF"), F.Copy)
+        act(S("B4080"), S("BonesF"), F.Copy, scale=4080.0)
+        act(S("ident"), S("identF"), F.Copy)
+        tt(S("Dm"), S("dtmp"), S("BonesF"), A.mult)
+        act(S("I16"), S("identF"), F.Copy, scale=16.0)
+        for b in range(8):
+            o, i = S("BW0", 512 * b, 512 * b + 512), S("BW1", 512 * b, 512 * b + 512)
+            if b in (2, 5, 7):
+                act(o, i, F.Identity, bias=4080.0, scale=-16.0)
+            else:
+                ts(o, i, -16.0, A.mult, 4080.0, A.add)
+        fill(S("BW0", XE, XC), 0.0)
+        fill(S("BW1", XE, XC), 0.0)
+        ts(S("mask16"), S("M16f"), 0.0625, A.mult)
+        fill(S("onesF"), 1.0)
+        for a, b in ((16, 24), (40, 48)):
+            fill(S("W2", a, b), 1000000.0)
+        for a, b in ((256, 264), (520, 528)):
+            fill(S("W3", a, b), 1000000.0)
+
+    def consts_b():
+        for n, s in (("EM241", 241.0), ("EM120", 120.5)):
+            act(S(n), S("EM1"), F.Copy, scale=s)
+        for n, s in (("nident", -1.0), ("I3856", 3856.0), ("I16384", 16384.0), ("I8192", 8192.0), ("N16384", -16384.0)):
+            act(S(n), S("identF"), F.Copy, scale=s)
+        for k in range(3):
+            act(S("FW", SV + 2048 * k, SV + 2048 * k + 2048), S("BW1", 0, 2048), F.Copy)
+        ts(S("Jm"), S("Ji"), 255, A.bitwise_and)
+        fill(S("m05"), -0.5)
+        ts(S("p37"), S("p16f"), 37.0, A.mult)
+        cp(S("JF"), S("Jm"))
+
+    def consts_c():
+        ts(S("JTk"), S("JTi"), S("p37"), A.add)
+        ts(S("JTm"), S("JTk"), 255, A.bitwise_and)
+
+    def consts_f():
+        tt(S("Ds"), S("Dm"), S("identF"), A.subtract)
+        ts(S("VT"), S("VTi"), S("p16f"), A.add, -24575.0, A.add)
+        ts(S("KT"), S("KT"), S("p16f"), A.add)
+
+    def consts_d():
+        cp(S("IU"), S("IF"))
+
+    def consts_e():
+        for k in range(4):
+            act(S("nQ4", 128 * k, 128 * k + 128), S("Qblk"), F.Copy, scale=-1.0)
+        fill(S("c4080"), 4080.0)
+        mm(S("b5"), S("c4080"), S("nQ4"), True, True)
+        act(S("kapT"), S("b5"), F.Copy, scale=-1.0)
+
+    peers = [r for r in range(len(T.cores)) if r != rank]
+    peers.sort(key=lambda r: len(topo.engines(core, T.cores[r])))
+    used, plan = [], []
+    for r in peers:
+        es = [e for e in topo.engines(core, T.cores[r]) if e not in used][:CE]
+        used += es
+        plan.append((r, sum(1 << e for e in es)))
+
+    def send_counts(t):
+        def f():
+            tr = []
+            for r, m in plan:
+                rid, pid, _s = topo.addr(T.cores[r])
+                c = [k for k in range(len(T.cores)) if k != r].index(rank)
+                tr.append(RemoteDMATransfer(dst_ids=[DstId(rid=rid, pnc=pid)], dma_engine_mask=m, remote_sem=T.sem["cs%d" % t],
+                                            src=AP(S("rown%d" % t)), dst=AP(S("cl%d" % t, 16 * c, 16 * c + 16))))
+            return g.remote_dma_fused(tr, local_sem=T.sem["lc%d" % t])
+        op("g", f, [S("rown%d" % t)], [], "lc%d" % t, CE * len(peers), True)
+        op(None, None, [], [S("cl%d" % t)], "cs%d" % t, CE * len(peers))
+
+    def send_guests(t):
+        dst = T.cores[rank ^ XS[t]]
+        es = topo.engines(core, dst)[:8]
+
+        def f():
+            rid, pid, _s = topo.addr(dst)
+            return g.remote_dma(T.Hl[:, 0:256], T.Hs[:, 0:256], T.sem["gs%d" % t], T.sem["lg%d" % t], pid, rid, sum(1 << e for e in es))
+        op("g", f, [S("Hs")], [], "lg%d" % t, len(es), True)
+
+    def guests_come(t):
+        src = T.cores[rank ^ XS[t]]
+        op(None, None, [], [S("Hl")], "gs%d" % t, len(topo.engines(src, core)[:8]))
+
+    def values(t, b):
+        xs, bank = "BW1" if t < 2 else "BW0", "b%d" % (b % 7)
+        shift = t > 0 and b % 2 == 1
+        if shift:
+            mm(S(bank), S("c4080"), S("nQ4"), True, False)
+        for k in range(4):
+            mm(S(bank, 128 * k, 128 * k + 128), S(xs, 512 * b + 128 * k, 512 * b + 128 * k + 128), S("Qblk"), not shift,
+               not shift or k == 3)
+
+    def nonzero(t, b):
+        bank, o = S("b%d" % (b % 7)), S("cmp", 512 * b, 512 * b + 512)
+        if b % 2 == 1:
+            act(o, bank, F.Sign)
+        elif t == 0:
+            ts(o, bank, 0.0, A.not_equal)
+        else:
+            tt(o, bank, S("kapT"), A.not_equal)
+
+    def diagonal(b):
+        for k in range(4):
+            c = S("cmp", 512 * b + 128 * k, 512 * b + 128 * k + 128)
+            mm(S("b7", 0, 128), c, c, b == 0 and k == 0, b == 7 and k == 3)
+
+    for b in range(4):
+        values(0, b)
+    for b in range(8):
+        nonzero(0, b)
+        diagonal(b)
+        if b < 4:
+            values(0, b + 4)
+    for t in range(3):
+        cur, nxt = ("BW0", "BW1") if t % 2 == 0 else ("BW1", "BW0")
+        X = S(cur, 0, XC)
+        cown, rown = S("cown%d" % t), S("rown%d" % t)
+        tt(S("dg"), S("b7", 0, 128), S("identF"), A.mult)
+        red(cown, S("dg"), A.add)
+        ts(rown, S("M16f"), cown, A.mult)
+        send_counts(t)
+        mm(S("b0", 0, 16), S("identF"), S("base"), True, False)
+        mm(S("b0", 0, 16), S("BonesF"), rown, False, False)
+        if t == 0:
+            consts_a()
+        if t == 1:
+            consts_d()
+        for k in range(3):
+            mm(S("b0", 0, 16), S("BonesF"), S("cl%d" % t, 16 * k, 16 * k + 16), False, k == 2)
+        red(S("mn"), S("b0", 0, 16), A.min)
+        ts(S("oh"), S("b0", 0, 16), S("mn"), A.is_equal)
+        tt(S("cq"), S("oh"), S("qf"), A.mult)
+        red(S("csel"), S("cq"), A.add)
+        ts(S("E"), S("EM1"), S("csel"), A.mult)
+        cp(S("csb"), S("csel"))
+        mm(S("b1", 0, 1), S("B4080"), S("csb"), True, True)
+        spread("b2", 0, 256, "E", cur, 0, True, True)
+        cp(S("kaps"), S("b1", 0, 1))
+        ts(S("obig"), S("oh"), BIG, A.mult)
+        ts(S("kap2"), S("kaps"), 2.0, A.mult)
+        tt(S("base"), S("base"), S("obig"), A.add)
+        if t == 0:
+            consts_b()
+        ts(S("Fl", 0, 256), S("b2", 0, 256), S("kaps"), A.is_gt)
+        ts(S("Fl", 256, 512), S("b2", 0, 256), S("kaps"), A.is_lt)
+        for p in range(16):
+            mm(S("b3", 0, 32), S("EM1", 15 - p, 143 - p), S("Fl", p, 512, 16), p == 0, p == 15)
+        mm(S("b4"), S("Bones"), S("Fl"), True, True)
+        mm(S("b5"), S("Dm"), S("Fl"), True, True)
+        if t == 0:
+            consts_c()
+        cp(S("T2b"), S("b3", 0, 32))
+        mm(S("b6", 0, 32), S("Bones"), S("T2b"), True, True)
+        mm(S("b6", 32, 64), S("Dm"), S("T2b"), True, True)
+        scan(S("I3", 0, 256), S("b4", 0, 256), 256)
+        scan(S("I2", 0, 16), S("b6", 0, 16), 16)
+        scan(S("I2", 16, 32), S("b6", 16, 32), 16)
+        tt(S("bt", 0, 16), S("I2", 0, 16), S("mask16"), A.mult)
+        tt(S("bt", 16, 32), S("I2", 16, 32), S("mask16"), A.mult)
+        red(S("bnd", 0, 1), S("bt", 0, 16), A.add)
+        red(S("bnd", 4, 5), S("bt", 16, 32), A.add)
+        J = S("JF", 173 * t, 173 * t + 256)
+        ts(S("c1n"), J, S("bnd", 0, 1), A.is_ge)
+        spread("b7", 0, 16, "EM1", "c1n", 0, True, True)
+        ts(S("c1p"), S("IF" if t == 0 else "IU"), S("bnd", 4, 5), A.is_ge)
+        spread("b1", 0, 64, "EM1", "c1p", 0, True, True)
+        tt(S("W2", 0, 16), S("I2", 0, 16), S("b6", 32, 48), A.add)
+        tt(S("W2", 24, 40), S("I2", 16, 32), S("b6", 48, 64), A.add)
+        cp(S("oAn"), S("b7", 0, 16))
+        act(S("lAn"), S("b7", 0, 16), F.Copy)
+        tt(S("c2n"), IND(S("W2", 0, 24), S("oAn")), J, A.is_le)
+        mm(S("b0", 0, 16), S("I16"), S("lAn"), True, False)
+        spread("b0", 0, 16, "EM1", "c2n", 0, False, True)
+        tt(S("W3", 0, 256), S("I3", 0, 256), S("b5", 0, 256), A.add)
+        cp(S("oAp"), S("b1", 0, 64))
+        act(S("lAp"), S("b1", 0, 64), F.Copy)
+        qb, pbk = ("b6", "b2"), ("b7", "b1")
+
+        def find2(h):
+            o, k = (512 * h, 512 * h + 512), (32 * h, 32 * h + 32)
+            tt(S("c2p", *o), IND(S("W2", 24, 48), S("oAp", *k)), S("IF", *o), A.is_le)
+            mm(S(qb[h], 0, 32), S("I16"), S("lAp", *k), True, False)
+            spread(qb[h], 0, 32, "EM1", "c2p", 512 * h, False, True)
+
+        def find3(h):
+            o, k = (512 * h, 512 * h + 512), (32 * h, 32 * h + 32)
+            cp(S("oQp", *k), S(qb[h], 0, 32))
+            act(S("lQp", *k), S(qb[h], 0, 32), F.Copy)
+            tt(S("c3p", *o), IND(S("W3", 264, 528), S("oQp", *k)), S("IF", *o), A.is_le)
+            mm(S(pbk[h], 0, 32), S("I16"), S("lQp", *k), True, False)
+            spread(pbk[h], 0, 32, "EM1", "c3p", 512 * h, False, True)
+
+        def start(h):
+            k = (32 * h, 32 * h + 32)
+            cp(S("oPp", *k), S(pbk[h], 0, 32))
+            ts(S("A17", *k), S(pbk[h], 0, 32), 17.0, A.mult)
+            cp(S("AF", *k), S(pbk[h], 0, 32))
+            act(S("Pg", 512 * h, 512 * h + 512), IND(X, S("oPp", *k)), F.Copy)
+            for ww in range(4):
+                o = 128 * h + 32 * ww
+                tt(S("t32", o, o + 32), S("A17", *k), S("JT", 128 * t + 32 * ww, 128 * t + 32 * ww + 32), A.add)
+            o = (128 * h, 128 * h + 128)
+            ts(S("vi", *o), S("t32", *o), 4095, A.bitwise_and)
+            cp(S("off", *o), S("vi", *o))
+
+        def own_places(h):
+            for c in (2 * h, 2 * h + 1):
+                for k in range(2):
+                    mm(S("b%d" % c, 384 + 32 * k, 416 + 32 * k), S("identF"), S("AF", 32 * h, 32 * h + 32), True, True)
+        cp(S("oQn"), S("b0", 0, 16))
+        act(S("lQn"), S("b0", 0, 16), F.Copy)
+        tt(S("c3n"), IND(S("W3", 0, 264), S("oQn")), J, A.is_le)
+        mm(S("b3", 0, 16), S("I16"), S("lQn"), True, False)
+        spread("b3", 0, 16, "EM1", "c3n", 0, False, True)
+        scan(S("I3", 256, 512), S("b4", 256, 512), 256)
+        find2(0)
+        tt(S("W3", 264, 520), S("I3", 256, 512), S("b5", 256, 512), A.add)
+        cp(S("oPn"), S("b3", 0, 16))
+        act(S("Hs"), IND(X, S("oPn")), F.Copy)
+        send_guests(t)
+        find2(1)
+        find3(0)
+        find3(1)
+        if t == 0:
+            ts(S("JT"), S("JTm"), 5.0, A.mult)
+        start(0)
+        own_places(0)
+        start(1)
+        own_places(1)
+        if t == 0:
+            consts_f()
+            consts_e()
+
+        def gather_s(c):
+            act(S("G", 1024 * (c - 2), 1024 * (c - 2) + 1024), IND(X, S("off", 64 * c, 64 * c + 64)), F.Copy)
+
+        def equal(c):
+            h = (64 * c, 64 * c + 64)
+            ts(S("Tf5", *h), S("vi", *h), 5.0, A.mult, 1.0 if c < 2 else 1929.0, A.add)
+            tt(S("eq", *h), S("vi", *h), S("b%d" % c, 384, 448), A.is_equal)
+        gather_s(2)
+        gather_s(3)
+        guests_come(t)
+        cast_in(S("FW", FX, FE), T[cur][:, 0:4096], [S(cur, 0, XE), S("Hl")], "fx%d" % t)
+        ub = {0: 4, 1: 6, 2: 6, 3: 4}
+
+        def sums(c):
+            for k in range(2):
+                ww = 2 * (c % 2) + k
+                b = "b%d" % (ub[c] + k)
+                mm(S(b), S("ident"), S("Pg", 512 * (c // 2), 512 * (c // 2) + 512), True, False)
+                for o in (0, 256):
+                    mm(S(b, o, o + 256 - 64 * ww), S("ident"), S("Hl", 64 * ww, 256), False, o == 256 and ww == 0)
+                    if ww:
+                        mm(S(b, o + 256 - 64 * ww, o + 256), S("ident"), S("Hl", 0, 64 * ww), False, o == 256)
+
+        def children(c):
+            for k in range(2):
+                b = S("b%d" % (ub[c] + k))
+                o = S("Zp", 1024 * c + 512 * k, 1024 * c + 512 * k + 512)
+                if c == 3:
+                    act(o, b, F.Relu, bias=-4080.0)
+                else:
+                    ts(o, b, -4080.0, A.add, 0.0, A.max)
+
+        def diff(c, ks=(0, 1)):
+            for k in ks:
+                b = "b%d" % (2 * c + k)
+                o = 1024 * (c - 2) + 512 * k
+                mm(S(b), S("ident"), S("Zp", 1024 * c + 512 * k, 1024 * c + 512 * k + 512), True, False)
+                mm(S(b), S("nident"), S("G", o, o + 512), False, True)
+
+        def sign(c, ks=(0, 1)):
+            for k in ks:
+                o = 1024 * c + 512 * k
+                act(S("cmp", o, o + 512), S("b%d" % (2 * c + k)), F.Sign, bias=-0.5)
+
+        def compare(c):
+            tt(S("cmp", 1024 * c, 1024 * c + 1024), IND(X, S("off", 64 * c, 64 * c + 64)), S("Zp", 1024 * c, 1024 * c + 1024), A.is_lt)
+
+        def total(c, n):
+            b = "b%d" % c
+            mm(S(b, 64 * n, 64 * n + 64), S("I3856"), S("eq", 64 * c, 64 * c + 64), True, False)
+            spread(b, 64 * n, 64, "EM241" if c < 2 else "EM120", "cmp", 1024 * c, False, True)
+
+        def update(c, n):
+            h = (64 * c, 64 * c + 64)
+            tt(S("t32", *h), S("b%d" % c, 64 * n, 64 * n + 64), S("Tf5", *h), A.add)
+
+        def wrap(c):
+            h = (64 * c, 64 * c + 64)
+            ts(S("vi", *h), S("t32", *h), 4095, A.bitwise_and)
+
+        def offs(c):
+            h = (64 * c, 64 * c + 64)
+            cp(S("off", *h), S("vi", *h))
+
+        def passed_probes(c, n0, n1):
+            ts(S("NZ", 384 * c + 64 * n0, 384 * c + 64 * n1), S("b%d" % c, 64 * n0, 64 * n1), 0.0 if c < 2 else -1928.0, A.not_equal)
+
+        def sum_ok(hf):
+            for ww in range(4):
+                o = 1536 + 128 * hf + 32 * ww
+                tt(S("NZ", o, o + 32), S("b1", 448 + 32 * hf, 480 + 32 * hf), S("shr", 4 * ww, 4 * ww + 32), A.is_le)
+
+        sums(0)
+        sums(2)
+        children(0)
+        for c in (0, 2, 1, 3):
+            equal(c)
+        sums(3)
+        children(2)
+        children(3)
+        sums(1)
+        diff(2)
+        compare(0)
+        children(1)
+        diff(3)
+        sign(2)
+        total(2, 0)
+        total(0, 0)
+        compare(1)
+        sign(3)
+        total(3, 0)
+        total(1, 0)
+        cast_in(S("Zf"), T.Zp[:, 2048:4096], [S("Zp", 2048, 4096)], "fz%d" % t)
+        do = {"a": update, "b": lambda c, n: wrap(c), "o": lambda c, n: offs(c), "e": lambda c, n: equal(c),
+              "g": lambda c, n: gather_s(c), "c": lambda c, n: compare(c), "t": lambda c, n: total(c, n + 1),
+              "x": lambda c, n: diff(c, (0,)), "y": lambda c, n: diff(c, (1,)),
+              "u": lambda c, n: sign(c, (0,)), "v": lambda c, n: sign(c, (1,))}
+        for n in range(5):
+            for k in LOOP.split():
+                if k == "s":
+                    if n == 0:
+                        spread("b1", 448, 64, "E", "Pg", 0, True, True)
+                        spread("b0", 448, 16, "E", "Hl", 0, True, True)
+                        for m in range(3):
+                            ts(S("shr", 16 * m, 16 * m + 16), S("b0", 448, 464), -1.0, A.mult, S("kap2"), A.add)
+                    elif n < 3:
+                        sum_ok(n - 1)
+                    else:
+                        for c in ((0, 2), (1, 3))[n - 3]:
+                            passed_probes(c, 0, n + 1)
+                elif (k, n) != ("t1", 4):
+                    do[k[0]](int(k[1]), n)
+
+        def tests(hf, early):
+            b = "b%d" % (4 + hf)
+            if early:
+                mm(S(b, 0, 128), S("ident"), S("NZ", 1536 + 128 * hf, 1664 + 128 * hf), True, False)
+            for n in (range(4) if early else (4, 5)):
+                for k in range(2):
+                    o = 384 * (2 * hf + k) + 64 * n
+                    mm(S(b, 64 * k, 64 * k + 64), S("ident"), S("NZ", o, o + 64), False, n == 5 and k == 1)
+
+        def passed(hf):
+            ts(S("AL", 128 * hf, 128 * hf + 128), S("b%d" % (4 + hf), 0, 128), 7.0, A.is_equal)
+
+        def alive(hf):
+            bs, bx, a0 = "b%d" % (2 * hf), "b%d" % (2 * hf + 1), 128 * hf
+            al = [S("AL", a0 + 32 * ww, a0 + 32 * ww + 32) for ww in range(4)]
+            for ww in range(4):
+                mm(S(bx, 0, 32), S("Bones"), al[ww], ww == 0, ww == 3)
+            for ww in range(4):
+                mm(S(bx, 32, 64), S("Ds"), al[ww], ww == 0, ww == 3)
+            for ww in range(4):
+                mm(S(bs, 32 * ww, 32 * ww + 32), S("I16384"), al[ww], True, ww == 0)
+                for w2 in range(ww):
+                    mm(S(bs, 32 * ww, 32 * ww + 32), S("ident"), al[w2], False, w2 == ww - 1)
+
+        def number(hf):
+            bs, bx, a0 = "b%d" % (2 * hf), "b%d" % (2 * hf + 1), 128 * hf
+            sc, pb = S("sc", 32 * hf, 32 * hf + 32), S("pb", 32 * hf, 32 * hf + 32)
+            scan(sc, S(bx, 0, 32), 32)
+            tt(pb, sc, S(bx, 32, 64), A.add)
+            for ww in range(4):
+                tt(S("of", a0 + 32 * ww, a0 + 32 * ww + 32), S(bs, 32 * ww, 32 * ww + 32), pb, A.add)
+
+        def offsets(hf):
+            a0 = 128 * hf
+            tt(S("mx", a0, a0 + 128), S("of", a0, a0 + 128), S("KT"), A.max)
+            ts(S("so", a0, a0 + 128), S("mx", a0, a0 + 128), float(SV - 16384), A.add)
+        tests(1, True)
+        passed_probes(2, 4, 6)
+        passed_probes(3, 5, 6)
+        passed_probes(0, 4, 6)
+        tests(1, False)
+        total(1, 5)
+        passed(1)
+        alive(1)
+        passed_probes(1, 5, 6)
+        tests(0, True)
+        tests(0, False)
+        number(1)
+        passed(0)
+        alive(0)
+        offsets(1)
+        act(IND(S("FW", SS, FX), S("so", 128, 256)), S("Zf"), F.Silu)
+        number(0)
+        offsets(0)
+        tt(S("nS"), S("m05"), S("sc", 31, 32), A.subtract)
+        ts(S("dA"), S("sc", 31, 32), -0.5, A.mult, 2048.0, A.add)
+        tt(S("nT"), S("nS"), S("sc", 63, 64), A.subtract)
+        act(S("g1"), S("W3", 0, 256), F.Sign, bias=S("nS"))
+        act(S("g2"), S("W3", 0, 256), F.Sign, bias=S("nT"))
+        act(S("g1"), S("g1"), F.Identity, bias=S("dA"), scale=S("dA"))
+        mm(S("b4", 0, 256), S("identF"), S("W3", 0, 256), True, False)
+        mm(S("b4", 0, 256), S("N16384"), S("Fl", 0, 256), False, False)
+        mm(S("b4", 0, 256), S("I8192"), S("g2"), False, False)
+        mm(S("b4", 0, 256), S("identF"), S("g1"), False, True)
+        cp(IND(S("FW", 0, SS), S("so", 0, 128)), S("Zp", 0, 2048))
+        tt(S("fo"), S("b4", 0, 256), S("VT"), A.min)
+        ts(S("fo16"), S("fo"), 24575.0, A.add)
+
+        def place(b):
+            win = IND(S("FW", SV, FE), S("fo16", 32 * b, 32 * b + 32))
+            o = S(nxt, 512 * b, 512 * b + 512)
+            if t < 2:
+                if b % 2 == 0:
+                    cp(o, win)
+                else:
+                    act(o, win, F.Copy)
+                return
+            if b % 2 == 0:
+                m = S("cmp", 512 * b, 512 * b + 512)
+                ts(m, win, -4079.986, A.add, 0.0, A.min)
+                ts(o, m, -0.0625, A.mult)
+            else:
+                act(o, win, F.Relu, bias=254.9991, scale=-0.0625)
+            op("sync", lambda: g.sync.dma_start(T.y[:, 512 * b:512 * b + 512], AP(o)), [o], [], "ys%d" % b, 16)
+        for k in range(4):
+            place(2 * k)
+            place(2 * k + 1)
+            if t < 2:
+                values(t + 1, 2 * k)
+                values(t + 1, 2 * k + 1)
+                if k:
+                    nonzero(t + 1, 2 * k - 2)
+                    nonzero(t + 1, 2 * k - 1)
+                    diagonal(2 * k - 2)
+                    diagonal(2 * k - 1)
+        if t < 2:
+            nonzero(t + 1, 6)
+            nonzero(t + 1, 7)
+            diagonal(6)
+            diagonal(7)
+    emit()

@@ -3,41 +3,37 @@ from concourse.bass import DstId, RemoteDMATransfer
 from concourse.mybir import dt, AluOpType as A, AxisListType, ActivationFunctionType as F
 
 XE, XC = 4096, 4128
-SV, SS, FX, FE = 2048, 4096, 8192, 12288
-SB = {
+D0, D1 = 1024, 256
+W0, WA, WB, FX, FE = 0, 3072, 4352, 6656, 10752
+OWN = {
     "BW0": (XC, "bfloat16"), "BW1": (XC, "bfloat16"), "FW": (FE, "float32"), "Zp": (4096, "bfloat16"),
-    "Zf": (2048, "float32"), "Pg": (1024, "bfloat16"), "Hs": (256, "bfloat16"), "Hl": (256, "bfloat16"),
-    "c1n": (256, "bfloat16"), "c2n": (256, "bfloat16"), "c3n": (256, "bfloat16"),
-    "c1p": (1024, "bfloat16"), "c2p": (1024, "bfloat16"), "c3p": (1024, "bfloat16"),
-    "cmp": (4096, "bfloat16"), "G": (2048, "bfloat16"), "dg": (128, "float32"),
-    "cown": (12, "float32"), "cl": (144, "float32"), "small": (16, "float32"), "lst": (160, "bfloat16"),
-    "qi": (16, "int32"), "qf": (16, "float32"), "Qblk": (128, "bfloat16"), "nQ4": (512, "bfloat16"), "kapT": (512, "float32"),
-    "pi": (1, "int32"), "p16i": (1, "int32"), "pgi": (1, "int32"), "pif": (1, "float32"), "p16f": (1, "float32"),
-    "pgf": (1, "float32"), "e15": (1, "float32"), "p37": (1, "float32"), "ci": (144, "int32"), "cg": (128, "int32"),
-    "Bones": (128, "bfloat16"), "BonesF": (128, "float32"), "ident": (128, "bfloat16"), "identF": (128, "float32"),
-    "nident": (128, "bfloat16"), "I3856": (128, "bfloat16"), "I16384": (128, "bfloat16"), "I8192": (128, "bfloat16"),
-    "N16384": (128, "bfloat16"), "EM1": (144, "bfloat16"), "I16": (128, "bfloat16"),
-    "EM241": (144, "bfloat16"), "EM120": (144, "bfloat16"), "E": (144, "bfloat16"), "M16f": (16, "float32"),
-    "mask16": (16, "float32"), "base": (16, "float32"), "obig": (16, "float32"), "rown": (48, "float32"),
-    "Dm": (128, "bfloat16"), "Ds": (128, "bfloat16"), "dtmp": (128, "bfloat16"),
-    "B4080": (128, "bfloat16"), "c4080": (128, "bfloat16"), "Ji": (602, "int32"), "Jm": (602, "int32"), "JF": (602, "float32"),
-    "IF": (1024, "float32"), "IU": (1024, "uint16"), "JTi": (384, "int32"), "JTk": (384, "int32"), "JTm": (384, "int32"),
-    "JT": (384, "float32"), "VTi": (256, "int32"), "VT": (256, "float32"), "KT": (128, "float32"),
-    "onesF": (256, "float32"), "W2": (48, "float32"), "W3": (528, "float32"),
-    "mn": (1, "float32"), "oh": (16, "float32"), "cq": (16, "float32"), "csel": (1, "float32"),
-    "csb": (1, "bfloat16"), "kaps": (1, "float32"), "kap2": (1, "float32"), "Fl": (512, "bfloat16"), "T2b": (32, "bfloat16"),
-    "I3": (512, "float32"), "I2": (32, "float32"), "bt": (32, "float32"), "bnd": (8, "float32"),
-    "oAn": (16, "uint16"), "oQn": (16, "uint16"), "oPn": (16, "uint16"), "oAp": (64, "uint16"), "oQp": (64, "uint16"),
-    "oPp": (64, "uint16"), "A17": (64, "float32"), "AF": (64, "float32"),
-    "t32": (256, "int32"), "vi": (256, "int32"), "off": (256, "uint16"), "Tf5": (256, "float32"), "eq": (256, "bfloat16"),
-    "NZ": (1792, "bfloat16"), "shr": (48, "float32"), "AL": (256, "bfloat16"), "sc": (64, "float32"), "pb": (64, "float32"),
-    "of": (256, "float32"), "mx": (256, "float32"), "so": (256, "uint16"),
-    "g1": (256, "float32"), "g2": (256, "bfloat16"), "fo": (256, "float32"), "fo16": (256, "uint16"),
+    "Zf": (4096, "float32"), "Pg": (1024, "bfloat16"), "Hs": (256, "bfloat16"), "Hl": (256, "bfloat16"),
+    "cmp": (4096, "bfloat16"), "G": (2048, "bfloat16"), "nzR": (4096, "bfloat16"), "nzC": (4096, "bfloat16"),
+    "qi": (16, "int32"), "rown": (48, "float32"), "cl": (144, "float32"),
 }
-PART = {"lAn": ("lst", 0, 16), "lQn": ("lst", 16, 16), "lAp": ("lst", 32, 64), "lQp": ("lst", 96, 64),
-        "m05": ("small", 0, 1), "nT": ("small", 4, 1), "nS": ("small", 8, 1), "dA": ("small", 12, 1)}
+POOL = {
+    "bfloat16": {"c1n": 256, "c2n": 256, "c3n": 256, "c1p": 1024, "c2p": 1024, "c3p": 1024, "lAn": 16, "lQn": 16, "lAp": 64,
+                 "lQp": 64, "Qblk": 128, "nQ4": 512, "Bones": 128, "ident": 128, "nident": 128, "I3856": 128, "I1928": 128,
+                 "I16384": 128, "I1280": 128, "EM1": 144, "EMh": 144, "I16": 128, "EM241": 144, "EM120": 144, "E": 144,
+                 "Dm": 128, "Ds": 128, "Dn": 128, "dtmp": 128, "B4080": 128, "c4080": 128, "csb": 1, "Fl": 512, "T2b": 32,
+                 "eq": 256, "AL": 256, "lt": 256, "keep": 256, "far": 256, "wT": 512, "onesB": 64},
+    "float32": {"dg": 128, "cown": 1, "qf": 16, "kapT": 512, "pif": 1, "p16f": 1, "pgf": 1, "e15": 1, "p37": 1, "BonesF": 128,
+                "identF": 128, "M16f": 16, "mask16": 16, "mask24": 24, "base": 16, "obig": 16, "JF": 602, "IF": 1024, "JT": 384,
+                "VT": 256, "KT": 256, "onesF": 256, "W2": 48, "W3": 528, "mn": 1, "oh": 16, "cq": 16, "csel": 1, "kaps": 1,
+                "kap2": 1, "I3": 512, "I2": 32, "bt": 32, "bn": 1, "bp": 1, "A17": 64, "AF": 64, "Tf5": 256, "shr": 48,
+                "sc": 64, "pb": 64, "of": 256, "mx": 256, "uu": 256, "g1": 256, "fo": 256, "nm": 1, "dA": 1, "l0": 1, "l1": 1},
+    "int32": {"pi": 1, "p16i": 1, "pgi": 1, "ci": 144, "cg": 128, "c8": 24, "Ji": 602, "Jm": 602, "JTi": 384, "JTk": 384,
+              "JTm": 384, "VTi": 256, "t32": 256, "vi": 256},
+    "uint16": {"oAn": 16, "oQn": 16, "oPn": 16, "oAp": 64, "oQp": 64, "oPp": 64, "off": 256, "so": 256, "fo16": 256},
+}
+SB, PART = dict(OWN), {}
+for _d, _names in POOL.items():
+    _o = 0
+    for _n, _c in _names.items():
+        PART[_n] = ("all_" + _d, _o, _c)
+        _o += -(-_c // 16) * 16
+    SB["all_" + _d] = (_o, _d)
 for _t in range(3):
-    PART["cown%d" % _t] = ("cown", 4 * _t, 1)
     PART["rown%d" % _t] = ("rown", 16 * _t, 16)
     PART["cl%d" % _t] = ("cl", 48 * _t, 48)
 SCRATCH = {n: ("sbuf", [128, -(-c // 16) * 16], d) for n, (c, d) in SB.items()}
@@ -46,58 +42,154 @@ for _b in range(8):
 NX = 8
 QSEM = {"tensor": "sT", "vector": "sV", "scalar": "sS", "g": "sG"}
 SEMAPHORES = (["sT", "sV", "sS", "sG", "qld"] + ["xl%d" % i for i in range(NX)] + ["ys%d" % i for i in range(8)]
-              + ["%s%d" % (s, t) for s in ("cs", "gs", "lc", "lg", "fx", "fz") for t in range(3)])
+              + ["%s%d" % (s, t) for s in ("cs", "gs", "lc", "lg", "fx", "fy", "fz") for t in range(3)])
 XS = (1, 2, 3)
 BIG = 1048576.0
-LOOP = "a2 b2 o2 a0 g2 e2 b0 a3 x2 b3 y2 o0 o3 c0 a1 g3 e0 u2 v2 b1 e3 s y3 v3 x3 o1 t2 e1 u3 t0 c1 t3 t1"
 CE = 4
+CY, PE, GATH, SCAT, LAT, DMA, FAR, RATE = 0.83, 0.42, 1.56, 3.8, 150.0, 1500.0, 2200.0, 200.0
+LOOK = 300.0
+OPT = {}
 
 
 def make_queue(g, T):
-    ops, hist = [], {}
+    ops, hist, runs, last, held = [], {}, {}, {}, {}
     eng = {"tensor": g.tensor, "vector": g.vector, "scalar": g.scalar, "sync": g.sync, "g": g}
 
-    def op(q, fn, reads, writes, sem=None, val=0, remote=False):
+    def hold(on):
+        held.clear()
+        held.update(last if on else {})
+
+    def width(x):
+        return 16 * (x[2][2] - x[2][1]) if x[0] == "IND" else x[3].shape[1]
+
+    def size(x):
+        return 2 if x[0] in SB and SB[x[0]][1] in ("bfloat16", "uint16") else 4
+
+    def length(q, kind, reads, writes):
+        if q is None:
+            return 0.0, 0.0
+        o, i = (writes + reads)[0], (reads + writes)[0]
+        if kind == "remote":
+            return 500.0, FAR + 128 * width(i) * size(i) / 50.0
+        if kind == "dma":
+            return (600.0 if q == "g" else 60.0), DMA + 128 * width(o) * size(o) / RATE
+        if q == "tensor":
+            return sum(size(r) ** 2 / 4 * max(64, width(r)) * PE for r in reads[1::2]), LAT
+        n = width(i)
+        if o[0] == "IND" or i[0] == "IND":
+            return 55 + n * CY * (SCAT if o[0] == "IND" else GATH), LAT
+        if q == "g":
+            return 130 + 2 * n * CY, LAT
+        if kind == "tt" and reads[0][0] in SB and reads[1][0] in SB:
+            n = 2 * n
+        elif kind == "half" and size(o) == 2 and size(i) == 2:
+            n = n / 2
+        return max(64, n) * CY, LAT
+
+    def op(q, fn, reads, writes, sem=None, val=0, kind="", after=None, lead=0.0, late=0.0):
         me = len(ops)
-        rec = {"q": q, "fn": fn, "deps": set(), "sem": sem, "val": val, "need": False, "m": [], "remote": remote}
+        c, lat = length(q, kind, reads, writes)
+        rec = {"q": q, "fn": fn, "deps": set(), "ord": set(), "sem": sem, "val": val, "need": False, "m": [],
+               "remote": kind == "remote", "cost": c, "lat": lat + late, "lead": lead, "w": (writes + reads)[0][:3]}
+        rec["ord"].update(x for x in (after, held.get(q)) if x is not None)
+        last[q] = me
         acc = []
-        for w in writes:
-            if w[0] == "IND":
-                acc += [(w[1], True), (w[2], False)]
-            else:
-                acc.append((w, True))
-        for r in reads:
-            if r[0] == "IND":
-                acc += [(r[1], False), (r[2], False)]
-            else:
-                acc.append((r, False))
+        for x, isw in [(w, True) for w in writes] + [(r, False) for r in reads]:
+            acc += [(x[1], isw), (x[2], False)] if x[0] == "IND" else [(x, isw)]
 
         def mine(o):
             return o["q"] == q and o["sem"] is None
         for (n, a, b, _ap), isw in acc:
-            ps = n[0] == "b" and len(n) == 2
-            for (oa, ob, o, ow) in hist.setdefault(n, []):
-                if o == me:
-                    continue
-                hit = oa < b and a < ob
-                if mine(ops[o]):
-                    need = hit and ow and not (ps and q == "tensor")
-                else:
-                    need = ps or (hit and (ow or isw))
-                if need:
-                    rec["deps"].add(o)
+            h = hist.setdefault(n, ([], []))
+            for (oa, ob, o, ow) in (h[0] + h[1] if isw else h[0]):
+                if o != me and oa < b and a < ob:
+                    rec["ord" if mine(ops[o]) and (not ow or q == "tensor") else "deps"].add(o)
+            if n not in SB:
+                r = runs.setdefault(n, [q, [], []])
+                if r[0] != q:
+                    r[0], r[1], r[2] = q, [], r[1]
+                rec["deps"].update(r[2])
+                if me not in r[1][-1:]:
+                    if q == "tensor":
+                        rec["ord"].update(r[1][-1:])
+                    r[1].append(me)
         ops.append(rec)
         for (n, a, b, _ap), isw in acc:
-            ps = n[0] == "b" and len(n) == 2
-            keep = []
-            for e in hist[n]:
-                inside = a <= e[0] and e[1] <= b
-                if e[2] != me and ((inside and isw) or (inside and not e[3] and mine(ops[e[2]]))
-                                   or (ps and not mine(ops[e[2]]) and not e[3])):
+            h = hist[n]
+            if isw and _ap.shape[1] == b - a:
+                for l in h:
+                    l[:] = [e for e in l if e[2] == me or not (a <= e[0] and e[1] <= b)]
+            h[0 if isw else 1].append((a, b, me, isw))
+        return me
+
+    def order():
+        n = len(ops)
+        pre = [[(d, ops[d]["lat"]) for d in r["deps"]] + [(d, ops[d]["lat"] if ops[d]["remote"] else 0.0) for d in r["ord"] - r["deps"]]
+               for r in ops]
+        post = [[] for _ in ops]
+        for i in range(n):
+            for d, lat in pre[i]:
+                post[d].append((i, lat))
+
+        def lay(seq, before):
+            start, used = [0.0] * n, {q: [] for q in eng}
+            for i in seq:
+                r = ops[i]
+                t = max([start[d] + ops[d]["cost"] + lat for d, lat in before[i]] + [0.0])
+                if r["q"] is not None:
+                    u = used[r["q"]]
+                    k = len(u)
+                    while k > 0 and u[k - 1][1] > t:
+                        k -= 1
+                    while k < len(u) and u[k][0] < t + r["cost"]:
+                        t = max(t, u[k][1])
+                        k += 1
+                    u.insert(k, (t, t + r["cost"]))
+                start[i] = t
+            return start
+        way = [0.0] * n
+        for i in reversed(range(n)):
+            way[i] += ops[i]["cost"] + ops[i]["lead"]
+            for d, lat in pre[i]:
+                way[d] = max(way[d], way[i] + lat)
+        left, ready, start = [len(p) for p in pre], [0.0] * n, [0.0] * n
+        free, can = {q: 0.0 for q in list(eng) + [None]}, {q: [] for q in list(eng) + [None]}
+        for i in range(n):
+            if not left[i]:
+                can[ops[i]["q"]].append(i)
+        for _ in range(n):
+            pick = None
+            for q, c in can.items():
+                if not c:
                     continue
-                keep.append(e)
-            keep.append((a, b, me, isw))
-            hist[n] = keep
+                t = max(free[q], min(ready[i] for i in c))
+                now = [i for i in c if ready[i] <= t]
+                i = max(now, key=lambda k: way[k])
+                for j in c:
+                    if t < ready[j] < t + min(LOOK, ops[i]["cost"]) and way[j] > way[i]:
+                        i = max([k for k in now if t + ops[k]["cost"] <= ready[j]] or [j], key=lambda k: way[k])
+                        break
+                if pick is None or max(free[q], ready[i]) < pick[0]:
+                    pick = (max(free[q], ready[i]), q, i)
+            t, q, i = pick
+            can[q].remove(i)
+            start[i] = t
+            if q is not None:
+                free[q] = t + ops[i]["cost"]
+            for j, lat in post[i]:
+                ready[j] = max(ready[j], t + ops[i]["cost"] + lat)
+                left[j] -= 1
+                if not left[j]:
+                    can[ops[j]["q"]].append(j)
+        best = start
+        for _ in range(OPT.get("it", 2)):
+            back = lay(sorted(range(n), key=lambda k: (-start[k] - ops[k]["cost"], -k)), post)
+            start = lay(sorted(range(n), key=lambda k: (-back[k] - ops[k]["cost"], k)), pre)
+            if max(start) < max(best):
+                best = start
+        OPT["span"] = max(best)
+        OPT["dbg"] = (ops, pre, way, best)
+        return sorted(range(n), key=lambda k: (best[k], k))
 
     def emit():
         for r in ops:
@@ -105,18 +197,18 @@ def make_queue(g, T):
                 ops[d]["need"] = True
         cnt = {q: 0 for q in QSEM}
         know = {q: {} for q in eng}
-        for r in ops:
+        for r in [ops[i] for i in order()]:
             q = r["q"]
             if q is None:
                 r["clock"] = {r["sem"]: r["val"], "own": r["sem"]}
                 continue
             k = know[q]
             todo = {}
-            for d in sorted(r["deps"], reverse=True):
+            for d in r["deps"]:
                 o = ops[d]
                 s, v = (o["sem"], o["val"]) if o["sem"] is not None else (QSEM[o["q"]], o["at"])
-                if k.get(s, 0) < v and todo.get(s, 0) < v:
-                    todo[s] = v
+                if k.get(s, 0) < v:
+                    todo[s] = max(v, todo.get(s, 0))
                     r["m"].append(o["clock"])
             for s in sorted(todo):
                 if not any(c["own"] != s and c.get(s, 0) >= todo[s] for c in r["m"]):
@@ -126,15 +218,14 @@ def make_queue(g, T):
                     if s != "own" and k.get(s, 0) < v:
                         k[s] = v
             ins = r["fn"]()
+            c = dict(k)
             if r["sem"] is not None:
-                c = dict(k)
                 c[r["sem"]] = r["val"]
                 c["own"] = r["sem"]
                 if not r["remote"]:
                     ins.then_inc(T.sem[r["sem"]], r["val"])
             else:
                 s = QSEM[q]
-                c = dict(k)
                 c["own"] = s
                 if r["need"]:
                     cnt[q] += 1
@@ -149,19 +240,22 @@ def make_queue(g, T):
             if r["sem"] is not None and r["sem"][:2] in ("ys", "lc", "lg"):
                 g.wait_ge(T.sem[r["sem"]], r["val"])
 
-    return op, emit
+    return op, hold, emit
 
 
 def rank_program(g, core, T, topo):
     rank = T.rank_of(core)
     if rank is None:
         return
-    op, emit = make_queue(g, T)
+    op, hold, emit = make_queue(g, T)
 
     def S(n, a=0, b=None, st=1):
         n, o, w = PART.get(n, (n, 0, SB[n][0] if n in SB else 512))
         a, b = a + o, (w if b is None else b) + o
         return (n, a, b, T[n][:, a:b] if st == 1 else T[n][:, a:b:st])
+
+    def B(k, a=0, b=None, st=1):
+        return S("b%d" % k, a, b, st)
 
     def IND(w, o):
         return ("IND", w, o)
@@ -172,45 +266,49 @@ def rank_program(g, core, T, topo):
     def num(x):
         return isinstance(x, (int, float))
 
-    def cp(out, in_):
-        op("vector", lambda: g.vector.tensor_copy(AP(out), AP(in_)), [in_], [out])
+    def cp(out, in_, lead=0.0):
+        op("vector", lambda: g.vector.tensor_copy(AP(out), AP(in_)), [in_], [out], kind="half", lead=lead)
 
     def tt(out, a, b, o):
-        op("vector", lambda: g.vector.tensor_tensor(AP(out), AP(a), AP(b), o), [a, b], [out])
+        op("vector", lambda: g.vector.tensor_tensor(AP(out), AP(a), AP(b), o), [a, b], [out], kind="tt")
 
     def ts(out, a, s1, o0, s2=None, o1=None):
         cols = [x for x in (s1, s2) if x is not None and not num(x)]
         u1 = s1 if num(s1) else AP(s1)
         if o1 is None:
-            op("vector", lambda: g.vector.tensor_scalar(AP(out), AP(a), u1, None, o0), [a] + cols, [out])
+            op("vector", lambda: g.vector.tensor_scalar(AP(out), AP(a), u1, None, o0), [a] + cols, [out], kind="half")
         else:
             u2 = s2 if num(s2) else AP(s2)
-            op("vector", lambda: g.vector.tensor_scalar(AP(out), AP(a), u1, u2, o0, o1), [a] + cols, [out])
+            op("vector", lambda: g.vector.tensor_scalar(AP(out), AP(a), u1, u2, o0, o1), [a] + cols, [out], kind="half")
 
     def red(out, a, o):
         op("vector", lambda: g.vector.tensor_reduce(AP(out), AP(a), AxisListType.X, o), [a], [out])
 
-    def scan(out, a, n):
+    def scan(out, a, n, first=0.0):
         one = S("onesF", 0, n)
-        op("vector", lambda: g.vector.tensor_tensor_scan(AP(out), AP(one), AP(a), 0.0, A.mult, A.add), [one, a], [out])
+        op("vector", lambda: g.vector.tensor_tensor_scan(AP(out), AP(one), AP(a), first, A.mult, A.add), [one, a], [out])
 
     def fill(out, c):
-        op("vector", lambda: g.vector.memset(AP(out), c), [], [out])
+        op("vector", lambda: g.vector.memset(AP(out), c), [], [out], kind="half")
 
-    def act(out, a, f, bias=0.0, scale=1.0):
+    def act(out, a, f, bias=0.0, scale=1.0, lead=0.0):
         if f == F.Silu:
-            op("scalar", lambda: g.scalar.activation(AP(out), AP(a), f), [a], [out])
+            op("scalar", lambda: g.scalar.activation(AP(out), AP(a), f), [a], [out], lead=lead)
         else:
             cols = [x for x in (bias, scale) if not num(x)]
             ub, us = bias if num(bias) else AP(bias), scale if num(scale) else AP(scale)
             op("scalar", lambda: g.scalar.activation(AP(out), AP(a), f, bias=ub, scale=us), [a] + cols, [out])
 
     def mm(out, l, r, start, stop):
-        op("tensor", lambda: g.tensor.matmul(AP(out), AP(l), AP(r), start, stop), [l, r], [out])
+        mms([(out, l, r, start, stop)])
+
+    def mms(calls):
+        op("tensor", lambda: [g.tensor.matmul(AP(o), AP(l), AP(r), a, b) for o, l, r, a, b in calls][-1],
+           [x for c in calls for x in c[1:3]], [c[0] for c in calls])
 
     def spread(bank, c0, n, emat, src, s0, start, stop):
-        for p in range(16):
-            mm(S(bank, c0, c0 + n), S(emat, 15 - p, 143 - p), S(src, s0 + p, s0 + 16 * n, 16), start and p == 0, stop and p == 15)
+        mms([(B(bank, c0, c0 + n), S(emat, 15 - p, 143 - p), S(src, s0 + p, s0 + 16 * n, 16), start and p == 0, stop and p == 15)
+             for p in range(16)])
 
     def iota(out, pattern, base=0, cm=0, fl=False):
         if fl:
@@ -218,24 +316,24 @@ def rank_program(g, core, T, topo):
         else:
             op("g", lambda: g.iota(AP(out), pattern, base, cm), [], [out])
 
-    def cast_in(out, in_ap, reads, sem):
-        op("g", lambda: g.dma_start(AP(out), in_ap), reads, [out], sem, 16)
+    def cast_in(out, in_, sem, also=()):
+        op("g", lambda: g.dma_start(AP(out), AP(in_)), [in_] + list(also), [out], sem, 16, "dma")
 
-    op("sync", lambda: g.sync.dma_start(T.qi[:, 0:16], T.q[:]), [], [S("qi")], "qld", 16)
+    op("sync", lambda: g.sync.dma_start(T.qi[:, 0:16], T.q[:]), [], [S("qi")], "qld", 16, "dma")
     w = 4096 // NX
 
     def load(i, q):
         o = S("BW1", w * i, w * i + w)
-        op(q, lambda: (g.sync if q == "sync" else g.scalar).dma_start(AP(o), T.x[:, w * i:w * i + w]), [], [o], "xl%d" % i, 16)
+        op(q, lambda: (g.sync if q == "sync" else g.scalar).dma_start(AP(o), T.x[:, w * i:w * i + w]), [], [o], "xl%d" % i, 16, "dma",
+           late=i * 256 * w / RATE)
     for i in range(NX):
+        hold(True)
         load(i, "sync" if i % 2 else "scalar")
+    hold(False)
     iota(S("pi"), [[1, 1]], 0, 1)
     iota(S("ci"), [[1, 144]])
     iota(S("Ji"), [[37, 602]])
     iota(S("IF"), [[1, 1024]], 0, 0, True)
-    iota(S("JTi"), [[1, 3], [64, 4], [592, 32]])
-    iota(S("VTi"), [[16, 256]], FX - SV)
-    iota(S("KT"), [[16, 128]], 16384 - SV, 0, True)
     ts(S("pgi"), S("pi"), 4, A.arith_shift_right)
     ts(S("cg"), S("ci", 0, 128), 4, A.arith_shift_right)
     ts(S("p16i"), S("pi"), 15, A.bitwise_and)
@@ -248,63 +346,60 @@ def rank_program(g, core, T, topo):
         ts(S("Qblk", 16 * k, 16 * k + 16), S("qi"), S("BonesF", 16 * k, 16 * k + 1), A.mult)
     ts(S("M16f"), S("ci", 0, 16), S("p16f"), A.is_equal, 16.0, A.mult)
     cp(S("base"), S("ci", 0, 16))
-    tt(S("e15"), S("pif"), S("p16f"), A.subtract)
+    ts(S("e15"), S("pif"), S("p16f"), A.subtract, 15.0, A.add)
+    cp(S("qf"), S("qi"))
+    ts(S("dtmp"), S("ci", 0, 128), S("pif"), A.is_lt, -1.0, A.mult)
+    ts(S("EM1"), S("ci"), S("e15"), A.is_equal)
+    act(S("Bones"), S("BonesF"), F.Copy)
+    act(S("B4080"), S("BonesF"), F.Copy, scale=4080.0)
+    tt(S("Dm"), S("dtmp"), S("BonesF"), A.mult)
+    for n, s in (("EMh", -0.5), ("EM241", 241.0), ("EM120", 120.5)):
+        act(S(n), S("EM1"), F.Copy, scale=s)
+    for n, s in (("ident", 1.0), ("I16", 16.0), ("nident", -1.0), ("I3856", 3856.0), ("I1928", 1928.0), ("I16384", 16384.0),
+                 ("I1280", float(WB - WA))):
+        act(S(n), S("identF"), F.Copy, scale=s)
+    tt(S("Ds"), S("Dm"), S("identF"), A.subtract)
+    tt(S("Dn"), S("Dm"), S("I16384"), A.subtract)
+    fill(S("BW0", XE, XC), 0.0)
+    ts(S("mask16"), S("M16f"), 0.0625, A.mult)
+    fill(S("onesF"), 1.0)
+    fill(S("onesB"), 1.0)
+    for a, b in ((16, 24), (40, 48)):
+        fill(S("W2", a, b), 1000000.0)
+    for a, b in ((256, 264), (520, 528)):
+        fill(S("W3", a, b), 1000000.0)
+    ts(S("p37"), S("p16f"), 37.0, A.mult)
+    fill(S("c4080"), 4080.0)
 
-    def consts_a():
-        ts(S("e15"), S("e15"), 15.0, A.add)
-        cp(S("qf"), S("qi"))
-        ts(S("dtmp"), S("ci", 0, 128), S("pif"), A.is_lt, -1.0, A.mult)
-        ts(S("EM1"), S("ci"), S("e15"), A.is_equal)
-        act(S("Bones"), S("BonesF"), F.Copy)
-        act(S("B4080"), S("BonesF"), F.Copy, scale=4080.0)
-        act(S("ident"), S("identF"), F.Copy)
-        tt(S("Dm"), S("dtmp"), S("BonesF"), A.mult)
-        act(S("I16"), S("identF"), F.Copy, scale=16.0)
+    def constants():
+        iota(S("JTi"), [[1, 3], [64, 4], [592, 32]])
+        iota(S("c8"), [[0, 3], [1, 8]])
+        iota(S("VTi"), [[16, 256]], FX - D0 - 16383)
+        iota(S("KT", 0, 128), [[0, 2], [16, 64]], 16384 - D0, 0, True)
+        iota(S("KT", 128, 256), [[0, 8], [16, 16]], 16384 - D1, 0, True)
         for b in range(8):
             o, i = S("BW0", 512 * b, 512 * b + 512), S("BW1", 512 * b, 512 * b + 512)
             if b in (2, 5, 7):
                 act(o, i, F.Identity, bias=4080.0, scale=-16.0)
             else:
                 ts(o, i, -16.0, A.mult, 4080.0, A.add)
-        fill(S("BW0", XE, XC), 0.0)
         fill(S("BW1", XE, XC), 0.0)
-        ts(S("mask16"), S("M16f"), 0.0625, A.mult)
-        fill(S("onesF"), 1.0)
-        for a, b in ((16, 24), (40, 48)):
-            fill(S("W2", a, b), 1000000.0)
-        for a, b in ((256, 264), (520, 528)):
-            fill(S("W3", a, b), 1000000.0)
-
-    def consts_b():
-        for n, s in (("EM241", 241.0), ("EM120", 120.5)):
-            act(S(n), S("EM1"), F.Copy, scale=s)
-        for n, s in (("nident", -1.0), ("I3856", 3856.0), ("I16384", 16384.0), ("I8192", 8192.0), ("N16384", -16384.0)):
-            act(S(n), S("identF"), F.Copy, scale=s)
-        for k in range(3):
-            act(S("FW", SV + 2048 * k, SV + 2048 * k + 2048), S("BW1", 0, 2048), F.Copy)
+        ts(S("mask24"), S("c8"), S("pgf"), A.is_equal)
+        for a in range(D0, FX, 512):
+            act(S("FW", a, a + 512), S("BW1", 0, 512), F.Silu)
         ts(S("Jm"), S("Ji"), 255, A.bitwise_and)
-        fill(S("m05"), -0.5)
-        ts(S("p37"), S("p16f"), 37.0, A.mult)
         cp(S("JF"), S("Jm"))
-
-    def consts_c():
         ts(S("JTk"), S("JTi"), S("p37"), A.add)
         ts(S("JTm"), S("JTk"), 255, A.bitwise_and)
-
-    def consts_f():
-        tt(S("Ds"), S("Dm"), S("identF"), A.subtract)
-        ts(S("VT"), S("VTi"), S("p16f"), A.add, -24575.0, A.add)
+        ts(S("JT"), S("JTm"), 5.0, A.mult)
+        ts(S("VT"), S("VTi"), S("p16f"), A.add)
         ts(S("KT"), S("KT"), S("p16f"), A.add)
-
-    def consts_d():
-        cp(S("IU"), S("IF"))
-
-    def consts_e():
         for k in range(4):
             act(S("nQ4", 128 * k, 128 * k + 128), S("Qblk"), F.Copy, scale=-1.0)
-        fill(S("c4080"), 4080.0)
-        mm(S("b5"), S("c4080"), S("nQ4"), True, True)
-        act(S("kapT"), S("b5"), F.Copy, scale=-1.0)
+        for b in range(1, 8, 2):
+            act(S("nzR", 512 * b, 512 * b + 512), S("nzR", 512 * b, 512 * b + 512), F.Abs)
+        mm(B(6), S("c4080"), S("nQ4"), True, True)
+        act(S("kapT"), B(6), F.Copy, scale=-1.0)
 
     peers = [r for r in range(len(T.cores)) if r != rank]
     peers.sort(key=lambda r: len(topo.engines(core, T.cores[r])))
@@ -323,8 +418,8 @@ def rank_program(g, core, T, topo):
                 tr.append(RemoteDMATransfer(dst_ids=[DstId(rid=rid, pnc=pid)], dma_engine_mask=m, remote_sem=T.sem["cs%d" % t],
                                             src=AP(S("rown%d" % t)), dst=AP(S("cl%d" % t, 16 * c, 16 * c + 16))))
             return g.remote_dma_fused(tr, local_sem=T.sem["lc%d" % t])
-        op("g", f, [S("rown%d" % t)], [], "lc%d" % t, CE * len(peers), True)
-        op(None, None, [], [S("cl%d" % t)], "cs%d" % t, CE * len(peers))
+        i = op("g", f, [S("rown%d" % t)], [], "lc%d" % t, CE * len(peers), "remote", late=0.0 if t else 2000.0)
+        op(None, None, [], [S("cl%d" % t)], "cs%d" % t, CE * len(peers), after=i)
 
     def send_guests(t):
         dst = T.cores[rank ^ XS[t]]
@@ -333,373 +428,291 @@ def rank_program(g, core, T, topo):
         def f():
             rid, pid, _s = topo.addr(dst)
             return g.remote_dma(T.Hl[:, 0:256], T.Hs[:, 0:256], T.sem["gs%d" % t], T.sem["lg%d" % t], pid, rid, sum(1 << e for e in es))
-        op("g", f, [S("Hs")], [], "lg%d" % t, len(es), True)
+        i = op("g", f, [S("Hs")], [], "lg%d" % t, len(es), "remote")
+        op(None, None, [], [S("Hl")], "gs%d" % t, len(topo.engines(dst, core)[:8]), after=i)
 
-    def guests_come(t):
-        src = T.cores[rank ^ XS[t]]
-        op(None, None, [], [S("Hl")], "gs%d" % t, len(topo.engines(src, core)[:8]))
+    def values(bank, c0, xs, k, start=True, stop=True):
+        o = 2048 * (k // 16)
+        mm(B(bank, c0, c0 + 128), S(xs, o + k % 16, o + 2048, 16), S("Qblk"), start, stop)
 
-    def values(t, b):
-        xs, bank = "BW1" if t < 2 else "BW0", "b%d" % (b % 7)
-        shift = t > 0 and b % 2 == 1
-        if shift:
-            mm(S(bank), S("c4080"), S("nQ4"), True, False)
-        for k in range(4):
-            mm(S(bank, 128 * k, 128 * k + 128), S(xs, 512 * b + 128 * k, 512 * b + 128 * k + 128), S("Qblk"), not shift,
-               not shift or k == 3)
+    def weigh(c0, nz, h, w0, start, stop):
+        for k in range(0, 16, 8):
+            mms([(B(5, c0, c0 + 8), S(nz, 2048 * h + 128 * p, 2048 * h + 128 * p + 128), S("wT", w0 + p, w0 + 128, 16),
+                  start and p == 0, stop and p == 15) for p in range(k, k + 8)])
 
-    def nonzero(t, b):
-        bank, o = S("b%d" % (b % 7)), S("cmp", 512 * b, 512 * b + 512)
-        if b % 2 == 1:
-            act(o, bank, F.Sign)
-        elif t == 0:
-            ts(o, bank, 0.0, A.not_equal)
-        else:
-            tt(o, bank, S("kapT"), A.not_equal)
-
-    def diagonal(b):
-        for k in range(4):
-            c = S("cmp", 512 * b + 128 * k, 512 * b + 128 * k + 128)
-            mm(S("b7", 0, 128), c, c, b == 0 and k == 0, b == 7 and k == 3)
-
-    for b in range(4):
-        values(0, b)
     for b in range(8):
-        nonzero(0, b)
-        diagonal(b)
-        if b < 4:
-            values(0, b + 4)
-    for t in range(3):
-        cur, nxt = ("BW0", "BW1") if t % 2 == 0 else ("BW1", "BW0")
-        X = S(cur, 0, XC)
-        cown, rown = S("cown%d" % t), S("rown%d" % t)
-        tt(S("dg"), S("b7", 0, 128), S("identF"), A.mult)
-        red(cown, S("dg"), A.add)
-        ts(rown, S("M16f"), cown, A.mult)
+        for k in range(4):
+            values(b % 7, 128 * k, "BW1", 4 * b + k)
+        o = S("nzR", 512 * b, 512 * b + 512)
+        if b % 2:
+            act(o, B(b % 7), F.Sign)
+        else:
+            ts(o, B(b % 7), 0.0, A.not_equal)
+        for k in range(4):
+            c = S("nzR", 512 * b + 128 * k, 512 * b + 128 * k + 128)
+            mm(B(7, 0, 128), c, c, b == 0 and k == 0, b == 7 and k == 3)
+    tt(S("dg"), B(7, 0, 128), S("identF"), A.mult)
+    red(S("cown"), S("dg"), A.add)
+
+    def choose(t):
+        rown = S("rown%d" % t)
+        ts(rown, S("M16f"), S("cown"), A.mult)
         send_counts(t)
-        mm(S("b0", 0, 16), S("identF"), S("base"), True, False)
-        mm(S("b0", 0, 16), S("BonesF"), rown, False, False)
         if t == 0:
-            consts_a()
-        if t == 1:
-            consts_d()
+            hold(True)
+            constants()
+            hold(False)
+        mm(B(0, 0, 16), S("identF"), S("base"), True, False)
+        mm(B(0, 0, 16), S("BonesF"), rown, False, False)
         for k in range(3):
-            mm(S("b0", 0, 16), S("BonesF"), S("cl%d" % t, 16 * k, 16 * k + 16), False, k == 2)
-        red(S("mn"), S("b0", 0, 16), A.min)
-        ts(S("oh"), S("b0", 0, 16), S("mn"), A.is_equal)
+            mm(B(0, 0, 16), S("BonesF"), S("cl%d" % t, 16 * k, 16 * k + 16), False, k == 2)
+        red(S("mn"), B(0, 0, 16), A.min)
+        ts(S("oh"), B(0, 0, 16), S("mn"), A.is_equal)
         tt(S("cq"), S("oh"), S("qf"), A.mult)
         red(S("csel"), S("cq"), A.add)
         ts(S("E"), S("EM1"), S("csel"), A.mult)
         cp(S("csb"), S("csel"))
-        mm(S("b1", 0, 1), S("B4080"), S("csb"), True, True)
-        spread("b2", 0, 256, "E", cur, 0, True, True)
-        cp(S("kaps"), S("b1", 0, 1))
+        mm(B(1, 0, 1), S("B4080"), S("csb"), True, True)
+        cp(S("kaps"), B(1, 0, 1))
         ts(S("obig"), S("oh"), BIG, A.mult)
         ts(S("kap2"), S("kaps"), 2.0, A.mult)
         tt(S("base"), S("base"), S("obig"), A.add)
-        if t == 0:
-            consts_b()
-        ts(S("Fl", 0, 256), S("b2", 0, 256), S("kaps"), A.is_gt)
-        ts(S("Fl", 256, 512), S("b2", 0, 256), S("kaps"), A.is_lt)
-        for p in range(16):
-            mm(S("b3", 0, 32), S("EM1", 15 - p, 143 - p), S("Fl", p, 512, 16), p == 0, p == 15)
-        mm(S("b4"), S("Bones"), S("Fl"), True, True)
-        mm(S("b5"), S("Dm"), S("Fl"), True, True)
-        if t == 0:
-            consts_c()
-        cp(S("T2b"), S("b3", 0, 32))
-        mm(S("b6", 0, 32), S("Bones"), S("T2b"), True, True)
-        mm(S("b6", 32, 64), S("Dm"), S("T2b"), True, True)
-        scan(S("I3", 0, 256), S("b4", 0, 256), 256)
-        scan(S("I2", 0, 16), S("b6", 0, 16), 16)
-        scan(S("I2", 16, 32), S("b6", 16, 32), 16)
-        tt(S("bt", 0, 16), S("I2", 0, 16), S("mask16"), A.mult)
-        tt(S("bt", 16, 32), S("I2", 16, 32), S("mask16"), A.mult)
-        red(S("bnd", 0, 1), S("bt", 0, 16), A.add)
-        red(S("bnd", 4, 5), S("bt", 16, 32), A.add)
+    choose(0)
+
+    for t in range(3):
+        cur, nxt = ("BW0", "BW1") if t % 2 == 0 else ("BW1", "BW0")
+        X = S(cur, 0, XC)
+        for k in range(4):
+            spread(2, 64 * k, 64, "E", cur, 1024 * k, True, True)
+        ts(S("Fl", 0, 256), B(2, 0, 256), S("kaps"), A.is_gt)
+        ts(S("Fl", 256, 512), B(2, 0, 256), S("kaps"), A.is_lt)
+        spread(3, 0, 32, "EM1", "Fl", 0, True, True)
+        mm(B(4), S("Bones"), S("Fl"), True, True)
+        mm(B(5), S("Dm"), S("Fl"), True, True)
+        mm(B(6, 0, 256), S("Dn"), S("Fl", 0, 256), True, True)
+        cp(S("T2b"), B(3, 0, 32))
+        mm(B(3, 32, 64), S("Bones"), S("T2b"), True, True)
+        mm(B(3, 64, 96), S("Dm"), S("T2b"), True, True)
+        scan(S("I3", 0, 256), B(4, 0, 256), 256)
+        scan(S("I3", 256, 512), B(4, 256, 512), 256)
+        tt(S("uu"), S("I3", 0, 256), B(6, 0, 256), A.add)
+        for k, bnd in enumerate(("bn", "bp")):
+            o = (16 * k, 16 * k + 16)
+            scan(S("I2", *o), B(3, 32 + 16 * k, 48 + 16 * k), 16, -0.5)
+            tt(S("bt", *o), S("I2", *o), S("mask16"), A.mult)
+            red(S(bnd), S("bt", *o), A.add)
+            tt(S("W2", 24 * k, 24 * k + 16), S("I2", *o), B(3, 64 + 16 * k, 80 + 16 * k), A.add)
+        tt(S("W3", 0, 256), S("I3", 0, 256), B(5, 0, 256), A.add)
+        tt(S("W3", 264, 520), S("I3", 256, 512), B(5, 256, 512), A.add)
+        if t == 1:
+            for b in range(8):
+                mm(B(6 + b % 2), S("c4080"), S("nQ4"), True, False)
+                for k in range(4):
+                    values(6 + b % 2, 128 * k, cur, 4 * b + k, False, k == 3)
+                o = S("nzR", 512 * b, 512 * b + 512)
+                act(o, B(6 + b % 2), F.Sign)
+                act(o, o, F.Abs)
         J = S("JF", 173 * t, 173 * t + 256)
-        ts(S("c1n"), J, S("bnd", 0, 1), A.is_ge)
-        spread("b7", 0, 16, "EM1", "c1n", 0, True, True)
-        ts(S("c1p"), S("IF" if t == 0 else "IU"), S("bnd", 4, 5), A.is_ge)
-        spread("b1", 0, 64, "EM1", "c1p", 0, True, True)
-        tt(S("W2", 0, 16), S("I2", 0, 16), S("b6", 32, 48), A.add)
-        tt(S("W2", 24, 40), S("I2", 16, 32), S("b6", 48, 64), A.add)
-        cp(S("oAn"), S("b7", 0, 16))
-        act(S("lAn"), S("b7", 0, 16), F.Copy)
+        ts(S("c1n"), J, S("bn"), A.is_ge)
+        spread(0, 0, 16, "EM1", "c1n", 0, True, True)
+        act(S("c1p"), S("IF"), F.Sign, bias=S("bp"), scale=-1.0)
+        spread(1, 0, 64, "EMh", "c1p", 0, True, True)
+        cp(S("oAn"), B(0, 0, 16))
+        act(S("lAn"), B(0, 0, 16), F.Copy)
         tt(S("c2n"), IND(S("W2", 0, 24), S("oAn")), J, A.is_le)
-        mm(S("b0", 0, 16), S("I16"), S("lAn"), True, False)
-        spread("b0", 0, 16, "EM1", "c2n", 0, False, True)
-        tt(S("W3", 0, 256), S("I3", 0, 256), S("b5", 0, 256), A.add)
-        cp(S("oAp"), S("b1", 0, 64))
-        act(S("lAp"), S("b1", 0, 64), F.Copy)
-        qb, pbk = ("b6", "b2"), ("b7", "b1")
-
-        def find2(h):
-            o, k = (512 * h, 512 * h + 512), (32 * h, 32 * h + 32)
-            tt(S("c2p", *o), IND(S("W2", 24, 48), S("oAp", *k)), S("IF", *o), A.is_le)
-            mm(S(qb[h], 0, 32), S("I16"), S("lAp", *k), True, False)
-            spread(qb[h], 0, 32, "EM1", "c2p", 512 * h, False, True)
-
-        def find3(h):
-            o, k = (512 * h, 512 * h + 512), (32 * h, 32 * h + 32)
-            cp(S("oQp", *k), S(qb[h], 0, 32))
-            act(S("lQp", *k), S(qb[h], 0, 32), F.Copy)
-            tt(S("c3p", *o), IND(S("W3", 264, 528), S("oQp", *k)), S("IF", *o), A.is_le)
-            mm(S(pbk[h], 0, 32), S("I16"), S("lQp", *k), True, False)
-            spread(pbk[h], 0, 32, "EM1", "c3p", 512 * h, False, True)
-
-        def start(h):
-            k = (32 * h, 32 * h + 32)
-            cp(S("oPp", *k), S(pbk[h], 0, 32))
-            ts(S("A17", *k), S(pbk[h], 0, 32), 17.0, A.mult)
-            cp(S("AF", *k), S(pbk[h], 0, 32))
-            act(S("Pg", 512 * h, 512 * h + 512), IND(X, S("oPp", *k)), F.Copy)
-            for ww in range(4):
-                o = 128 * h + 32 * ww
-                tt(S("t32", o, o + 32), S("A17", *k), S("JT", 128 * t + 32 * ww, 128 * t + 32 * ww + 32), A.add)
-            o = (128 * h, 128 * h + 128)
-            ts(S("vi", *o), S("t32", *o), 4095, A.bitwise_and)
-            cp(S("off", *o), S("vi", *o))
-
-        def own_places(h):
-            for c in (2 * h, 2 * h + 1):
-                for k in range(2):
-                    mm(S("b%d" % c, 384 + 32 * k, 416 + 32 * k), S("identF"), S("AF", 32 * h, 32 * h + 32), True, True)
-        cp(S("oQn"), S("b0", 0, 16))
-        act(S("lQn"), S("b0", 0, 16), F.Copy)
+        mm(B(2, 0, 16), S("I16"), S("lAn"), True, False)
+        spread(2, 0, 16, "EM1", "c2n", 0, False, True)
+        ts(S("oAp"), B(1, 0, 64), 8.0, A.add)
+        act(S("lAp"), B(1, 0, 64), F.Identity, bias=8.0)
+        cp(S("oQn"), B(2, 0, 16))
+        act(S("lQn"), B(2, 0, 16), F.Copy)
         tt(S("c3n"), IND(S("W3", 0, 264), S("oQn")), J, A.is_le)
-        mm(S("b3", 0, 16), S("I16"), S("lQn"), True, False)
-        spread("b3", 0, 16, "EM1", "c3n", 0, False, True)
-        scan(S("I3", 256, 512), S("b4", 256, 512), 256)
-        find2(0)
-        tt(S("W3", 264, 520), S("I3", 256, 512), S("b5", 256, 512), A.add)
-        cp(S("oPn"), S("b3", 0, 16))
+        mm(B(0, 0, 16), S("I16"), S("lQn"), True, False)
+        spread(0, 0, 16, "EM1", "c3n", 0, False, True)
+        cp(S("oPn"), B(0, 0, 16))
         act(S("Hs"), IND(X, S("oPn")), F.Copy)
         send_guests(t)
-        find2(1)
-        find3(0)
-        find3(1)
-        if t == 0:
-            ts(S("JT"), S("JTm"), 5.0, A.mult)
-        start(0)
-        own_places(0)
-        start(1)
-        own_places(1)
-        if t == 0:
-            consts_f()
-            consts_e()
-
-        def gather_s(c):
-            act(S("G", 1024 * (c - 2), 1024 * (c - 2) + 1024), IND(X, S("off", 64 * c, 64 * c + 64)), F.Copy)
-
-        def equal(c):
-            h = (64 * c, 64 * c + 64)
-            ts(S("Tf5", *h), S("vi", *h), 5.0, A.mult, 1.0 if c < 2 else 1929.0, A.add)
-            tt(S("eq", *h), S("vi", *h), S("b%d" % c, 384, 448), A.is_equal)
-        gather_s(2)
-        gather_s(3)
-        guests_come(t)
-        cast_in(S("FW", FX, FE), T[cur][:, 0:4096], [S(cur, 0, XE), S("Hl")], "fx%d" % t)
-        ub = {0: 4, 1: 6, 2: 6, 3: 4}
-
-        def sums(c):
-            for k in range(2):
-                ww = 2 * (c % 2) + k
-                b = "b%d" % (ub[c] + k)
-                mm(S(b), S("ident"), S("Pg", 512 * (c // 2), 512 * (c // 2) + 512), True, False)
-                for o in (0, 256):
-                    mm(S(b, o, o + 256 - 64 * ww), S("ident"), S("Hl", 64 * ww, 256), False, o == 256 and ww == 0)
-                    if ww:
-                        mm(S(b, o + 256 - 64 * ww, o + 256), S("ident"), S("Hl", 0, 64 * ww), False, o == 256)
-
-        def children(c):
-            for k in range(2):
-                b = S("b%d" % (ub[c] + k))
-                o = S("Zp", 1024 * c + 512 * k, 1024 * c + 512 * k + 512)
-                if c == 3:
-                    act(o, b, F.Relu, bias=-4080.0)
-                else:
-                    ts(o, b, -4080.0, A.add, 0.0, A.max)
-
-        def diff(c, ks=(0, 1)):
-            for k in ks:
-                b = "b%d" % (2 * c + k)
-                o = 1024 * (c - 2) + 512 * k
-                mm(S(b), S("ident"), S("Zp", 1024 * c + 512 * k, 1024 * c + 512 * k + 512), True, False)
-                mm(S(b), S("nident"), S("G", o, o + 512), False, True)
-
-        def sign(c, ks=(0, 1)):
-            for k in ks:
-                o = 1024 * c + 512 * k
-                act(S("cmp", o, o + 512), S("b%d" % (2 * c + k)), F.Sign, bias=-0.5)
-
-        def compare(c):
-            tt(S("cmp", 1024 * c, 1024 * c + 1024), IND(X, S("off", 64 * c, 64 * c + 64)), S("Zp", 1024 * c, 1024 * c + 1024), A.is_lt)
-
-        def total(c, n):
-            b = "b%d" % c
-            mm(S(b, 64 * n, 64 * n + 64), S("I3856"), S("eq", 64 * c, 64 * c + 64), True, False)
-            spread(b, 64 * n, 64, "EM241" if c < 2 else "EM120", "cmp", 1024 * c, False, True)
-
-        def update(c, n):
-            h = (64 * c, 64 * c + 64)
-            tt(S("t32", *h), S("b%d" % c, 64 * n, 64 * n + 64), S("Tf5", *h), A.add)
-
-        def wrap(c):
-            h = (64 * c, 64 * c + 64)
-            ts(S("vi", *h), S("t32", *h), 4095, A.bitwise_and)
-
-        def offs(c):
-            h = (64 * c, 64 * c + 64)
-            cp(S("off", *h), S("vi", *h))
-
-        def passed_probes(c, n0, n1):
-            ts(S("NZ", 384 * c + 64 * n0, 384 * c + 64 * n1), S("b%d" % c, 64 * n0, 64 * n1), 0.0 if c < 2 else -1928.0, A.not_equal)
-
-        def sum_ok(hf):
+        cast_in(S("FW", FX, FE), S(cur, 0, XE), "fx%d" % t, [S("Hl")])
+        qb, pbk = (3, 1), (2, 3)
+        for h in range(2):
+            o, k = (512 * h, 512 * h + 512), (32 * h, 32 * h + 32)
+            tt(S("c2p", *o), IND(S("W2", 24, 48), S("oAp", *k)), S("IF", *o), A.is_le)
+            mm(B(qb[h], 0, 32), S("I16"), S("lAp", *k), True, False)
+            spread(qb[h], 0, 32, "EM1", "c2p", 512 * h, False, True)
+            cp(S("oQp", *k), B(qb[h], 0, 32))
+            act(S("lQp", *k), B(qb[h], 0, 32), F.Copy)
+        for h in range(2):
+            o, k = (512 * h, 512 * h + 512), (32 * h, 32 * h + 32)
+            tt(S("c3p", *o), IND(S("W3", 264, 528), S("oQp", *k)), S("IF", *o), A.is_le)
+            mm(B(pbk[h], 0, 32), S("I16"), S("lQp", *k), True, False)
+            spread(pbk[h], 0, 32, "EM1", "c3p", 512 * h, False, True)
+            cp(S("oPp", *k), B(pbk[h], 0, 32))
+            ts(S("A17", *k), B(pbk[h], 0, 32), 17.0, A.mult)
+            cp(S("AF", *k), B(pbk[h], 0, 32))
+            act(S("Pg", *o), IND(X, S("oPp", *k)), F.Copy)
             for ww in range(4):
-                o = 1536 + 128 * hf + 32 * ww
-                tt(S("NZ", o, o + 32), S("b1", 448 + 32 * hf, 480 + 32 * hf), S("shr", 4 * ww, 4 * ww + 32), A.is_le)
-
-        sums(0)
-        sums(2)
-        children(0)
-        for c in (0, 2, 1, 3):
-            equal(c)
-        sums(3)
-        children(2)
-        children(3)
-        sums(1)
-        diff(2)
-        compare(0)
-        children(1)
-        diff(3)
-        sign(2)
-        total(2, 0)
-        total(0, 0)
-        compare(1)
-        sign(3)
-        total(3, 0)
-        total(1, 0)
-        cast_in(S("Zf"), T.Zp[:, 2048:4096], [S("Zp", 2048, 4096)], "fz%d" % t)
-        do = {"a": update, "b": lambda c, n: wrap(c), "o": lambda c, n: offs(c), "e": lambda c, n: equal(c),
-              "g": lambda c, n: gather_s(c), "c": lambda c, n: compare(c), "t": lambda c, n: total(c, n + 1),
-              "x": lambda c, n: diff(c, (0,)), "y": lambda c, n: diff(c, (1,)),
-              "u": lambda c, n: sign(c, (0,)), "v": lambda c, n: sign(c, (1,))}
-        for n in range(5):
-            for k in LOOP.split():
-                if k == "s":
-                    if n == 0:
-                        spread("b1", 448, 64, "E", "Pg", 0, True, True)
-                        spread("b0", 448, 16, "E", "Hl", 0, True, True)
-                        for m in range(3):
-                            ts(S("shr", 16 * m, 16 * m + 16), S("b0", 448, 464), -1.0, A.mult, S("kap2"), A.add)
-                    elif n < 3:
-                        sum_ok(n - 1)
-                    else:
-                        for c in ((0, 2), (1, 3))[n - 3]:
-                            passed_probes(c, 0, n + 1)
-                elif (k, n) != ("t1", 4):
-                    do[k[0]](int(k[1]), n)
-
-        def tests(hf, early):
-            b = "b%d" % (4 + hf)
-            if early:
-                mm(S(b, 0, 128), S("ident"), S("NZ", 1536 + 128 * hf, 1664 + 128 * hf), True, False)
-            for n in (range(4) if early else (4, 5)):
+                c = 128 * h + 32 * ww
+                tt(S("t32", c, c + 32), S("A17", *k), S("JT", 128 * t + 32 * ww, 128 * t + 32 * ww + 32), A.add)
+            c = (128 * h, 128 * h + 128)
+            ts(S("vi", *c), S("t32", *c), 4095, A.bitwise_and)
+            cp(S("off", *c), S("vi", *c))
+        for h in range(2):
+            for c in (2 * h, 2 * h + 1):
                 for k in range(2):
-                    o = 384 * (2 * hf + k) + 64 * n
-                    mm(S(b, 64 * k, 64 * k + 64), S("ident"), S("NZ", o, o + 64), False, n == 5 and k == 1)
+                    mm(B(c, 64 + 32 * k, 96 + 32 * k), S("identF"), S("AF", 32 * h, 32 * h + 32), True, True)
 
-        def passed(hf):
-            ts(S("AL", 128 * hf, 128 * hf + 128), S("b%d" % (4 + hf), 0, 128), 7.0, A.is_equal)
+        def children(c, banks, engines):
+            for k in range(2):
+                ww, b = 2 * (c % 2) + k, banks[k]
+                mm(B(b), S("ident"), S("Pg", 512 * (c // 2), 512 * (c // 2) + 512), True, False)
+                for o in (0, 256):
+                    mm(B(b, o, o + 256 - 64 * ww), S("ident"), S("Hl", 64 * ww, 256), False, o == 256 and ww == 0)
+                    if ww:
+                        mm(B(b, o + 256 - 64 * ww, o + 256), S("ident"), S("Hl", 0, 64 * ww), False, o == 256)
+                o = S("Zp", 1024 * c + 512 * k, 1024 * c + 512 * k + 512)
+                if engines[k] == "S":
+                    act(o, B(b), F.Relu, bias=-4080.0)
+                else:
+                    ts(o, B(b), -4080.0, A.add, 0.0, A.max)
+        ch = OPT.get("ch", ("VS", "SS", "VS", "SS"))
+        children(0, (4, 5), ch[0])
+        children(1, (6, 7), ch[1])
+        children(2, (6, 7), ch[2])
+        children(3, (6, 7), ch[3])
+        z0 = 256 * OPT.get("s0", "VVSSSSSS").index("S")
+        cast_in(S("Zf", z0, 2048), S("Zp", z0, 2048), "fy%d" % t)
+        cast_in(S("Zf", 2304, 4096), S("Zp", 2304, 4096), "fz%d" % t)
 
-        def alive(hf):
-            bs, bx, a0 = "b%d" % (2 * hf), "b%d" % (2 * hf + 1), 128 * hf
+        def not_zero(bank, h, k0, k1):
+            for k in range(k0, k1):
+                values(bank, 128 + 128 * (k - k0), "Zp", 16 * h + k)
+            n = 128 * (k1 - k0)
+            tt(S("nzC", 2048 * h + 128 * k0, 2048 * h + 128 * k1), B(bank, 128, 128 + n), S("kapT", 0, n), A.not_equal)
+
+        def sum_ok(h):
+            spread(2 * h, 128, 32, "E", "Pg", 512 * h, True, True)
+            if h == 0:
+                spread(0, 160, 16, "E", "Hl", 0, True, True)
+                for m in range(3):
+                    ts(S("shr", 16 * m, 16 * m + 16), B(0, 160, 176), -1.0, A.mult, S("kap2"), A.add)
+            for ww in range(4):
+                o = 128 * h + 32 * ww
+                tt(S("AL", o, o + 32), B(2 * h, 128, 160), S("shr", 4 * ww, 4 * ww + 32), A.is_le)
+
+        def probe(c, n):
+            h, l, z = c // 2, (64 * c, 64 * c + 64), (1024 * c, 1024 * c + 1024)
+            tt(S("eq", *l), S("vi", *l), B(c, 64, 128), A.is_equal)
+            if n < 5:
+                ts(S("Tf5", *l), S("vi", *l), 5.0, A.mult, 1.0, A.add)
+            if t < 2 and c % 2 and n:
+                not_zero(c, h, 3 * n - 3, 3 * n)
+            if t < 2 and c % 2 == 0 and n == 3:
+                not_zero(c, h, 15, 16)
+            if c % 2 == 0:
+                tt(S("cmp", *z), IND(X, S("off", *l)), S("Zp", *z), A.is_lt)
+            else:
+                act(S("G", 1024 * h, 1024 * h + 1024), IND(X, S("off", *l)), F.Copy)
+                for k in range(2):
+                    b, o = 4 + 2 * h + k, 1024 * c + 512 * k
+                    mm(B(b), S("ident"), S("Zp", o, o + 512), True, False)
+                    mm(B(b), S("nident"), S("G", 1024 * h + 512 * k, 1024 * h + 512 * k + 512), False, True)
+                    act(S("cmp", o, o + 512), B(b), F.Sign, bias=-0.5)
+            mm(B(c, 0, 64), S("I3856"), S("eq", *l), True, False)
+            if c % 2:
+                mm(B(c, 0, 64), S("I1928"), S("onesB"), False, False)
+            spread(c, 0, 64, "EM120" if c % 2 else "EM241", "cmp", 1024 * c, False, True)
+            if n < 5:
+                tt(S("t32", *l), B(c, 0, 64), S("Tf5", *l), A.add)
+                ts(S("vi", *l), S("t32", *l), 4095, A.bitwise_and)
+                cp(S("off", *l), S("vi", *l))
+            if n == 0 and c % 2 == 0:
+                sum_ok(h)
+            tt(S("AL", *l), B(c, 0, 64), S("AL", *l), A.min)
+
+        def number(h):
+            bs, bx, a0 = 2 * h, 2 * h + 1, 128 * h
             al = [S("AL", a0 + 32 * ww, a0 + 32 * ww + 32) for ww in range(4)]
             for ww in range(4):
-                mm(S(bx, 0, 32), S("Bones"), al[ww], ww == 0, ww == 3)
+                mm(B(bx, 0, 32), S("Bones"), al[ww], ww == 0, ww == 3)
             for ww in range(4):
-                mm(S(bx, 32, 64), S("Ds"), al[ww], ww == 0, ww == 3)
+                mm(B(bx, 32, 64), S("Ds"), al[ww], ww == 0, ww == 3)
             for ww in range(4):
-                mm(S(bs, 32 * ww, 32 * ww + 32), S("I16384"), al[ww], True, ww == 0)
+                mm(B(bs, 32 * ww, 32 * ww + 32), S("I16384"), al[ww], True, ww == 0)
                 for w2 in range(ww):
-                    mm(S(bs, 32 * ww, 32 * ww + 32), S("ident"), al[w2], False, w2 == ww - 1)
-
-        def number(hf):
-            bs, bx, a0 = "b%d" % (2 * hf), "b%d" % (2 * hf + 1), 128 * hf
-            sc, pb = S("sc", 32 * hf, 32 * hf + 32), S("pb", 32 * hf, 32 * hf + 32)
-            scan(sc, S(bx, 0, 32), 32)
-            tt(pb, sc, S(bx, 32, 64), A.add)
+                    mm(B(bs, 32 * ww, 32 * ww + 32), S("ident"), al[w2], False, w2 == ww - 1)
+            sc, pb = S("sc", 32 * h, 32 * h + 32), S("pb", 32 * h, 32 * h + 32)
+            scan(sc, B(bx, 0, 32), 32)
+            tt(pb, sc, B(bx, 32, 64), A.add)
             for ww in range(4):
-                tt(S("of", a0 + 32 * ww, a0 + 32 * ww + 32), S(bs, 32 * ww, 32 * ww + 32), pb, A.add)
+                tt(S("of", a0 + 32 * ww, a0 + 32 * ww + 32), B(bs, 32 * ww, 32 * ww + 32), pb, A.add)
+            tt(S("mx", a0, a0 + 128), S("of", a0, a0 + 128), S("KT", a0, a0 + 128), A.max)
+            ts(S("so", a0, a0 + 128), S("mx", a0, a0 + 128), float((D1 if h else D0) - 16384), A.add)
 
-        def offsets(hf):
-            a0 = 128 * hf
-            tt(S("mx", a0, a0 + 128), S("of", a0, a0 + 128), S("KT"), A.max)
-            ts(S("so", a0, a0 + 128), S("mx", a0, a0 + 128), float(SV - 16384), A.add)
-        tests(1, True)
-        passed_probes(2, 4, 6)
-        passed_probes(3, 5, 6)
-        passed_probes(0, 4, 6)
-        tests(1, False)
-        total(1, 5)
-        passed(1)
-        alive(1)
-        passed_probes(1, 5, 6)
-        tests(0, True)
-        tests(0, False)
-        number(1)
-        passed(0)
-        alive(0)
-        offsets(1)
-        act(IND(S("FW", SS, FX), S("so", 128, 256)), S("Zf"), F.Silu)
-        number(0)
-        offsets(0)
-        tt(S("nS"), S("m05"), S("sc", 31, 32), A.subtract)
-        ts(S("dA"), S("sc", 31, 32), -0.5, A.mult, 2048.0, A.add)
-        tt(S("nT"), S("nS"), S("sc", 63, 64), A.subtract)
-        act(S("g1"), S("W3", 0, 256), F.Sign, bias=S("nS"))
-        act(S("g2"), S("W3", 0, 256), F.Sign, bias=S("nT"))
-        act(S("g1"), S("g1"), F.Identity, bias=S("dA"), scale=S("dA"))
-        mm(S("b4", 0, 256), S("identF"), S("W3", 0, 256), True, False)
-        mm(S("b4", 0, 256), S("N16384"), S("Fl", 0, 256), False, False)
-        mm(S("b4", 0, 256), S("I8192"), S("g2"), False, False)
-        mm(S("b4", 0, 256), S("identF"), S("g1"), False, True)
-        cp(IND(S("FW", 0, SS), S("so", 0, 128)), S("Zp", 0, 2048))
-        tt(S("fo"), S("b4", 0, 256), S("VT"), A.min)
-        ts(S("fo16"), S("fo"), 24575.0, A.add)
-
-        def place(b):
-            win = IND(S("FW", SV, FE), S("fo16", 32 * b, 32 * b + 32))
+        def landed(h, bank):
+            l = (128 * h, 128 * h + 128)
+            ts(S("lt", *l), S("of", *l), S("l%d" % h), A.is_lt)
+            mm(B(bank, 0, 128), S("lt", *l), S("ident"), True, False)
+            mm(B(bank, 0, 128), S("AL", *l), S("ident"), False, True)
+            act(S("wT", *l), B(bank, 0, 128), F.Identity, bias=-1.0)
+            weigh(8 * h, "nzC", h, 128 * h, True, True)
+        n0, n1a, n1 = S("sc", 31, 32), S("sc", 47, 48), S("sc", 63, 64)
+        u = S("W3", 0, 256)
+        for h in range(2):
+            for n in range(6):
+                probe(2 * h, n)
+                probe(2 * h + 1, n)
+            number(h)
+            if h == 0:
+                for k, e in enumerate(OPT.get("s0", "VVSSSSSS")):
+                    win = IND(S("FW", W0, WA), S("so", 16 * k, 16 * k + 16))
+                    if e == "V":
+                        cp(win, S("Zp", 256 * k, 256 * k + 256))
+                    else:
+                        act(win, S("Zf", 256 * k, 256 * k + 256), F.Silu, lead=OPT.get("lead", 0.0) if k == 7 else 0.0)
+                if t < 2:
+                    ts(S("l0"), S("I3", 255, 256), 16384.0, A.add)
+                    tt(S("l1"), S("l0"), n0, A.subtract)
+                    landed(0, 4)
+                ts(S("nm"), n0, -16384.0, A.add)
+                ts(S("dA"), n0, -1.0, A.mult, float(WA + D1 - D0), A.add)
+                ts(S("g1"), u, n0, A.is_gt, S("dA"), A.mult)
+                mm(B(4, 0, 256), S("identF"), S("uu"), True, False)
+                mm(B(4, 0, 256), S("identF"), S("g1"), False, False)
+        for ww in range(4):
+            o = 128 + 32 * ww
+            cp(IND(S("FW", WA, WB), S("so", o, o + 16)), S("Zp", 16 * o, 16 * o + 256))
+            act(IND(S("FW", WB, FX), S("so", o + 16, o + 32)), S("Zf", 16 * o + 256, 16 * o + 512), F.Silu)
+        ts(S("keep"), S("uu"), S("nm"), A.subtract, n1, A.is_gt)
+        ts(S("far"), u, n0, A.subtract, n1a, A.is_gt)
+        mm(B(4, 0, 256), S("I16384"), S("keep"), False, False)
+        mm(B(4, 0, 256), S("I1280"), S("far"), False, True)
+        tt(S("fo"), B(4, 0, 256), S("VT"), A.min)
+        ts(S("fo16"), S("fo"), 16383.0, A.add)
+        if t < 2:
+            landed(1, 6)
+            for h in range(2):
+                mm(B(7, 128 * h, 128 * h + 128), S("keep", 128 * h, 128 * h + 128), S("ident"), True, True)
+            act(S("wT", 256, 512), B(7, 0, 256), F.Copy)
+            for h in range(2):
+                weigh(16, "nzR", h, 256 + 128 * h, h == 0, h == 1)
+            tt(S("dg", 0, 24), B(5, 0, 24), S("mask24"), A.mult)
+            red(S("cown"), S("dg", 0, 24), A.add)
+            choose(t + 1)
+        for b in range(8):
+            win = IND(S("FW", D0, FE), S("fo16", 32 * b, 32 * b + 32))
             o = S(nxt, 512 * b, 512 * b + 512)
+            e = OPT.get("pl", "VSVSVSVS")[b]
             if t < 2:
-                if b % 2 == 0:
+                if e == "V":
                     cp(o, win)
                 else:
                     act(o, win, F.Copy)
-                return
-            if b % 2 == 0:
+                continue
+            if e == "V":
                 m = S("cmp", 512 * b, 512 * b + 512)
                 ts(m, win, -4079.986, A.add, 0.0, A.min)
                 ts(o, m, -0.0625, A.mult)
             else:
                 act(o, win, F.Relu, bias=254.9991, scale=-0.0625)
-            op("sync", lambda: g.sync.dma_start(T.y[:, 512 * b:512 * b + 512], AP(o)), [o], [], "ys%d" % b, 16)
-        for k in range(4):
-            place(2 * k)
-            place(2 * k + 1)
-            if t < 2:
-                values(t + 1, 2 * k)
-                values(t + 1, 2 * k + 1)
-                if k:
-                    nonzero(t + 1, 2 * k - 2)
-                    nonzero(t + 1, 2 * k - 1)
-                    diagonal(2 * k - 2)
-                    diagonal(2 * k - 1)
-        if t < 2:
-            nonzero(t + 1, 6)
-            nonzero(t + 1, 7)
-            diagonal(6)
-            diagonal(7)
+            op("sync", lambda o=o, b=b: g.sync.dma_start(T.y[:, 512 * b:512 * b + 512], AP(o)), [o], [], "ys%d" % b, 16, "dma")
     emit()

@@ -7,22 +7,22 @@ D0, D1 = 1024, 256
 W0, WA, WB, FX, FE = 0, 3072, 4352, 6656, 10752
 OWN = {
     "BW0": (XC, "bfloat16"), "BW1": (XC, "bfloat16"), "FW": (FE, "float32"), "Zp": (4096, "bfloat16"),
-    "Zf": (4096, "float32"), "Pg": (1024, "bfloat16"), "Hs": (256, "bfloat16"), "Hl": (256, "bfloat16"),
+    "Zf": (4096, "float32"), "PH": (1280, "bfloat16"), "Hs": (256, "bfloat16"),
     "cmp": (4096, "bfloat16"), "G": (2048, "bfloat16"), "nzR": (4096, "bfloat16"), "nzC": (4096, "bfloat16"),
-    "qi": (16, "int32"), "rown": (48, "float32"), "cl": (144, "float32"),
+    "qi": (16, "int32"), "rown": (96, "float32"), "cl": (288, "float32"),
 }
 POOL = {
     "bfloat16": {"c1n": 256, "c2n": 256, "c3n": 256, "c1p": 1024, "c2p": 1024, "c3p": 1024, "lAn": 16, "lQn": 16, "lAp": 64,
                  "lQp": 64, "Qblk": 128, "nQ4": 512, "Bones": 128, "ident": 128, "nident": 128, "I3856": 128, "I1928": 128,
                  "I16384": 128, "I1280": 128, "EM1": 144, "EMh": 144, "I16": 128, "EM241": 144, "EM120": 144, "E": 144,
-                 "Dm": 128, "Ds": 128, "Dn": 128, "dtmp": 128, "B4080": 128, "c4080": 128, "csb": 1, "Fl": 512, "T2b": 32,
-                 "eq": 256, "AL": 256, "lt": 256, "keep": 256, "far": 256, "wT": 512, "onesB": 64},
+                 "Dm": 128, "Ds": 128, "Dn": 128, "Lo": 128, "Up": 128, "dtmp": 128, "B4080": 128, "c4080": 128, "csb": 1, "Fl": 512, "T2b": 32,
+                 "eq": 256, "AL": 256, "lt": 256, "keep": 256, "far": 256, "wT": 512, "onesB": 64, "other": 8},
     "float32": {"dg": 128, "cown": 1, "qf": 16, "kapT": 512, "pif": 1, "p16f": 1, "pgf": 1, "e15": 1, "p37": 1, "BonesF": 128,
-                "identF": 128, "M16f": 16, "mask16": 16, "mask24": 24, "base": 16, "obig": 16, "JF": 602, "IF": 1024, "JT": 384,
-                "VT": 256, "KT": 256, "onesF": 256, "W2": 48, "W3": 528, "mn": 1, "oh": 16, "cq": 16, "csel": 1, "kaps": 1,
-                "kap2": 1, "I3": 512, "I2": 32, "bt": 32, "bn": 1, "bp": 1, "A17": 64, "AF": 64, "Tf5": 256, "shr": 48,
+                "identF": 128, "M16f": 32, "base": 32, "obig": 16, "mq": 1, "JF": 602, "IF": 1024, "JT": 384,
+                "VT": 256, "KT": 256, "onesF": 256, "W2": 48, "W3": 528, "mn": 1, "csel": 1, "kaps": 1,
+                "kap2": 1, "nn": 1, "bnd": 512, "KM": 256, "Kp": 1, "Kn": 1, "p17": 1, "A17": 64, "AF": 128, "Tf5": 256, "shr": 48,
                 "sc": 64, "pb": 64, "of": 256, "mx": 256, "uu": 256, "g1": 256, "fo": 256, "nm": 1, "dA": 1, "l0": 1, "l1": 1},
-    "int32": {"pi": 1, "p16i": 1, "pgi": 1, "ci": 144, "cg": 128, "c8": 24, "Ji": 602, "Jm": 602, "JTi": 384, "JTk": 384,
+    "int32": {"pi": 1, "p16i": 1, "pgi": 1, "ci": 144, "cg": 128, "Ji": 602, "Jm": 602, "JTi": 384, "JTk": 384,
               "JTm": 384, "VTi": 256, "t32": 256, "vi": 256},
     "uint16": {"oAn": 16, "oQn": 16, "oPn": 16, "oAp": 64, "oQp": 64, "oPp": 64, "off": 256, "so": 256, "fo16": 256},
 }
@@ -33,9 +33,10 @@ for _d, _names in POOL.items():
         PART[_n] = ("all_" + _d, _o, _c)
         _o += -(-_c // 16) * 16
     SB["all_" + _d] = (_o, _d)
+PART["Pg"], PART["Hl"] = ("PH", 0, 1024), ("PH", 1024, 256)
 for _t in range(3):
-    PART["rown%d" % _t] = ("rown", 16 * _t, 16)
-    PART["cl%d" % _t] = ("cl", 48 * _t, 48)
+    PART["rown%d" % _t] = ("rown", 32 * _t, 32)
+    PART["cl%d" % _t] = ("cl", 96 * _t, 96)
 SCRATCH = {n: ("sbuf", [128, -(-c // 16) * 16], d) for n, (c, d) in SB.items()}
 for _b in range(8):
     SCRATCH["b%d" % _b] = ("psum", [128, 512], "float32")
@@ -46,8 +47,14 @@ SEMAPHORES = (["sT", "sV", "sS", "sG", "qld"] + ["xl%d" % i for i in range(NX)] 
 XS = (1, 2, 3)
 BIG = 1048576.0
 CE = 4
-CY, PE, GATH, SCAT, LAT, DMA, FAR, RATE = 0.83, 0.42, 1.56, 3.8, 150.0, 1500.0, 2200.0, 200.0
-LOOK = 300.0
+CY, PE, LAT, SLAT, WAKE, DMA, FAR, RATE = 0.83, 0.42, 70.0, 245.0, 70.0, 1500.0, 2200.0, 200.0
+PACES = ((1.0, 1.56, 3.8), (1.25, 1.56, 3.8), (1.25, 1.3, 2.7), (1.25, 1.8, 4.9), (1.25, 1.9, 2.4), (1.25, 1.2, 5.2))
+LOOKS = (200.0, 300.0, 400.0)
+CHILD = ("VV VS VV VS",) * 3
+FIRST = ("SSS SSS VV",) * 3
+PLACE = ("VSVSVSVS",) * 3
+RAYS = "VSVSVSVS"
+MOVES = {"lAp": "S", "lQp": "S", "AF": "S", "Hs": "S", "w0": "V", "w1": "V", "wk": "V", "Pg0": "S", "Pg1": "S"}
 OPT = {}
 
 
@@ -67,30 +74,34 @@ def make_queue(g, T):
 
     def length(q, kind, reads, writes):
         if q is None:
-            return 0.0, 0.0
+            return (0.0, 0.0, 0.0, 0.0), 0.0
         o, i = (writes + reads)[0], (reads + writes)[0]
         if kind == "remote":
-            return 500.0, FAR + 128 * width(i) * size(i) / 50.0
+            return (500.0, 0.0, 0.0, 0.0), FAR + 128 * width(i) * size(i) / 50.0
+        if kind == "store":
+            return (128 * width(o) * size(o) / RATE, 0.0, 0.0, 0.0), DMA
         if kind == "dma":
-            return (600.0 if q == "g" else 60.0), DMA + 128 * width(o) * size(o) / RATE
+            return (600.0 if q == "g" else 60.0, 0.0, 0.0, 0.0), DMA + 128 * width(o) * size(o) / RATE
         if q == "tensor":
-            return sum(size(r) ** 2 / 4 * max(64, width(r)) * PE for r in reads[1::2]), LAT
+            return (0.0, sum(size(r) ** 2 / 4 * max(64, width(r)) * PE for r in reads[1::2]), 0.0, 0.0), LAT
         n = width(i)
         if o[0] == "IND" or i[0] == "IND":
-            return 55 + n * CY * (SCAT if o[0] == "IND" else GATH), LAT
+            return (0.0, 55.0, n * CY * (o[0] != "IND"), n * CY * (o[0] == "IND")), LAT
         if q == "g":
-            return 130 + 2 * n * CY, LAT
+            return (0.0, 130 + 2 * n * CY, 0.0, 0.0), LAT
         if kind == "tt" and reads[0][0] in SB and reads[1][0] in SB:
             n = 2 * n
         elif kind == "half" and size(o) == 2 and size(i) == 2:
             n = n / 2
-        return max(64, n) * CY, LAT
+        return (0.0, max(64, n) * CY, 0.0, 0.0), LAT
 
     def op(q, fn, reads, writes, sem=None, val=0, kind="", after=None, lead=0.0, late=0.0):
         me = len(ops)
         c, lat = length(q, kind, reads, writes)
+        if q == "scalar" and sem is None:
+            lat = SLAT
         rec = {"q": q, "fn": fn, "deps": set(), "ord": set(), "sem": sem, "val": val, "need": False, "m": [],
-               "remote": kind == "remote", "cost": c, "lat": lat + late, "lead": lead, "w": (writes + reads)[0][:3]}
+               "remote": kind == "remote", "len": c, "lat": lat + late, "w": (writes + reads)[0][:3]}
         rec["ord"].update(x for x in (after, held.get(q)) if x is not None)
         last[q] = me
         acc = []
@@ -124,12 +135,16 @@ def make_queue(g, T):
 
     def order():
         n = len(ops)
-        pre = [[(d, ops[d]["lat"]) for d in r["deps"]] + [(d, ops[d]["lat"] if ops[d]["remote"] else 0.0) for d in r["ord"] - r["deps"]]
-               for r in ops]
-        post = [[] for _ in ops]
-        for i in range(n):
-            for d, lat in pre[i]:
-                post[d].append((i, lat))
+        links = {}
+        for f in set(p[0] for p in PACES):
+            lag = [r["lat"] if r["sem"] else WAKE + f * r["lat"] for r in ops]
+            pre = [[(d, lag[d]) for d in r["deps"]] + [(d, lag[d] if ops[d]["remote"] else 0.0) for d in r["ord"] - r["deps"]]
+                   for r in ops]
+            post = [[] for _ in ops]
+            for i in range(n):
+                for d, lat in pre[i]:
+                    post[d].append((i, lat))
+            links[f] = (pre, post)
 
         def lay(seq, before):
             start, used = [0.0] * n, {q: [] for q in eng}
@@ -147,49 +162,82 @@ def make_queue(g, T):
                     u.insert(k, (t, t + r["cost"]))
                 start[i] = t
             return start
-        way = [0.0] * n
-        for i in reversed(range(n)):
-            way[i] += ops[i]["cost"] + ops[i]["lead"]
-            for d, lat in pre[i]:
-                way[d] = max(way[d], way[i] + lat)
-        left, ready, start = [len(p) for p in pre], [0.0] * n, [0.0] * n
-        free, can = {q: 0.0 for q in list(eng) + [None]}, {q: [] for q in list(eng) + [None]}
-        for i in range(n):
-            if not left[i]:
-                can[ops[i]["q"]].append(i)
-        for _ in range(n):
-            pick = None
-            for q, c in can.items():
-                if not c:
-                    continue
-                t = max(free[q], min(ready[i] for i in c))
-                now = [i for i in c if ready[i] <= t]
-                i = max(now, key=lambda k: way[k])
-                for j in c:
-                    if t < ready[j] < t + min(LOOK, ops[i]["cost"]) and way[j] > way[i]:
-                        i = max([k for k in now if t + ops[k]["cost"] <= ready[j]] or [j], key=lambda k: way[k])
-                        break
-                if pick is None or max(free[q], ready[i]) < pick[0]:
-                    pick = (max(free[q], ready[i]), q, i)
-            t, q, i = pick
-            can[q].remove(i)
-            start[i] = t
-            if q is not None:
-                free[q] = t + ops[i]["cost"]
-            for j, lat in post[i]:
-                ready[j] = max(ready[j], t + ops[i]["cost"] + lat)
-                left[j] -= 1
-                if not left[j]:
-                    can[ops[j]["q"]].append(j)
-        best = start
-        for _ in range(OPT.get("it", 2)):
-            back = lay(sorted(range(n), key=lambda k: (-start[k] - ops[k]["cost"], -k)), post)
-            start = lay(sorted(range(n), key=lambda k: (-back[k] - ops[k]["cost"], k)), pre)
-            if max(start) < max(best):
-                best = start
-        OPT["span"] = max(best)
-        OPT["dbg"] = (ops, pre, way, best)
-        return sorted(range(n), key=lambda k: (best[k], k))
+
+        def run(urge, before, behind, look):
+            left, ready, start = [len(p) for p in before], [0.0] * n, [0.0] * n
+            free, can = {q: 0.0 for q in list(eng) + [None]}, {q: [] for q in list(eng) + [None]}
+            for i in range(n):
+                if not left[i]:
+                    can[ops[i]["q"]].append(i)
+            for _ in range(n):
+                pick = None
+                for q, c in can.items():
+                    if not c:
+                        continue
+                    t = max(free[q], min(ready[i] for i in c))
+                    now = [i for i in c if ready[i] <= t]
+                    i = max(now, key=lambda k: urge[k])
+                    for j in c:
+                        if t < ready[j] < t + min(look, ops[i]["cost"]) and urge[j] > urge[i]:
+                            i = max([k for k in now if t + ops[k]["cost"] <= ready[j]] or [j], key=lambda k: urge[k])
+                            break
+                    if pick is None or max(free[q], ready[i]) < pick[0]:
+                        pick = (max(free[q], ready[i]), q, i)
+                t, q, i = pick
+                can[q].remove(i)
+                start[i] = t
+                if q is not None:
+                    free[q] = t + ops[i]["cost"]
+                for j, lat in behind[i]:
+                    ready[j] = max(ready[j], t + ops[i]["cost"] + lat)
+                    left[j] -= 1
+                    if not left[j]:
+                        can[ops[j]["q"]].append(j)
+            return start
+
+        def ends(start):
+            return [s + r["cost"] for s, r in zip(start, ops)]
+
+        def price(pace):
+            for r in ops:
+                r["cost"] = r["len"][0] + pace[0] * (r["len"][1] + pace[1] * r["len"][2] + pace[2] * r["len"][3])
+            return links[pace[0]]
+
+        def span(seq):
+            total = 0.0
+            for pace in PACES:
+                pre = price(pace)[0]
+                end, free = [0.0] * n, {}
+                for i in seq:
+                    q = ops[i]["q"]
+                    end[i] = max([end[d] + lat for d, lat in pre[i]] + [free.get(q, 0.0)]) + ops[i]["cost"]
+                    if q is not None:
+                        free[q] = end[i]
+                total += max(end) / pace[0]
+            return total
+        best = None
+        for pace in PACES[:OPT.get("np", 2)]:
+            for look in LOOKS:
+                pre, post = price(pace)
+                way = [0.0] * n
+                for i in reversed(range(n)):
+                    way[i] += ops[i]["cost"]
+                    for d, lat in pre[i]:
+                        way[d] = max(way[d], way[i] + lat)
+                start = run(way, pre, post, look)
+                for _ in range(OPT.get("it", 3)):
+                    price(pace)
+                    start = run(ends(run(ends(start), post, pre, look)), pre, post, look)
+                    e = ends(start)
+                    e = ends(lay(sorted(range(n), key=lambda k: (-e[k], -k)), post))
+                    tight = lay(sorted(range(n), key=lambda k: (-e[k], k)), pre)
+                    seq = sorted(range(n), key=lambda k: (tight[k], k))
+                    mark = span(seq)
+                    if best is None or mark < best[0]:
+                        best = (mark, seq, tight)
+        OPT["span"] = best[0] / len(PACES)
+        OPT["dbg"] = (ops, price(PACES[0])[0], way, best[2])
+        return best[1]
 
     def emit():
         for r in ops:
@@ -197,7 +245,9 @@ def make_queue(g, T):
                 ops[d]["need"] = True
         cnt = {q: 0 for q in QSEM}
         know = {q: {} for q in eng}
-        for r in [ops[i] for i in order()]:
+        if "order" not in OPT:
+            OPT["order"] = order()
+        for r in [ops[i] for i in OPT["order"]]:
             q = r["q"]
             if q is None:
                 r["clock"] = {r["sem"]: r["val"], "own": r["sem"]}
@@ -240,14 +290,17 @@ def make_queue(g, T):
             if r["sem"] is not None and r["sem"][:2] in ("ys", "lc", "lg"):
                 g.wait_ge(T.sem[r["sem"]], r["val"])
 
-    return op, hold, emit
+    def urgent(name):
+        return name
+
+    return op, hold, urgent, emit
 
 
 def rank_program(g, core, T, topo):
     rank = T.rank_of(core)
     if rank is None:
         return
-    op, hold, emit = make_queue(g, T)
+    op, hold, urgent, emit = make_queue(g, T)
 
     def S(n, a=0, b=None, st=1):
         n, o, w = PART.get(n, (n, 0, SB[n][0] if n in SB else 512))
@@ -284,8 +337,8 @@ def rank_program(g, core, T, topo):
     def red(out, a, o):
         op("vector", lambda: g.vector.tensor_reduce(AP(out), AP(a), AxisListType.X, o), [a], [out])
 
-    def scan(out, a, n, first=0.0):
-        one = S("onesF", 0, n)
+    def scan(out, a, n, first=0.0, by="onesF"):
+        one = S(by, 0, n)
         op("vector", lambda: g.vector.tensor_tensor_scan(AP(out), AP(one), AP(a), first, A.mult, A.add), [one, a], [out])
 
     def fill(out, c):
@@ -299,6 +352,14 @@ def rank_program(g, core, T, topo):
             ub, us = bias if num(bias) else AP(bias), scale if num(scale) else AP(scale)
             op("scalar", lambda: g.scalar.activation(AP(out), AP(a), f, bias=ub, scale=us), [a] + cols, [out])
 
+    def move(name, out, in_, add=0.0):
+        if OPT.get("mv", MOVES)[name] == "S":
+            act(out, in_, F.Identity if add else F.Copy, bias=add)
+        elif add:
+            ts(out, in_, add, A.add)
+        else:
+            cp(out, in_)
+
     def mm(out, l, r, start, stop):
         mms([(out, l, r, start, stop)])
 
@@ -309,6 +370,10 @@ def rank_program(g, core, T, topo):
     def spread(bank, c0, n, emat, src, s0, start, stop):
         mms([(B(bank, c0, c0 + n), S(emat, 15 - p, 143 - p), S(src, s0 + p, s0 + 16 * n, 16), start and p == 0, stop and p == 15)
              for p in range(16)])
+
+    def steps(bank, c0, n, src, s0):
+        mms([(B(bank, c0, c0 + n), S("Lo"), S(src, s0, s0 + n), True, False),
+             (B(bank, c0 + 1, c0 + n), S("Up"), S(src, s0, s0 + n - 1), False, True)])
 
     def iota(out, pattern, base=0, cm=0, fl=False):
         if fl:
@@ -344,10 +409,12 @@ def rank_program(g, core, T, topo):
     ts(S("identF"), S("ci", 0, 128), S("pif"), A.is_equal)
     for k in range(8):
         ts(S("Qblk", 16 * k, 16 * k + 16), S("qi"), S("BonesF", 16 * k, 16 * k + 1), A.mult)
-    ts(S("M16f"), S("ci", 0, 16), S("p16f"), A.is_equal, 16.0, A.mult)
-    cp(S("base"), S("ci", 0, 16))
+    for k in (0, 16):
+        ts(S("M16f", k, k + 16), S("ci", 0, 16), S("p16f"), A.is_equal, 16.0, A.mult)
+    cp(S("base", 0, 16), S("ci", 0, 16))
     ts(S("e15"), S("pif"), S("p16f"), A.subtract, 15.0, A.add)
-    cp(S("qf"), S("qi"))
+    ts(S("qf"), S("qi"), 0.125, A.mult)
+    tt(S("base", 16, 32), S("base", 0, 16), S("qf"), A.add)
     ts(S("dtmp"), S("ci", 0, 128), S("pif"), A.is_lt, -1.0, A.mult)
     ts(S("EM1"), S("ci"), S("e15"), A.is_equal)
     act(S("Bones"), S("BonesF"), F.Copy)
@@ -359,9 +426,14 @@ def rank_program(g, core, T, topo):
                  ("I1280", float(WB - WA))):
         act(S(n), S("identF"), F.Copy, scale=s)
     tt(S("Ds"), S("Dm"), S("identF"), A.subtract)
-    tt(S("Dn"), S("Dm"), S("I16384"), A.subtract)
+    tt(S("Lo"), S("Dm"), S("BonesF"), A.add)
+    act(S("Up"), S("Dm"), F.Copy, scale=-1.0)
+    act(S("Dn"), S("identF"), F.Copy, scale=-16384.0)
     fill(S("BW0", XE, XC), 0.0)
-    ts(S("mask16"), S("M16f"), 0.0625, A.mult)
+    ts(S("Kp"), S("p16f"), 15.0, A.is_lt, 4095.0, A.mult)
+    ts(S("Kp"), S("Kp"), 1.0, A.add)
+    ts(S("Kn"), S("Kp"), -1.0, A.mult)
+    ts(S("p17"), S("p16f"), 16.0, A.mult, 16.0, A.add)
     fill(S("onesF"), 1.0)
     fill(S("onesB"), 1.0)
     for a, b in ((16, 24), (40, 48)):
@@ -373,9 +445,8 @@ def rank_program(g, core, T, topo):
 
     def constants():
         iota(S("JTi"), [[1, 3], [64, 4], [592, 32]])
-        iota(S("c8"), [[0, 3], [1, 8]])
         iota(S("VTi"), [[16, 256]], FX - D0 - 16383)
-        iota(S("KT", 0, 128), [[0, 2], [16, 64]], 16384 - D0, 0, True)
+        iota(S("KT", 0, 128), [[0, 2048 // D0], [16, D0 // 16]], 16384 - D0, 0, True)
         iota(S("KT", 128, 256), [[0, 8], [16, 16]], 16384 - D1, 0, True)
         for b in range(8):
             o, i = S("BW0", 512 * b, 512 * b + 512), S("BW1", 512 * b, 512 * b + 512)
@@ -384,7 +455,10 @@ def rank_program(g, core, T, topo):
             else:
                 ts(o, i, -16.0, A.mult, 4080.0, A.add)
         fill(S("BW1", XE, XC), 0.0)
-        ts(S("mask24"), S("c8"), S("pgf"), A.is_equal)
+        ts(S("KM"), S("IF", 0, 256), S("p17"), A.is_equal, 4095.0, A.mult)
+        ts(S("KM"), S("KM"), 1.0, A.add)
+        act(S("IF"), S("IF"), F.Identity, bias=1.0 - 2.0 ** -13)
+        ts(S("other"), S("ci", 0, 8), S("pgf"), A.not_equal, -65536.0, A.mult)
         for a in range(D0, FX, 512):
             act(S("FW", a, a + 512), S("BW1", 0, 512), F.Silu)
         ts(S("Jm"), S("Ji"), 255, A.bitwise_and)
@@ -416,7 +490,7 @@ def rank_program(g, core, T, topo):
                 rid, pid, _s = topo.addr(T.cores[r])
                 c = [k for k in range(len(T.cores)) if k != r].index(rank)
                 tr.append(RemoteDMATransfer(dst_ids=[DstId(rid=rid, pnc=pid)], dma_engine_mask=m, remote_sem=T.sem["cs%d" % t],
-                                            src=AP(S("rown%d" % t)), dst=AP(S("cl%d" % t, 16 * c, 16 * c + 16))))
+                                            src=AP(S("rown%d" % t)), dst=AP(S("cl%d" % t, 32 * c, 32 * c + 32))))
             return g.remote_dma_fused(tr, local_sem=T.sem["lc%d" % t])
         i = op("g", f, [S("rown%d" % t)], [], "lc%d" % t, CE * len(peers), "remote", late=0.0 if t else 2000.0)
         op(None, None, [], [S("cl%d" % t)], "cs%d" % t, CE * len(peers), after=i)
@@ -427,7 +501,7 @@ def rank_program(g, core, T, topo):
 
         def f():
             rid, pid, _s = topo.addr(dst)
-            return g.remote_dma(T.Hl[:, 0:256], T.Hs[:, 0:256], T.sem["gs%d" % t], T.sem["lg%d" % t], pid, rid, sum(1 << e for e in es))
+            return g.remote_dma(AP(S("Hl")), AP(S("Hs")), T.sem["gs%d" % t], T.sem["lg%d" % t], pid, rid, sum(1 << e for e in es))
         i = op("g", f, [S("Hs")], [], "lg%d" % t, len(es), "remote")
         op(None, None, [], [S("Hl")], "gs%d" % t, len(topo.engines(dst, core)[:8]), after=i)
 
@@ -435,10 +509,10 @@ def rank_program(g, core, T, topo):
         o = 2048 * (k // 16)
         mm(B(bank, c0, c0 + 128), S(xs, o + k % 16, o + 2048, 16), S("Qblk"), start, stop)
 
-    def weigh(c0, nz, h, w0, start, stop):
+    def weigh(nz, h, w0, stop):
         for k in range(0, 16, 8):
-            mms([(B(5, c0, c0 + 8), S(nz, 2048 * h + 128 * p, 2048 * h + 128 * p + 128), S("wT", w0 + p, w0 + 128, 16),
-                  start and p == 0, stop and p == 15) for p in range(k, k + 8)])
+            mms([(B(5, 0, 8), S(nz, 2048 * h + 128 * p, 2048 * h + 128 * p + 128), S("wT", w0 + p, w0 + 128, 16),
+                  False, stop and p == 15) for p in range(k, k + 8)])
 
     for b in range(8):
         for k in range(4):
@@ -457,109 +531,117 @@ def rank_program(g, core, T, topo):
     def choose(t):
         rown = S("rown%d" % t)
         ts(rown, S("M16f"), S("cown"), A.mult)
+        urgent("counts")
         send_counts(t)
         if t == 0:
             hold(True)
             constants()
             hold(False)
-        mm(B(0, 0, 16), S("identF"), S("base"), True, False)
-        mm(B(0, 0, 16), S("BonesF"), rown, False, False)
+        mm(B(0, 0, 32), S("identF"), S("base"), True, False)
+        mm(B(0, 0, 32), S("BonesF"), rown, False, False)
         for k in range(3):
-            mm(B(0, 0, 16), S("BonesF"), S("cl%d" % t, 16 * k, 16 * k + 16), False, k == 2)
+            mm(B(0, 0, 32), S("BonesF"), S("cl%d" % t, 32 * k, 32 * k + 32), False, k == 2)
         red(S("mn"), B(0, 0, 16), A.min)
-        ts(S("oh"), B(0, 0, 16), S("mn"), A.is_equal)
-        tt(S("cq"), S("oh"), S("qf"), A.mult)
-        red(S("csel"), S("cq"), A.add)
+        red(S("mq"), B(0, 16, 32), A.min)
+        ts(S("csel"), S("mq"), S("mn"), A.subtract, 8.0, A.mult)
         ts(S("E"), S("EM1"), S("csel"), A.mult)
+        urgent("E")
         cp(S("csb"), S("csel"))
         mm(B(1, 0, 1), S("B4080"), S("csb"), True, True)
         cp(S("kaps"), B(1, 0, 1))
-        ts(S("obig"), S("oh"), BIG, A.mult)
+        urgent("kaps")
         ts(S("kap2"), S("kaps"), 2.0, A.mult)
-        tt(S("base"), S("base"), S("obig"), A.add)
+        if t < 2:
+            ts(S("obig"), B(0, 0, 16), S("mn"), A.is_equal, BIG, A.mult)
+            for k in (0, 16):
+                tt(S("base", k, k + 16), S("base", k, k + 16), S("obig"), A.add)
     choose(0)
 
     for t in range(3):
         cur, nxt = ("BW0", "BW1") if t % 2 == 0 else ("BW1", "BW0")
         X = S(cur, 0, XC)
-        for k in range(4):
-            spread(2, 64 * k, 64, "E", cur, 1024 * k, True, True)
+        for a, b in OPT.get("sp", ((0, 256),) if t == 0 else ((0, 128), (128, 192), (192, 256))):
+            spread(2, a, b - a, "E", cur, 16 * a, True, True)
         ts(S("Fl", 0, 256), B(2, 0, 256), S("kaps"), A.is_gt)
         ts(S("Fl", 256, 512), B(2, 0, 256), S("kaps"), A.is_lt)
+        mm(B(4, 0, 256), S("Bones"), S("Fl", 0, 256), True, True)
+        mm(B(1, 0, 256), S("Bones"), S("Fl", 256, 512), True, True)
         spread(3, 0, 32, "EM1", "Fl", 0, True, True)
-        mm(B(4), S("Bones"), S("Fl"), True, True)
-        mm(B(5), S("Dm"), S("Fl"), True, True)
-        mm(B(6, 0, 256), S("Dn"), S("Fl", 0, 256), True, True)
         cp(S("T2b"), B(3, 0, 32))
-        mm(B(3, 32, 64), S("Bones"), S("T2b"), True, True)
-        mm(B(3, 64, 96), S("Dm"), S("T2b"), True, True)
-        scan(S("I3", 0, 256), B(4, 0, 256), 256)
-        scan(S("I3", 256, 512), B(4, 256, 512), 256)
-        tt(S("uu"), S("I3", 0, 256), B(6, 0, 256), A.add)
-        for k, bnd in enumerate(("bn", "bp")):
-            o = (16 * k, 16 * k + 16)
-            scan(S("I2", *o), B(3, 32 + 16 * k, 48 + 16 * k), 16, -0.5)
-            tt(S("bt", *o), S("I2", *o), S("mask16"), A.mult)
-            red(S(bnd), S("bt", *o), A.add)
-            tt(S("W2", 24 * k, 24 * k + 16), S("I2", *o), B(3, 64 + 16 * k, 80 + 16 * k), A.add)
-        tt(S("W3", 0, 256), S("I3", 0, 256), B(5, 0, 256), A.add)
-        tt(S("W3", 264, 520), S("I3", 256, 512), B(5, 256, 512), A.add)
+        for k in range(2):
+            steps(3, 32 + 16 * k, 16, "T2b", 16 * k)
+        mm(B(3, 64, 80), S("Bones"), S("T2b", 0, 16), True, True)
+        for k, bank in enumerate((4, 1)):
+            scan(S("bnd", 256 * k, 256 * k + 256), B(bank, 0, 256), 256, k - 1.0, "KM")
+            scan(S("W2", 24 * k, 24 * k + 16), B(3, 32 + 16 * k, 48 + 16 * k), 16)
+            steps(5, 256 * k, 256, "Fl", 256 * k)
+            scan(S("W3", 264 * k, 264 * k + 256), B(5, 256 * k, 256 * k + 256), 256)
+        red(S("nn"), B(3, 64, 80), A.add)
         if t == 1:
             for b in range(8):
-                mm(B(6 + b % 2), S("c4080"), S("nQ4"), True, False)
+                e, o = OPT.get("nzr", RAYS)[b], S("nzR", 512 * b, 512 * b + 512)
+                if e != "V":
+                    mm(B(6 + b % 2), S("c4080"), S("nQ4"), True, False)
                 for k in range(4):
-                    values(6 + b % 2, 128 * k, cur, 4 * b + k, False, k == 3)
-                o = S("nzR", 512 * b, 512 * b + 512)
+                    values(6 + b % 2, 128 * k, cur, 4 * b + k, e == "V", e == "V" or k == 3)
+                if e == "V":
+                    tt(o, B(6 + b % 2), S("kapT"), A.not_equal)
+                    continue
                 act(o, B(6 + b % 2), F.Sign)
-                act(o, o, F.Abs)
+                if e == "S":
+                    act(o, o, F.Abs)
+                else:
+                    ts(o, o, 0.0, A.not_equal)
         J = S("JF", 173 * t, 173 * t + 256)
-        ts(S("c1n"), J, S("bn"), A.is_ge)
+        ts(S("c1n"), J, S("Kp"), A.mult, S("bnd", 255, 256), A.is_gt)
         spread(0, 0, 16, "EM1", "c1n", 0, True, True)
-        act(S("c1p"), S("IF"), F.Sign, bias=S("bp"), scale=-1.0)
+        act(S("c1p"), S("IF"), F.Sign, bias=S("bnd", 511, 512), scale=S("Kn"))
         spread(1, 0, 64, "EMh", "c1p", 0, True, True)
         cp(S("oAn"), B(0, 0, 16))
-        act(S("lAn"), B(0, 0, 16), F.Copy)
+        cp(S("lAn"), B(0, 0, 16))
         tt(S("c2n"), IND(S("W2", 0, 24), S("oAn")), J, A.is_le)
         mm(B(2, 0, 16), S("I16"), S("lAn"), True, False)
         spread(2, 0, 16, "EM1", "c2n", 0, False, True)
         ts(S("oAp"), B(1, 0, 64), 8.0, A.add)
-        act(S("lAp"), B(1, 0, 64), F.Identity, bias=8.0)
+        move("lAp", S("lAp"), B(1, 0, 64), 8.0)
         cp(S("oQn"), B(2, 0, 16))
-        act(S("lQn"), B(2, 0, 16), F.Copy)
+        cp(S("lQn"), B(2, 0, 16))
         tt(S("c3n"), IND(S("W3", 0, 264), S("oQn")), J, A.is_le)
         mm(B(0, 0, 16), S("I16"), S("lQn"), True, False)
         spread(0, 0, 16, "EM1", "c3n", 0, False, True)
         cp(S("oPn"), B(0, 0, 16))
-        act(S("Hs"), IND(X, S("oPn")), F.Copy)
+        move("Hs", S("Hs"), IND(X, S("oPn")))
+        urgent("guests")
         send_guests(t)
+        mm(B(4, 256, 512), S("Dn"), S("Fl", 0, 256), True, True)
+        tt(S("uu"), S("W3", 0, 256), B(4, 256, 512), A.add)
         cast_in(S("FW", FX, FE), S(cur, 0, XE), "fx%d" % t, [S("Hl")])
         qb, pbk = (3, 1), (2, 3)
         for h in range(2):
             o, k = (512 * h, 512 * h + 512), (32 * h, 32 * h + 32)
-            tt(S("c2p", *o), IND(S("W2", 24, 48), S("oAp", *k)), S("IF", *o), A.is_le)
+            tt(S("c2p", *o), IND(S("W2", 24, 48), S("oAp", *k)), S("IF", *o), A.is_lt)
             mm(B(qb[h], 0, 32), S("I16"), S("lAp", *k), True, False)
             spread(qb[h], 0, 32, "EM1", "c2p", 512 * h, False, True)
             cp(S("oQp", *k), B(qb[h], 0, 32))
-            act(S("lQp", *k), B(qb[h], 0, 32), F.Copy)
+            move("lQp", S("lQp", *k), B(qb[h], 0, 32))
         for h in range(2):
             o, k = (512 * h, 512 * h + 512), (32 * h, 32 * h + 32)
-            tt(S("c3p", *o), IND(S("W3", 264, 528), S("oQp", *k)), S("IF", *o), A.is_le)
+            tt(S("c3p", *o), IND(S("W3", 264, 528), S("oQp", *k)), S("IF", *o), A.is_lt)
             mm(B(pbk[h], 0, 32), S("I16"), S("lQp", *k), True, False)
             spread(pbk[h], 0, 32, "EM1", "c3p", 512 * h, False, True)
             cp(S("oPp", *k), B(pbk[h], 0, 32))
             ts(S("A17", *k), B(pbk[h], 0, 32), 17.0, A.mult)
-            cp(S("AF", *k), B(pbk[h], 0, 32))
-            act(S("Pg", *o), IND(X, S("oPp", *k)), F.Copy)
+            for c in (64 * h, 64 * h + 32):
+                move("AF", S("AF", c, c + 32), B(pbk[h], 0, 32))
+            move("Pg%d" % h, S("Pg", *o), IND(X, S("oPp", *k)))
             for ww in range(4):
                 c = 128 * h + 32 * ww
                 tt(S("t32", c, c + 32), S("A17", *k), S("JT", 128 * t + 32 * ww, 128 * t + 32 * ww + 32), A.add)
             c = (128 * h, 128 * h + 128)
             ts(S("vi", *c), S("t32", *c), 4095, A.bitwise_and)
             cp(S("off", *c), S("vi", *c))
-        for h in range(2):
-            for c in (2 * h, 2 * h + 1):
-                for k in range(2):
-                    mm(B(c, 64 + 32 * k, 96 + 32 * k), S("identF"), S("AF", 32 * h, 32 * h + 32), True, True)
+        for c in range(4):
+            mm(B(c, 64, 128), S("identF"), S("AF", 64 * (c // 2), 64 * (c // 2) + 64), True, True)
 
         def children(c, banks, engines):
             for k in range(2):
@@ -574,13 +656,14 @@ def rank_program(g, core, T, topo):
                     act(o, B(b), F.Relu, bias=-4080.0)
                 else:
                     ts(o, B(b), -4080.0, A.add, 0.0, A.max)
-        ch = OPT.get("ch", ("VS", "SS", "VS", "SS"))
+        ch = OPT.get("ch", CHILD)[t].split()
         children(0, (4, 5), ch[0])
         children(1, (6, 7), ch[1])
         children(2, (6, 7), ch[2])
         children(3, (6, 7), ch[3])
-        z0 = 256 * OPT.get("s0", "VVSSSSSS").index("S")
-        cast_in(S("Zf", z0, 2048), S("Zp", z0, 2048), "fy%d" % t)
+        s0 = OPT.get("s0", FIRST)[t].replace(" ", "")
+        z0, z1 = 256 * s0.index("S"), 256 * s0.rindex("S") + 256
+        cast_in(S("Zf", z0, z1), S("Zp", z0, z1), "fy%d" % t)
         cast_in(S("Zf", 2304, 4096), S("Zp", 2304, 4096), "fz%d" % t)
 
         def not_zero(bank, h, k0, k1):
@@ -589,15 +672,12 @@ def rank_program(g, core, T, topo):
             n = 128 * (k1 - k0)
             tt(S("nzC", 2048 * h + 128 * k0, 2048 * h + 128 * k1), B(bank, 128, 128 + n), S("kapT", 0, n), A.not_equal)
 
-        def sum_ok(h):
-            spread(2 * h, 128, 32, "E", "Pg", 512 * h, True, True)
-            if h == 0:
-                spread(0, 160, 16, "E", "Hl", 0, True, True)
-                for m in range(3):
-                    ts(S("shr", 16 * m, 16 * m + 16), B(0, 160, 176), -1.0, A.mult, S("kap2"), A.add)
-            for ww in range(4):
-                o = 128 * h + 32 * ww
-                tt(S("AL", o, o + 32), B(2 * h, 128, 160), S("shr", 4 * ww, 4 * ww + 32), A.is_le)
+        def sum_ok():
+            spread(0, 128, 80, "E", "PH", 0, True, True)
+            for m in range(3):
+                ts(S("shr", 16 * m, 16 * m + 16), B(0, 192, 208), -1.0, A.mult, S("kap2"), A.add)
+            for o in range(0, 256, 32):
+                tt(S("AL", o, o + 32), B(0, 128 + o // 128 * 32, 160 + o // 128 * 32), S("shr", o % 128 // 8, o % 128 // 8 + 32), A.is_le)
 
         def probe(c, n):
             h, l, z = c // 2, (64 * c, 64 * c + 64), (1024 * c, 1024 * c + 1024)
@@ -625,8 +705,8 @@ def rank_program(g, core, T, topo):
                 tt(S("t32", *l), B(c, 0, 64), S("Tf5", *l), A.add)
                 ts(S("vi", *l), S("t32", *l), 4095, A.bitwise_and)
                 cp(S("off", *l), S("vi", *l))
-            if n == 0 and c % 2 == 0:
-                sum_ok(h)
+            if n == 0 and c == 0:
+                sum_ok()
             tt(S("AL", *l), B(c, 0, 64), S("AL", *l), A.min)
 
         def number(h):
@@ -636,10 +716,9 @@ def rank_program(g, core, T, topo):
                 mm(B(bx, 0, 32), S("Bones"), al[ww], ww == 0, ww == 3)
             for ww in range(4):
                 mm(B(bx, 32, 64), S("Ds"), al[ww], ww == 0, ww == 3)
-            for ww in range(4):
-                mm(B(bs, 32 * ww, 32 * ww + 32), S("I16384"), al[ww], True, ww == 0)
-                for w2 in range(ww):
-                    mm(B(bs, 32 * ww, 32 * ww + 32), S("ident"), al[w2], False, w2 == ww - 1)
+            mm(B(bs, 0, 128), S("I16384"), S("AL", a0, a0 + 128), True, False)
+            for ww in range(1, 4):
+                mm(B(bs, 32 * ww, 128), S("ident"), S("AL", a0, a0 + 128 - 32 * ww), False, ww == 3)
             sc, pb = S("sc", 32 * h, 32 * h + 32), S("pb", 32 * h, 32 * h + 32)
             scan(sc, B(bx, 0, 32), 32)
             tt(pb, sc, B(bx, 32, 64), A.add)
@@ -653,8 +732,10 @@ def rank_program(g, core, T, topo):
             ts(S("lt", *l), S("of", *l), S("l%d" % h), A.is_lt)
             mm(B(bank, 0, 128), S("lt", *l), S("ident"), True, False)
             mm(B(bank, 0, 128), S("AL", *l), S("ident"), False, True)
-            act(S("wT", *l), B(bank, 0, 128), F.Identity, bias=-1.0)
-            weigh(8 * h, "nzC", h, 128 * h, True, True)
+            move("w%d" % h, S("wT", *l), B(bank, 0, 128), -1.0)
+            if h == 0:
+                mm(B(5, 0, 8), S("ident"), S("other"), True, False)
+            weigh("nzC", h, 128 * h, False)
         n0, n1a, n1 = S("sc", 31, 32), S("sc", 47, 48), S("sc", 63, 64)
         u = S("W3", 0, 256)
         for h in range(2):
@@ -663,14 +744,16 @@ def rank_program(g, core, T, topo):
                 probe(2 * h + 1, n)
             number(h)
             if h == 0:
-                for k, e in enumerate(OPT.get("s0", "VVSSSSSS")):
-                    win = IND(S("FW", W0, WA), S("so", 16 * k, 16 * k + 16))
-                    if e == "V":
-                        cp(win, S("Zp", 256 * k, 256 * k + 256))
+                k = 0
+                for e in OPT.get("s0", FIRST)[t].split():
+                    win = IND(S("FW", W0, WA), S("so", 16 * k, 16 * (k + len(e))))
+                    if e[0] == "V":
+                        cp(win, S("Zp", 256 * k, 256 * (k + len(e))))
                     else:
-                        act(win, S("Zf", 256 * k, 256 * k + 256), F.Silu, lead=OPT.get("lead", 0.0) if k == 7 else 0.0)
+                        act(win, S("Zf", 256 * k, 256 * (k + len(e))), F.Silu)
+                    k += len(e)
                 if t < 2:
-                    ts(S("l0"), S("I3", 255, 256), 16384.0, A.add)
+                    ts(S("l0"), S("nn"), 16384.0, A.add)
                     tt(S("l1"), S("l0"), n0, A.subtract)
                     landed(0, 4)
                 ts(S("nm"), n0, -16384.0, A.add)
@@ -688,20 +771,20 @@ def rank_program(g, core, T, topo):
         mm(B(4, 0, 256), S("I1280"), S("far"), False, True)
         tt(S("fo"), B(4, 0, 256), S("VT"), A.min)
         ts(S("fo16"), S("fo"), 16383.0, A.add)
+        urgent("fo16")
         if t < 2:
             landed(1, 6)
             for h in range(2):
                 mm(B(7, 128 * h, 128 * h + 128), S("keep", 128 * h, 128 * h + 128), S("ident"), True, True)
-            act(S("wT", 256, 512), B(7, 0, 256), F.Copy)
+            move("wk", S("wT", 256, 512), B(7, 0, 256))
             for h in range(2):
-                weigh(16, "nzR", h, 256 + 128 * h, h == 0, h == 1)
-            tt(S("dg", 0, 24), B(5, 0, 24), S("mask24"), A.mult)
-            red(S("cown"), S("dg", 0, 24), A.add)
+                weigh("nzR", h, 256 + 128 * h, h == 1)
+            red(S("cown"), B(5, 0, 8), A.max)
             choose(t + 1)
         for b in range(8):
             win = IND(S("FW", D0, FE), S("fo16", 32 * b, 32 * b + 32))
             o = S(nxt, 512 * b, 512 * b + 512)
-            e = OPT.get("pl", "VSVSVSVS")[b]
+            e = OPT.get("pl", PLACE)[t][b]
             if t < 2:
                 if e == "V":
                     cp(o, win)
@@ -714,5 +797,5 @@ def rank_program(g, core, T, topo):
                 ts(o, m, -0.0625, A.mult)
             else:
                 act(o, win, F.Relu, bias=254.9991, scale=-0.0625)
-            op("sync", lambda o=o, b=b: g.sync.dma_start(T.y[:, 512 * b:512 * b + 512], AP(o)), [o], [], "ys%d" % b, 16, "dma")
+            op("sync", lambda o=o, b=b: g.sync.dma_start(T.y[:, 512 * b:512 * b + 512], AP(o)), [o], [], "ys%d" % b, 16, "store")
     emit()

import numpy as np
from concourse.bass import DstId, RemoteDMATransfer
from concourse.mybir import dt, AluOpType as A, AxisListType, ActivationFunctionType as F

XE, XC = 4096, 4128
D0, D1 = 1024, 256
W0, WA, WB, FX, FE = 0, 3072, 4352, 6656, 10752
OWN = {
    "BW0": (XC, "bfloat16"), "BW1": (XC, "bfloat16"), "FW": (FE, "float32"), "Zp": (4096, "bfloat16"),
    "Zf": (4096, "float32"), "PH": (1280, "bfloat16"), "Hs": (256, "bfloat16"),
    "cmp": (4096, "bfloat16"), "G": (2048, "bfloat16"), "nzR": (4096, "bfloat16"), "nzC": (4096, "bfloat16"),
    "qi": (16, "int32"), "rown": (96, "float32"), "cl": (288, "float32"),
}
POOL = {
    "bfloat16": {"c1n": 256, "c2n": 256, "c3n": 256, "c1p": 1024, "c2p": 1024, "c3p": 1024, "lAn": 16, "lQn": 16, "lAp": 64,
                 "lQp": 64, "Qblk": 128, "nQ4": 512, "Bones": 128, "ident": 128, "nident": 128, "I3856": 128, "I1928": 128,
                 "I16384": 128, "I1280": 128, "EM1": 144, "EMh": 144, "I16": 128, "EM241": 144, "EM120": 144, "E": 144,
                 "Dm": 128, "Ds": 128, "Dn": 128, "Lo": 128, "Up": 128, "dtmp": 128, "B4080": 128, "c4080": 128, "csb": 1, "Fl": 512, "T2b": 32,
                 "eq": 256, "AL": 256, "lt": 256, "keep": 256, "far": 256, "wT": 512, "onesB": 64, "other": 8},
    "float32": {"dg": 128, "cown": 1, "qf": 16, "kapT": 512, "pif": 1, "p16f": 1, "pgf": 1, "e15": 1, "p37": 1, "BonesF": 128,
                "identF": 128, "M16f": 32, "base": 32, "obig": 16, "mq": 1, "JF": 602, "IF": 1024, "JT": 384,
                "VT": 256, "KT": 256, "onesF": 256, "W2": 48, "W3": 528, "mn": 1, "csel": 1, "kaps": 1,
                "kap2": 1, "nn": 1, "bnd": 512, "KM": 256, "Kp": 1, "Kn": 1, "p17": 1, "A17": 64, "AF": 128, "Tf5": 256, "shr": 48,
                "sc": 64, "pb": 64, "of": 256, "mx": 256, "uu": 256, "g1": 256, "fo": 256, "nm": 1, "dA": 1, "l0": 1, "l1": 1},
    "int32": {"pi": 1, "p16i": 1, "pgi": 1, "ci": 144, "cg": 128, "Ji": 602, "Jm": 602, "JTi": 384, "JTk": 384,
              "JTm": 384, "VTi": 256, "t32": 256, "vi": 256},
    "uint16": {"oAn": 16, "oQn": 16, "oPn": 16, "oAp": 64, "oQp": 64, "oPp": 64, "off": 256, "so": 256, "fo16": 256},
}
SB, PART = dict(OWN), {}
for _d, _names in POOL.items():
    _o = 0
    for _n, _c in _names.items():
        PART[_n] = ("all_" + _d, _o, _c)
        _o += -(-_c // 16) * 16
    SB["all_" + _d] = (_o, _d)
PART["Pg"], PART["Hl"] = ("PH", 0, 1024), ("PH", 1024, 256)
for _t in range(3):
    PART["rown%d" % _t] = ("rown", 32 * _t, 32)
    PART["cl%d" % _t] = ("cl", 96 * _t, 96)
SCRATCH = {n: ("sbuf", [128, -(-c // 16) * 16], d) for n, (c, d) in SB.items()}
for _b in range(8):
    SCRATCH["b%d" % _b] = ("psum", [128, 512], "float32")
NX = 8
QSEM = {"tensor": "sT", "vector": "sV", "scalar": "sS", "g": "sG"}
SEMAPHORES = (["sT", "sV", "sS", "sG", "qld"] + ["xl%d" % i for i in range(NX)] + ["ys%d" % i for i in range(8)]
              + ["%s%d" % (s, t) for s in ("cs", "gs", "lc", "lg", "fx", "fy", "fz") for t in range(3)])
XS = (1, 2, 3)
BIG = 1048576.0
CE = 4
CY, PE, LAT, SLAT, WAKE, DMA, FAR, RATE = 0.83, 0.42, 70.0, 245.0, 70.0, 1500.0, 2200.0, 200.0
PACES = ((1.0, 1.56, 3.8), (1.25, 1.56, 3.8), (1.25, 1.3, 2.7), (1.25, 1.8, 4.9), (1.25, 1.9, 2.4), (1.25, 1.2, 5.2))
LOOKS = (200.0, 300.0, 400.0)
CHILD = ("VV VS VV VS",) * 3
FIRST = ("SSS SSS VV",) * 3
PLACE = ("VSVSVSVS",) * 3
RAYS = "VSVSVSVS"
MOVES = {"lAp": "S", "lQp": "S", "AF": "S", "Hs": "S", "w0": "V", "w1": "V", "wk": "V", "Pg0": "S", "Pg1": "S"}
OPT = {}


def make_queue(g, T):
    ops, hist, runs, last, held = [], {}, {}, {}, {}
    eng = {"tensor": g.tensor, "vector": g.vector, "scalar": g.scalar, "sync": g.sync, "g": g}

    def hold(on):
        held.clear()
        held.update(last if on else {})

    def width(x):
        return 16 * (x[2][2] - x[2][1]) if x[0] == "IND" else x[3].shape[1]

    def size(x):
        return 2 if x[0] in SB and SB[x[0]][1] in ("bfloat16", "uint16") else 4

    def length(q, kind, reads, writes):
        if q is None:
            return (0.0, 0.0, 0.0, 0.0), 0.0
        o, i = (writes + reads)[0], (reads + writes)[0]
        if kind == "remote":
            return (500.0, 0.0, 0.0, 0.0), FAR + 128 * width(i) * size(i) / 50.0
        if kind == "store":
            return (128 * width(o) * size(o) / RATE, 0.0, 0.0, 0.0), DMA
        if kind == "dma":
            return (600.0 if q == "g" else 60.0, 0.0, 0.0, 0.0), DMA + 128 * width(o) * size(o) / RATE
        if q == "tensor":
            return (0.0, sum(size(r) ** 2 / 4 * max(64, width(r)) * PE for r in reads[1::2]), 0.0, 0.0), LAT
        n = width(i)
        if o[0] == "IND" or i[0] == "IND":
            return (0.0, 55.0, n * CY * (o[0] != "IND"), n * CY * (o[0] == "IND")), LAT
        if q == "g":
            return (0.0, 130 + 2 * n * CY, 0.0, 0.0), LAT
        if kind == "tt" and reads[0][0] in SB and reads[1][0] in SB:
            n = 2 * n
        elif kind == "half" and size(o) == 2 and size(i) == 2:
            n = n / 2
        return (0.0, max(64, n) * CY, 0.0, 0.0), LAT

    def op(q, fn, reads, writes, sem=None, val=0, kind="", after=None, lead=0.0, late=0.0):
        me = len(ops)
        c, lat = length(q, kind, reads, writes)
        if q == "scalar" and sem is None:
            lat = SLAT
        rec = {"q": q, "fn": fn, "deps": set(), "ord": set(), "sem": sem, "val": val, "need": False, "m": [],
               "remote": kind == "remote", "len": c, "lat": lat + late, "w": (writes + reads)[0][:3]}
        rec["ord"].update(x for x in (after, held.get(q)) if x is not None)
        last[q] = me
        acc = []
        for x, isw in [(w, True) for w in writes] + [(r, False) for r in reads]:
            acc += [(x[1], isw), (x[2], False)] if x[0] == "IND" else [(x, isw)]

        def mine(o):
            return o["q"] == q and o["sem"] is None
        for (n, a, b, _ap), isw in acc:
            h = hist.setdefault(n, ([], []))
            for (oa, ob, o, ow) in (h[0] + h[1] if isw else h[0]):
                if o != me and oa < b and a < ob:
                    rec["ord" if mine(ops[o]) and (not ow or q == "tensor") else "deps"].add(o)
            if n not in SB:
                r = runs.setdefault(n, [q, [], []])
                if r[0] != q:
                    r[0], r[1], r[2] = q, [], r[1]
                rec["deps"].update(r[2])
                if me not in r[1][-1:]:
                    if q == "tensor":
                        rec["ord"].update(r[1][-1:])
                    r[1].append(me)
        ops.append(rec)
        for (n, a, b, _ap), isw in acc:
            h = hist[n]
            if isw and _ap.shape[1] == b - a:
                for l in h:
                    l[:] = [e for e in l if e[2] == me or not (a <= e[0] and e[1] <= b)]
            h[0 if isw else 1].append((a, b, me, isw))
        return me

    def order():
        n = len(ops)
        links = {}
        for f in set(p[0] for p in PACES):
            lag = [r["lat"] if r["sem"] else WAKE + f * r["lat"] for r in ops]
            pre = [[(d, lag[d]) for d in r["deps"]] + [(d, lag[d] if ops[d]["remote"] else 0.0) for d in r["ord"] - r["deps"]]
                   for r in ops]
            post = [[] for _ in ops]
            for i in range(n):
                for d, lat in pre[i]:
                    post[d].append((i, lat))
            links[f] = (pre, post)

        def lay(seq, before):
            start, used = [0.0] * n, {q: [] for q in eng}
            for i in seq:
                r = ops[i]
                t = max([start[d] + ops[d]["cost"] + lat for d, lat in before[i]] + [0.0])
                if r["q"] is not None:
                    u = used[r["q"]]
                    k = len(u)
                    while k > 0 and u[k - 1][1] > t:
                        k -= 1
                    while k < len(u) and u[k][0] < t + r["cost"]:
                        t = max(t, u[k][1])
                        k += 1
                    u.insert(k, (t, t + r["cost"]))
                start[i] = t
            return start

        def run(urge, before, behind, look):
            left, ready, start = [len(p) for p in before], [0.0] * n, [0.0] * n
            free, can = {q: 0.0 for q in list(eng) + [None]}, {q: [] for q in list(eng) + [None]}
            for i in range(n):
                if not left[i]:
                    can[ops[i]["q"]].append(i)
            for _ in range(n):
                pick = None
                for q, c in can.items():
                    if not c:
                        continue
                    t = max(free[q], min(ready[i] for i in c))
                    now = [i for i in c if ready[i] <= t]
                    i = max(now, key=lambda k: urge[k])
                    for j in c:
                        if t < ready[j] < t + min(look, ops[i]["cost"]) and urge[j] > urge[i]:
                            i = max([k for k in now if t + ops[k]["cost"] <= ready[j]] or [j], key=lambda k: urge[k])
                            break
                    if pick is None or max(free[q], ready[i]) < pick[0]:
                        pick = (max(free[q], ready[i]), q, i)
                t, q, i = pick
                can[q].remove(i)
                start[i] = t
                if q is not None:
                    free[q] = t + ops[i]["cost"]
                for j, lat in behind[i]:
                    ready[j] = max(ready[j], t + ops[i]["cost"] + lat)
                    left[j] -= 1
                    if not left[j]:
                        can[ops[j]["q"]].append(j)
            return start

        def ends(start):
            return [s + r["cost"] for s, r in zip(start, ops)]

        def price(pace):
            for r in ops:
                r["cost"] = r["len"][0] + pace[0] * (r["len"][1] + pace[1] * r["len"][2] + pace[2] * r["len"][3])
            return links[pace[0]]

        def span(seq):
            total = 0.0
            for pace in PACES:
                pre = price(pace)[0]
                end, free = [0.0] * n, {}
                for i in seq:
                    q = ops[i]["q"]
                    end[i] = max([end[d] + lat for d, lat in pre[i]] + [free.get(q, 0.0)]) + ops[i]["cost"]
                    if q is not None:
                        free[q] = end[i]
                total += max(end) / pace[0]
            return total
        best = None
        for pace in PACES[:OPT.get("np", 2)]:
            for look in LOOKS:
                pre, post = price(pace)
                way = [0.0] * n
                for i in reversed(range(n)):
                    way[i] += ops[i]["cost"]
                    for d, lat in pre[i]:
                        way[d] = max(way[d], way[i] + lat)
                start = run(way, pre, post, look)
                for _ in range(OPT.get("it", 3)):
                    price(pace)
                    start = run(ends(run(ends(start), post, pre, look)), pre, post, look)
                    e = ends(start)
                    e = ends(lay(sorted(range(n), key=lambda k: (-e[k], -k)), post))
                    tight = lay(sorted(range(n), key=lambda k: (-e[k], k)), pre)
                    seq = sorted(range(n), key=lambda k: (tight[k], k))
                    mark = span(seq)
                    if best is None or mark < best[0]:
                        best = (mark, seq, tight)
        OPT["span"] = best[0] / len(PACES)
        OPT["dbg"] = (ops, price(PACES[0])[0], way, best[2])
        return best[1]

    def emit():
        for r in ops:
            for d in r["deps"]:
                ops[d]["need"] = True
        cnt = {q: 0 for q in QSEM}
        know = {q: {} for q in eng}
        if "order" not in OPT:
            OPT["order"] = order()
        for r in [ops[i] for i in OPT["order"]]:
            q = r["q"]
            if q is None:
                r["clock"] = {r["sem"]: r["val"], "own": r["sem"]}
                continue
            k = know[q]
            todo = {}
            for d in r["deps"]:
                o = ops[d]
                s, v = (o["sem"], o["val"]) if o["sem"] is not None else (QSEM[o["q"]], o["at"])
                if k.get(s, 0) < v:
                    todo[s] = max(v, todo.get(s, 0))
                    r["m"].append(o["clock"])
            for s in sorted(todo):
                if not any(c["own"] != s and c.get(s, 0) >= todo[s] for c in r["m"]):
                    eng[q].wait_ge(T.sem[s], int(todo[s]))
            for c in r["m"]:
                for s, v in c.items():
                    if s != "own" and k.get(s, 0) < v:
                        k[s] = v
            ins = r["fn"]()
            c = dict(k)
            if r["sem"] is not None:
                c[r["sem"]] = r["val"]
                c["own"] = r["sem"]
                if not r["remote"]:
                    ins.then_inc(T.sem[r["sem"]], r["val"])
            else:
                s = QSEM[q]
                c["own"] = s
                if r["need"]:
                    cnt[q] += 1
                    ins.then_inc(T.sem[s], 1)
                    c[s] = cnt[q]
                    r["at"] = cnt[q]
            r["clock"] = c
        for q, n in cnt.items():
            if n:
                g.wait_ge(T.sem[QSEM[q]], n)
        for r in ops:
            if r["sem"] is not None and r["sem"][:2] in ("ys", "lc", "lg"):
                g.wait_ge(T.sem[r["sem"]], r["val"])

    def urgent(name):
        return name

    return op, hold, urgent, emit


def rank_program(g, core, T, topo):
    rank = T.rank_of(core)
    if rank is None:
        return
    op, hold, urgent, emit = make_queue(g, T)

    def S(n, a=0, b=None, st=1):
        n, o, w = PART.get(n, (n, 0, SB[n][0] if n in SB else 512))
        a, b = a + o, (w if b is None else b) + o
        return (n, a, b, T[n][:, a:b] if st == 1 else T[n][:, a:b:st])

    def B(k, a=0, b=None, st=1):
        return S("b%d" % k, a, b, st)

    def IND(w, o):
        return ("IND", w, o)

    def AP(x):
        return x[1][3].indirect(x[2][3]) if x[0] == "IND" else x[3]

    def num(x):
        return isinstance(x, (int, float))

    def cp(out, in_, lead=0.0):
        op("vector", lambda: g.vector.tensor_copy(AP(out), AP(in_)), [in_], [out], kind="half", lead=lead)

    def tt(out, a, b, o):
        op("vector", lambda: g.vector.tensor_tensor(AP(out), AP(a), AP(b), o), [a, b], [out], kind="tt")

    def ts(out, a, s1, o0, s2=None, o1=None):
        cols = [x for x in (s1, s2) if x is not None and not num(x)]
        u1 = s1 if num(s1) else AP(s1)
        if o1 is None:
            op("vector", lambda: g.vector.tensor_scalar(AP(out), AP(a), u1, None, o0), [a] + cols, [out], kind="half")
        else:
            u2 = s2 if num(s2) else AP(s2)
            op("vector", lambda: g.vector.tensor_scalar(AP(out), AP(a), u1, u2, o0, o1), [a] + cols, [out], kind="half")

    def red(out, a, o):
        op("vector", lambda: g.vector.tensor_reduce(AP(out), AP(a), AxisListType.X, o), [a], [out])

    def scan(out, a, n, first=0.0, by="onesF"):
        one = S(by, 0, n)
        op("vector", lambda: g.vector.tensor_tensor_scan(AP(out), AP(one), AP(a), first, A.mult, A.add), [one, a], [out])

    def fill(out, c):
        op("vector", lambda: g.vector.memset(AP(out), c), [], [out], kind="half")

    def act(out, a, f, bias=0.0, scale=1.0, lead=0.0):
        if f == F.Silu:
            op("scalar", lambda: g.scalar.activation(AP(out), AP(a), f), [a], [out], lead=lead)
        else:
            cols = [x for x in (bias, scale) if not num(x)]
            ub, us = bias if num(bias) else AP(bias), scale if num(scale) else AP(scale)
            op("scalar", lambda: g.scalar.activation(AP(out), AP(a), f, bias=ub, scale=us), [a] + cols, [out])

    def move(name, out, in_, add=0.0):
        if OPT.get("mv", MOVES)[name] == "S":
            act(out, in_, F.Identity if add else F.Copy, bias=add)
        elif add:
            ts(out, in_, add, A.add)
        else:
            cp(out, in_)

    def mm(out, l, r, start, stop):
        mms([(out, l, r, start, stop)])

    def mms(calls):
        op("tensor", lambda: [g.tensor.matmul(AP(o), AP(l), AP(r), a, b) for o, l, r, a, b in calls][-1],
           [x for c in calls for x in c[1:3]], [c[0] for c in calls])

    def spread(bank, c0, n, emat, src, s0, start, stop):
        mms([(B(bank, c0, c0 + n), S(emat, 15 - p, 143 - p), S(src, s0 + p, s0 + 16 * n, 16), start and p == 0, stop and p == 15)
             for p in range(16)])

    def steps(bank, c0, n, src, s0):
        mms([(B(bank, c0, c0 + n), S("Lo"), S(src, s0, s0 + n), True, False),
             (B(bank, c0 + 1, c0 + n), S("Up"), S(src, s0, s0 + n - 1), False, True)])

    def iota(out, pattern, base=0, cm=0, fl=False):
        if fl:
            op("g", lambda: g.iota(AP(out), pattern, base, cm, allow_small_or_imprecise_dtypes=True), [], [out])
        else:
            op("g", lambda: g.iota(AP(out), pattern, base, cm), [], [out])

    def cast_in(out, in_, sem, also=()):
        op("g", lambda: g.dma_start(AP(out), AP(in_)), [in_] + list(also), [out], sem, 16, "dma")

    op("sync", lambda: g.sync.dma_start(T.qi[:, 0:16], T.q[:]), [], [S("qi")], "qld", 16, "dma")
    w = 4096 // NX

    def load(i, q):
        o = S("BW1", w * i, w * i + w)
        op(q, lambda: (g.sync if q == "sync" else g.scalar).dma_start(AP(o), T.x[:, w * i:w * i + w]), [], [o], "xl%d" % i, 16, "dma",
           late=i * 256 * w / RATE)
    for i in range(NX):
        hold(True)
        load(i, "sync" if i % 2 else "scalar")
    hold(False)
    iota(S("pi"), [[1, 1]], 0, 1)
    iota(S("ci"), [[1, 144]])
    iota(S("Ji"), [[37, 602]])
    iota(S("IF"), [[1, 1024]], 0, 0, True)
    ts(S("pgi"), S("pi"), 4, A.arith_shift_right)
    ts(S("cg"), S("ci", 0, 128), 4, A.arith_shift_right)
    ts(S("p16i"), S("pi"), 15, A.bitwise_and)
    cp(S("pgf"), S("pgi"))
    cp(S("pif"), S("pi"))
    cp(S("p16f"), S("p16i"))
    ts(S("BonesF"), S("cg"), S("pgf"), A.is_equal)
    ts(S("identF"), S("ci", 0, 128), S("pif"), A.is_equal)
    for k in range(8):
        ts(S("Qblk", 16 * k, 16 * k + 16), S("qi"), S("BonesF", 16 * k, 16 * k + 1), A.mult)
    for k in (0, 16):
        ts(S("M16f", k, k + 16), S("ci", 0, 16), S("p16f"), A.is_equal, 16.0, A.mult)
    cp(S("base", 0, 16), S("ci", 0, 16))
    ts(S("e15"), S("pif"), S("p16f"), A.subtract, 15.0, A.add)
    ts(S("qf"), S("qi"), 0.125, A.mult)
    tt(S("base", 16, 32), S("base", 0, 16), S("qf"), A.add)
    ts(S("dtmp"), S("ci", 0, 128), S("pif"), A.is_lt, -1.0, A.mult)
    ts(S("EM1"), S("ci"), S("e15"), A.is_equal)
    act(S("Bones"), S("BonesF"), F.Copy)
    act(S("B4080"), S("BonesF"), F.Copy, scale=4080.0)
    tt(S("Dm"), S("dtmp"), S("BonesF"), A.mult)
    for n, s in (("EMh", -0.5), ("EM241", 241.0), ("EM120", 120.5)):
        act(S(n), S("EM1"), F.Copy, scale=s)
    for n, s in (("ident", 1.0), ("I16", 16.0), ("nident", -1.0), ("I3856", 3856.0), ("I1928", 1928.0), ("I16384", 16384.0),
                 ("I1280", float(WB - WA))):
        act(S(n), S("identF"), F.Copy, scale=s)
    tt(S("Ds"), S("Dm"), S("identF"), A.subtract)
    tt(S("Lo"), S("Dm"), S("BonesF"), A.add)
    act(S("Up"), S("Dm"), F.Copy, scale=-1.0)
    act(S("Dn"), S("identF"), F.Copy, scale=-16384.0)
    fill(S("BW0", XE, XC), 0.0)
    ts(S("Kp"), S("p16f"), 15.0, A.is_lt, 4095.0, A.mult)
    ts(S("Kp"), S("Kp"), 1.0, A.add)
    ts(S("Kn"), S("Kp"), -1.0, A.mult)
    ts(S("p17"), S("p16f"), 16.0, A.mult, 16.0, A.add)
    fill(S("onesF"), 1.0)
    fill(S("onesB"), 1.0)
    for a, b in ((16, 24), (40, 48)):
        fill(S("W2", a, b), 1000000.0)
    for a, b in ((256, 264), (520, 528)):
        fill(S("W3", a, b), 1000000.0)
    ts(S("p37"), S("p16f"), 37.0, A.mult)
    fill(S("c4080"), 4080.0)

    def constants():
        iota(S("JTi"), [[1, 3], [64, 4], [592, 32]])
        iota(S("VTi"), [[16, 256]], FX - D0 - 16383)
        iota(S("KT", 0, 128), [[0, 2048 // D0], [16, D0 // 16]], 16384 - D0, 0, True)
        iota(S("KT", 128, 256), [[0, 8], [16, 16]], 16384 - D1, 0, True)
        for b in range(8):
            o, i = S("BW0", 512 * b, 512 * b + 512), S("BW1", 512 * b, 512 * b + 512)
            if b in (2, 5, 7):
                act(o, i, F.Identity, bias=4080.0, scale=-16.0)
            else:
                ts(o, i, -16.0, A.mult, 4080.0, A.add)
        fill(S("BW1", XE, XC), 0.0)
        ts(S("KM"), S("IF", 0, 256), S("p17"), A.is_equal, 4095.0, A.mult)
        ts(S("KM"), S("KM"), 1.0, A.add)
        act(S("IF"), S("IF"), F.Identity, bias=1.0 - 2.0 ** -13)
        ts(S("other"), S("ci", 0, 8), S("pgf"), A.not_equal, -65536.0, A.mult)
        for a in range(D0, FX, 512):
            act(S("FW", a, a + 512), S("BW1", 0, 512), F.Silu)
        ts(S("Jm"), S("Ji"), 255, A.bitwise_and)
        cp(S("JF"), S("Jm"))
        ts(S("JTk"), S("JTi"), S("p37"), A.add)
        ts(S("JTm"), S("JTk"), 255, A.bitwise_and)
        ts(S("JT"), S("JTm"), 5.0, A.mult)
        ts(S("VT"), S("VTi"), S("p16f"), A.add)
        ts(S("KT"), S("KT"), S("p16f"), A.add)
        for k in range(4):
            act(S("nQ4", 128 * k, 128 * k + 128), S("Qblk"), F.Copy, scale=-1.0)
        for b in range(1, 8, 2):
            act(S("nzR", 512 * b, 512 * b + 512), S("nzR", 512 * b, 512 * b + 512), F.Abs)
        mm(B(6), S("c4080"), S("nQ4"), True, True)
        act(S("kapT"), B(6), F.Copy, scale=-1.0)

    peers = [r for r in range(len(T.cores)) if r != rank]
    peers.sort(key=lambda r: len(topo.engines(core, T.cores[r])))
    used, plan = [], []
    for r in peers:
        es = [e for e in topo.engines(core, T.cores[r]) if e not in used][:CE]
        used += es
        plan.append((r, sum(1 << e for e in es)))

    def send_counts(t):
        def f():
            tr = []
            for r, m in plan:
                rid, pid, _s = topo.addr(T.cores[r])
                c = [k for k in range(len(T.cores)) if k != r].index(rank)
                tr.append(RemoteDMATransfer(dst_ids=[DstId(rid=rid, pnc=pid)], dma_engine_mask=m, remote_sem=T.sem["cs%d" % t],
                                            src=AP(S("rown%d" % t)), dst=AP(S("cl%d" % t, 32 * c, 32 * c + 32))))
            return g.remote_dma_fused(tr, local_sem=T.sem["lc%d" % t])
        i = op("g", f, [S("rown%d" % t)], [], "lc%d" % t, CE * len(peers), "remote", late=0.0 if t else 2000.0)
        op(None, None, [], [S("cl%d" % t)], "cs%d" % t, CE * len(peers), after=i)

    def send_guests(t):
        dst = T.cores[rank ^ XS[t]]
        es = topo.engines(core, dst)[:8]

        def f():
            rid, pid, _s = topo.addr(dst)
            return g.remote_dma(AP(S("Hl")), AP(S("Hs")), T.sem["gs%d" % t], T.sem["lg%d" % t], pid, rid, sum(1 << e for e in es))
        i = op("g", f, [S("Hs")], [], "lg%d" % t, len(es), "remote")
        op(None, None, [], [S("Hl")], "gs%d" % t, len(topo.engines(dst, core)[:8]), after=i)

    def values(bank, c0, xs, k, start=True, stop=True):
        o = 2048 * (k // 16)
        mm(B(bank, c0, c0 + 128), S(xs, o + k % 16, o + 2048, 16), S("Qblk"), start, stop)

    def weigh(nz, h, w0, stop):
        for k in range(0, 16, 8):
            mms([(B(5, 0, 8), S(nz, 2048 * h + 128 * p, 2048 * h + 128 * p + 128), S("wT", w0 + p, w0 + 128, 16),
                  False, stop and p == 15) for p in range(k, k + 8)])

    for b in range(8):
        for k in range(4):
            values(b % 7, 128 * k, "BW1", 4 * b + k)
        o = S("nzR", 512 * b, 512 * b + 512)
        if b % 2:
            act(o, B(b % 7), F.Sign)
        else:
            ts(o, B(b % 7), 0.0, A.not_equal)
        for k in range(4):
            c = S("nzR", 512 * b + 128 * k, 512 * b + 128 * k + 128)
            mm(B(7, 0, 128), c, c, b == 0 and k == 0, b == 7 and k == 3)
    tt(S("dg"), B(7, 0, 128), S("identF"), A.mult)
    red(S("cown"), S("dg"), A.add)

    def choose(t):
        rown = S("rown%d" % t)
        ts(rown, S("M16f"), S("cown"), A.mult)
        urgent("counts")
        send_counts(t)
        if t == 0:
            hold(True)
            constants()
            hold(False)
        mm(B(0, 0, 32), S("identF"), S("base"), True, False)
        mm(B(0, 0, 32), S("BonesF"), rown, False, False)
        for k in range(3):
            mm(B(0, 0, 32), S("BonesF"), S("cl%d" % t, 32 * k, 32 * k + 32), False, k == 2)
        red(S("mn"), B(0, 0, 16), A.min)
        red(S("mq"), B(0, 16, 32), A.min)
        ts(S("csel"), S("mq"), S("mn"), A.subtract, 8.0, A.mult)
        ts(S("E"), S("EM1"), S("csel"), A.mult)
        urgent("E")
        cp(S("csb"), S("csel"))
        mm(B(1, 0, 1), S("B4080"), S("csb"), True, True)
        cp(S("kaps"), B(1, 0, 1))
        urgent("kaps")
        ts(S("kap2"), S("kaps"), 2.0, A.mult)
        if t < 2:
            ts(S("obig"), B(0, 0, 16), S("mn"), A.is_equal, BIG, A.mult)
            for k in (0, 16):
                tt(S("base", k, k + 16), S("base", k, k + 16), S("obig"), A.add)
    choose(0)

    for t in range(3):
        cur, nxt = ("BW0", "BW1") if t % 2 == 0 else ("BW1", "BW0")
        X = S(cur, 0, XC)
        for a, b in OPT.get("sp", ((0, 256),) if t == 0 else ((0, 128), (128, 192), (192, 256))):
            spread(2, a, b - a, "E", cur, 16 * a, True, True)
        ts(S("Fl", 0, 256), B(2, 0, 256), S("kaps"), A.is_gt)
        ts(S("Fl", 256, 512), B(2, 0, 256), S("kaps"), A.is_lt)
        mm(B(4, 0, 256), S("Bones"), S("Fl", 0, 256), True, True)
        mm(B(1, 0, 256), S("Bones"), S("Fl", 256, 512), True, True)
        spread(3, 0, 32, "EM1", "Fl", 0, True, True)
        cp(S("T2b"), B(3, 0, 32))
        for k in range(2):
            steps(3, 32 + 16 * k, 16, "T2b", 16 * k)
        mm(B(3, 64, 80), S("Bones"), S("T2b", 0, 16), True, True)
        for k, bank in enumerate((4, 1)):
            scan(S("bnd", 256 * k, 256 * k + 256), B(bank, 0, 256), 256, k - 1.0, "KM")
            scan(S("W2", 24 * k, 24 * k + 16), B(3, 32 + 16 * k, 48 + 16 * k), 16)
            steps(5, 256 * k, 256, "Fl", 256 * k)
            scan(S("W3", 264 * k, 264 * k + 256), B(5, 256 * k, 256 * k + 256), 256)
        red(S("nn"), B(3, 64, 80), A.add)
        if t == 1:
            for b in range(8):
                e, o = OPT.get("nzr", RAYS)[b], S("nzR", 512 * b, 512 * b + 512)
                if e != "V":
                    mm(B(6 + b % 2), S("c4080"), S("nQ4"), True, False)
                for k in range(4):
                    values(6 + b % 2, 128 * k, cur, 4 * b + k, e == "V", e == "V" or k == 3)
                if e == "V":
                    tt(o, B(6 + b % 2), S("kapT"), A.not_equal)
                    continue
                act(o, B(6 + b % 2), F.Sign)
                if e == "S":
                    act(o, o, F.Abs)
                else:
                    ts(o, o, 0.0, A.not_equal)
        J = S("JF", 173 * t, 173 * t + 256)
        ts(S("c1n"), J, S("Kp"), A.mult, S("bnd", 255, 256), A.is_gt)
        spread(0, 0, 16, "EM1", "c1n", 0, True, True)
        act(S("c1p"), S("IF"), F.Sign, bias=S("bnd", 511, 512), scale=S("Kn"))
        spread(1, 0, 64, "EMh", "c1p", 0, True, True)
        cp(S("oAn"), B(0, 0, 16))
        cp(S("lAn"), B(0, 0, 16))
        tt(S("c2n"), IND(S("W2", 0, 24), S("oAn")), J, A.is_le)
        mm(B(2, 0, 16), S("I16"), S("lAn"), True, False)
        spread(2, 0, 16, "EM1", "c2n", 0, False, True)
        ts(S("oAp"), B(1, 0, 64), 8.0, A.add)
        move("lAp", S("lAp"), B(1, 0, 64), 8.0)
        cp(S("oQn"), B(2, 0, 16))
        cp(S("lQn"), B(2, 0, 16))
        tt(S("c3n"), IND(S("W3", 0, 264), S("oQn")), J, A.is_le)
        mm(B(0, 0, 16), S("I16"), S("lQn"), True, False)
        spread(0, 0, 16, "EM1", "c3n", 0, False, True)
        cp(S("oPn"), B(0, 0, 16))
        move("Hs", S("Hs"), IND(X, S("oPn")))
        urgent("guests")
        send_guests(t)
        mm(B(4, 256, 512), S("Dn"), S("Fl", 0, 256), True, True)
        tt(S("uu"), S("W3", 0, 256), B(4, 256, 512), A.add)
        cast_in(S("FW", FX, FE), S(cur, 0, XE), "fx%d" % t, [S("Hl")])
        qb, pbk = (3, 1), (2, 3)
        for h in range(2):
            o, k = (512 * h, 512 * h + 512), (32 * h, 32 * h + 32)
            tt(S("c2p", *o), IND(S("W2", 24, 48), S("oAp", *k)), S("IF", *o), A.is_lt)
            mm(B(qb[h], 0, 32), S("I16"), S("lAp", *k), True, False)
            spread(qb[h], 0, 32, "EM1", "c2p", 512 * h, False, True)
            cp(S("oQp", *k), B(qb[h], 0, 32))
            move("lQp", S("lQp", *k), B(qb[h], 0, 32))
        for h in range(2):
            o, k = (512 * h, 512 * h + 512), (32 * h, 32 * h + 32)
            tt(S("c3p", *o), IND(S("W3", 264, 528), S("oQp", *k)), S("IF", *o), A.is_lt)
            mm(B(pbk[h], 0, 32), S("I16"), S("lQp", *k), True, False)
            spread(pbk[h], 0, 32, "EM1", "c3p", 512 * h, False, True)
            cp(S("oPp", *k), B(pbk[h], 0, 32))
            ts(S("A17", *k), B(pbk[h], 0, 32), 17.0, A.mult)
            for c in (64 * h, 64 * h + 32):
                move("AF", S("AF", c, c + 32), B(pbk[h], 0, 32))
            move("Pg%d" % h, S("Pg", *o), IND(X, S("oPp", *k)))
            for ww in range(4):
                c = 128 * h + 32 * ww
                tt(S("t32", c, c + 32), S("A17", *k), S("JT", 128 * t + 32 * ww, 128 * t + 32 * ww + 32), A.add)
            c = (128 * h, 128 * h + 128)
            ts(S("vi", *c), S("t32", *c), 4095, A.bitwise_and)
            cp(S("off", *c), S("vi", *c))
        for c in range(4):
            mm(B(c, 64, 128), S("identF"), S("AF", 64 * (c // 2), 64 * (c // 2) + 64), True, True)

        def children(c, banks, engines):
            for k in range(2):
                ww, b = 2 * (c % 2) + k, banks[k]
                mm(B(b), S("ident"), S("Pg", 512 * (c // 2), 512 * (c // 2) + 512), True, False)
                for o in (0, 256):
                    mm(B(b, o, o + 256 - 64 * ww), S("ident"), S("Hl", 64 * ww, 256), False, o == 256 and ww == 0)
                    if ww:
                        mm(B(b, o + 256 - 64 * ww, o + 256), S("ident"), S("Hl", 0, 64 * ww), False, o == 256)
                o = S("Zp", 1024 * c + 512 * k, 1024 * c + 512 * k + 512)
                if engines[k] == "S":
                    act(o, B(b), F.Relu, bias=-4080.0)
                else:
                    ts(o, B(b), -4080.0, A.add, 0.0, A.max)
        ch = OPT.get("ch", CHILD)[t].split()
        children(0, (4, 5), ch[0])
        children(1, (6, 7), ch[1])
        children(2, (6, 7), ch[2])
        children(3, (6, 7), ch[3])
        s0 = OPT.get("s0", FIRST)[t].replace(" ", "")
        z0, z1 = 256 * s0.index("S"), 256 * s0.rindex("S") + 256
        cast_in(S("Zf", z0, z1), S("Zp", z0, z1), "fy%d" % t)
        cast_in(S("Zf", 2304, 4096), S("Zp", 2304, 4096), "fz%d" % t)

        def not_zero(bank, h, k0, k1):
            for k in range(k0, k1):
                values(bank, 128 + 128 * (k - k0), "Zp", 16 * h + k)
            n = 128 * (k1 - k0)
            tt(S("nzC", 2048 * h + 128 * k0, 2048 * h + 128 * k1), B(bank, 128, 128 + n), S("kapT", 0, n), A.not_equal)

        def sum_ok():
            spread(0, 128, 80, "E", "PH", 0, True, True)
            for m in range(3):
                ts(S("shr", 16 * m, 16 * m + 16), B(0, 192, 208), -1.0, A.mult, S("kap2"), A.add)
            for o in range(0, 256, 32):
                tt(S("AL", o, o + 32), B(0, 128 + o // 128 * 32, 160 + o // 128 * 32), S("shr", o % 128 // 8, o % 128 // 8 + 32), A.is_le)

        def probe(c, n):
            h, l, z = c // 2, (64 * c, 64 * c + 64), (1024 * c, 1024 * c + 1024)
            tt(S("eq", *l), S("vi", *l), B(c, 64, 128), A.is_equal)
            if n < 5:
                ts(S("Tf5", *l), S("vi", *l), 5.0, A.mult, 1.0, A.add)
            if t < 2 and c % 2 and n:
                not_zero(c, h, 3 * n - 3, 3 * n)
            if t < 2 and c % 2 == 0 and n == 3:
                not_zero(c, h, 15, 16)
            if c % 2 == 0:
                tt(S("cmp", *z), IND(X, S("off", *l)), S("Zp", *z), A.is_lt)
            else:
                act(S("G", 1024 * h, 1024 * h + 1024), IND(X, S("off", *l)), F.Copy)
                for k in range(2):
                    b, o = 4 + 2 * h + k, 1024 * c + 512 * k
                    mm(B(b), S("ident"), S("Zp", o, o + 512), True, False)
                    mm(B(b), S("nident"), S("G", 1024 * h + 512 * k, 1024 * h + 512 * k + 512), False, True)
                    act(S("cmp", o, o + 512), B(b), F.Sign, bias=-0.5)
            mm(B(c, 0, 64), S("I3856"), S("eq", *l), True, False)
            if c % 2:
                mm(B(c, 0, 64), S("I1928"), S("onesB"), False, False)
            spread(c, 0, 64, "EM120" if c % 2 else "EM241", "cmp", 1024 * c, False, True)
            if n < 5:
                tt(S("t32", *l), B(c, 0, 64), S("Tf5", *l), A.add)
                ts(S("vi", *l), S("t32", *l), 4095, A.bitwise_and)
                cp(S("off", *l), S("vi", *l))
            if n == 0 and c == 0:
                sum_ok()
            tt(S("AL", *l), B(c, 0, 64), S("AL", *l), A.min)

        def number(h):
            bs, bx, a0 = 2 * h, 2 * h + 1, 128 * h
            al = [S("AL", a0 + 32 * ww, a0 + 32 * ww + 32) for ww in range(4)]
            for ww in range(4):
                mm(B(bx, 0, 32), S("Bones"), al[ww], ww == 0, ww == 3)
            for ww in range(4):
                mm(B(bx, 32, 64), S("Ds"), al[ww], ww == 0, ww == 3)
            mm(B(bs, 0, 128), S("I16384"), S("AL", a0, a0 + 128), True, False)
            for ww in range(1, 4):
                mm(B(bs, 32 * ww, 128), S("ident"), S("AL", a0, a0 + 128 - 32 * ww), False, ww == 3)
            sc, pb = S("sc", 32 * h, 32 * h + 32), S("pb", 32 * h, 32 * h + 32)
            scan(sc, B(bx, 0, 32), 32)
            tt(pb, sc, B(bx, 32, 64), A.add)
            for ww in range(4):
                tt(S("of", a0 + 32 * ww, a0 + 32 * ww + 32), B(bs, 32 * ww, 32 * ww + 32), pb, A.add)
            tt(S("mx", a0, a0 + 128), S("of", a0, a0 + 128), S("KT", a0, a0 + 128), A.max)
            ts(S("so", a0, a0 + 128), S("mx", a0, a0 + 128), float((D1 if h else D0) - 16384), A.add)

        def landed(h, bank):
            l = (128 * h, 128 * h + 128)
            ts(S("lt", *l), S("of", *l), S("l%d" % h), A.is_lt)
            mm(B(bank, 0, 128), S("lt", *l), S("ident"), True, False)
            mm(B(bank, 0, 128), S("AL", *l), S("ident"), False, True)
            move("w%d" % h, S("wT", *l), B(bank, 0, 128), -1.0)
            if h == 0:
                mm(B(5, 0, 8), S("ident"), S("other"), True, False)
            weigh("nzC", h, 128 * h, False)
        n0, n1a, n1 = S("sc", 31, 32), S("sc", 47, 48), S("sc", 63, 64)
        u = S("W3", 0, 256)
        for h in range(2):
            for n in range(6):
                probe(2 * h, n)
                probe(2 * h + 1, n)
            number(h)
            if h == 0:
                k = 0
                for e in OPT.get("s0", FIRST)[t].split():
                    win = IND(S("FW", W0, WA), S("so", 16 * k, 16 * (k + len(e))))
                    if e[0] == "V":
                        cp(win, S("Zp", 256 * k, 256 * (k + len(e))))
                    else:
                        act(win, S("Zf", 256 * k, 256 * (k + len(e))), F.Silu)
                    k += len(e)
                if t < 2:
                    ts(S("l0"), S("nn"), 16384.0, A.add)
                    tt(S("l1"), S("l0"), n0, A.subtract)
                    landed(0, 4)
                ts(S("nm"), n0, -16384.0, A.add)
                ts(S("dA"), n0, -1.0, A.mult, float(WA + D1 - D0), A.add)
                ts(S("g1"), u, n0, A.is_gt, S("dA"), A.mult)
                mm(B(4, 0, 256), S("identF"), S("uu"), True, False)
                mm(B(4, 0, 256), S("identF"), S("g1"), False, False)
        for ww in range(4):
            o = 128 + 32 * ww
            cp(IND(S("FW", WA, WB), S("so", o, o + 16)), S("Zp", 16 * o, 16 * o + 256))
            act(IND(S("FW", WB, FX), S("so", o + 16, o + 32)), S("Zf", 16 * o + 256, 16 * o + 512), F.Silu)
        ts(S("keep"), S("uu"), S("nm"), A.subtract, n1, A.is_gt)
        ts(S("far"), u, n0, A.subtract, n1a, A.is_gt)
        mm(B(4, 0, 256), S("I16384"), S("keep"), False, False)
        mm(B(4, 0, 256), S("I1280"), S("far"), False, True)
        tt(S("fo"), B(4, 0, 256), S("VT"), A.min)
        ts(S("fo16"), S("fo"), 16383.0, A.add)
        urgent("fo16")
        if t < 2:
            landed(1, 6)
            for h in range(2):
                mm(B(7, 128 * h, 128 * h + 128), S("keep", 128 * h, 128 * h + 128), S("ident"), True, True)
            move("wk", S("wT", 256, 512), B(7, 0, 256))
            for h in range(2):
                weigh("nzR", h, 256 + 128 * h, h == 1)
            red(S("cown"), B(5, 0, 8), A.max)
            choose(t + 1)
        for b in range(8):
            win = IND(S("FW", D0, FE), S("fo16", 32 * b, 32 * b + 32))
            o = S(nxt, 512 * b, 512 * b + 512)
            e = OPT.get("pl", PLACE)[t][b]
            if t < 2:
                if e == "V":
                    cp(o, win)
                else:
                    act(o, win, F.Copy)
                continue
            if e == "V":
                m = S("cmp", 512 * b, 512 * b + 512)
                ts(m, win, -4079.986, A.add, 0.0, A.min)
                ts(o, m, -0.0625, A.mult)
            else:
                act(o, win, F.Relu, bias=254.9991, scale=-0.0625)
            op("sync", lambda o=o, b=b: g.sync.dma_start(T.y[:, 512 * b:512 * b + 512], AP(o)), [o], [], "ys%d" % b, 16, "store")
    emit()
